import numpy as np, ml_dtypes
CORES = [51,54,179,182]
N = 4
BF = ml_dtypes.bfloat16
W, C, L, CAP, H, RO = 2048, 2, 256, 64, 2, 3
def ends(a):
    return np.arange(W).reshape(L, C, N)[:, a].reshape(-1)
def pairs(rng):
    o = np.argsort(rng.random((8, W)), axis=1); b = np.zeros((8, W), np.int64)
    np.put_along_axis(b, o, np.concatenate([o[:, W // 2:], o[:, :W // 2]], axis=1), 1)
    return b
def mix(rng, p, z):
    a, b = pairs(rng)[None, :, None], pairs(rng)[None, :, None]; u = rng.random((N, 8, 16, W), dtype=np.float32)
    return np.where(u < p, a, np.where(u < p + (1 - p) * 0.8, b, z))
def odds(rng):
    k = np.array([0.95, 0.75, 0.5, 0.3, 0.1])
    return np.where(rng.random((N, 8, 1, W)) < 0.25, rng.choice(k, (N, 8, 1, W)), rng.choice(k, (1, 8, 1, W)))
def anyone(rng):
    return rng.integers(0, W, (N, 8, 16, W))
def pack(m, x, t):
    return {"mt": np.ascontiguousarray(m.reshape(N, 128, W)).astype(np.int32), "xv": np.ascontiguousarray(x.reshape(N, 128, W)).astype(np.float32).astype(BF),
            "th": np.ascontiguousarray(t.reshape(N, 8, 1)).astype(np.int32)}
def put(o, v, i):
    e = int(np.nonzero(o == v)[0][0]); o[e] = o[i]; o[i] = v
def brim(rng, mg, h, less):
    mg[:] = rng.integers(0, W, mg.shape); k = np.arange(N); n = np.arange(8); j = np.arange(12)
    p = N * C * rng.permutation(L)[:, None] + k; w = N * C * rng.permutation(L)[:, None] + N + k; p2 = p + N * (2 % C)
    v = p[:CAP].reshape(-1); c = rng.permutation(w[:CAP].reshape(-1)); mg[:, :, v] = c; mg[:, :, c] = v
    if less: mg[:, :, int(c[-1])] = int(v[0])
    far = rng.permutation(p[CAP:CAP + 12].reshape(-1)).reshape(12, N)
    for r in range(N):
        q = (r + 1 + 1 % (N - 1)) % N; u, d = w[CAP:CAP + 12, r], far[:, r]; o = np.argsort(rng.random((16, 12)), axis=0)
        mg[r][:, u] = d; mg[r][:, d] = u; mg[q][:, d] = np.where(o < h - 16 + j % 4, u, (u + 1) % W)
        q = (r + 1 + 2 % (N - 1)) % N; z, y = p2[CAP + 12:CAP + 20, r], w[CAP + 12:CAP + 20, q]; o = np.argsort(rng.random((16, 8)), axis=0); e = n * N + (q + 1) % N
        mg[r][:, z] = y; mg[r][:, y] = z; mg[q][:, v[e]] = z
        mg[q][:, y] = np.where(o < np.where(n % 2 == 0, 16, h - 16 + n // 2), c[e], mg[q][:, y])
def setup_inputs(rng):
    return pack(mix(rng, odds(rng), anyone(rng)), rng.integers(0, 256, (N, 8, 16, W)), rng.integers(6, 33, (N, 8, 1)))
def setup_inputs_spread(rng):
    p = np.exp2(-5 * rng.random((N, 8, 1, W))); z = (W * rng.random((N, 8, 16, W)) ** 4).astype(np.int64)
    x = np.floor(np.exp2(8 * rng.random((N, 8, 1, W))) * rng.random((N, 8, 16, W))) * (rng.random((N, 8, 1, W)) > 0.0625)
    return pack(mix(rng, p, z), x, (33 * rng.random((N, 8, 1)) ** 2).astype(np.int64))
def setup_inputs_ends(rng):
    k = rng.integers(0, 4, (N, 8, 1, W)); m = np.where(k < 2, k, rng.integers(0, 2, (N, 8, 16, W))) * (W - 1)
    x = rng.integers(0, 2, (N, 8, 16, W)) * 255; k = rng.integers(0, 4, (N, 8, 1, W)); last = x[..., W - 1:].copy()
    x = np.where(k == 0, last, np.where(k == 1, 255 - last, x)); n = W // (10 * C)
    for g in range(8):
        pr = []; mg, xg = m[:, g], x[:, g]
        for a in range(C):
            o = rng.permutation(ends(a)); put(o, W - N * C + N * a + N - 1, n if a == C - 1 else 0)
            if a == C - 1: put(o, N * a, 2 * n)
            pr.append(o)
        for a in range(C):
            v, c, b = pr[a][:n], pr[a - 1][n:2 * n], pr[a - 1][2 * n:3 * n]; kind = rng.integers(0, 4, n); kind[0] = 0
            first = rng.random((N, 16, n)) < 0.5; first[:, 0, 0] = g % 2 == 1; first[:, 15] = ~first[:, 0]
            mg[:, :, v] = np.where(first, c, b); mg[:, :, c] = v; mg[:, :, b] = v
            xc = xg[:, :, c]
            xg[:, :, v] = np.where(kind == 1, 255 - xc, np.where(kind == 2, xg[:, :, v], xc)); xg[:, :, b] = np.where(kind == 3, 255 - xc, xc)
    t = 32 * rng.integers(0, 2, (N, 8, 1)); t[:, 0] = 0; t[:, 7] = 32
    return pack(m, x, t)
def setup_inputs_corners(rng):
    z = ends(0); m = np.where(rng.random((N, 8, 16, W), dtype=np.float32) < 0.6, z[rng.integers(0, len(z), (N, 8, 16, W))], anyone(rng))
    x = rng.choice(np.array([0, 1, 254, 255]), (N, 8, 16, W)); t = rng.choice(np.array([1, 2, 7, 16, 17, 31, 32]), (N, 8, 1)); off = int(rng.integers(0, 6))
    for g in range(8):
        w = rng.permutation(ends(1))
        for r in range(N):
            v = z[r::N]; c = w[r * L:r * L + L]; h = int(t[r, g, 0]); q = (r + 1) % N
            ok = np.zeros(L, bool); ok[rng.permutation(L)[:(0, 1, CAP - 1, CAP, CAP + 1, L)[(g + r + off) % 6]]] = True
            s = np.where(ok, rng.integers(h, 33, L), rng.integers(0, h, L)); s = np.where(rng.random(L) < 0.6, h - 1 + ok, s)
            own = rng.integers(np.maximum(s - 16, 0), np.minimum(s, 16) + 1); o = np.argsort(rng.random((2, 16, L)), axis=1)
            for b, e, n in ((r, 0, own), (q, 1, s - own)):
                y = m[b, g][:, c]; y = np.where(y == v, (v + N * C) % W, y); m[b, g][:, c] = np.where(o[e] < n, v, y)
            m[r, g][:, v] = c
    return pack(m, x, t)
def setup_inputs_crowd(rng):
    m = mix(rng, odds(rng), anyone(rng)); x = rng.integers(0, 256, (N, 8, 16, W)); t = rng.integers(6, 33, (N, 8, 1))
    for g, h in ((0, 0), (1, 0), (2, 0), (4, 32), (5, 30), (6, 1)):
        mg = m[:, g]; late = []; t[:, g] = h
        for a in range(C):
            v = ends(a); w = rng.permutation(ends((a + 1) % C)); f = w[:4 if g % 4 == 2 else 1]
            mg[:, :, v] = f[rng.integers(0, len(f), len(v))]
            if g % 4 == 1: mg[:, :, int(v[int(rng.integers(0, N * CAP))])] = int(w[9])
            if a < C - 1: late.append((f, np.append(v[-1:], rng.choice(v, len(f) - 1))))
        for f, v in late:
            mg[:, :, f] = v
            if g % 4 == 1: mg[:, 5, f] = (v + 1) % W
    for g in (3, 7):
        h = int(rng.integers(18, 28)); t[:, g] = h; brim(rng, m[:, g], h, g == 7)
    return pack(m, x, t)
def setup_inputs_ties(rng):
    m = mix(rng, rng.choice(np.array([0.4, 0.5, 0.6]), (1, 8, 1, W)), anyone(rng))
    x = rng.integers(0, 255, (N, 8, 16, 1)) + rng.integers(0, 2, (N, 8, 1, W)) * (np.arange(8) % 2).reshape(1, 8, 1, 1)
    return pack(m, x, rng.integers(8, 20, (N, 8, 1)))
def check_inputs(d):
    bad = []
    for k, lo, hi in (("mt", 0, W - 1), ("xv", 0, 255), ("th", 0, 32)):
        a = np.asarray(d[k]).astype(np.float64)
        if not (np.min(a) >= lo and np.max(a) <= hi and np.all(a == np.floor(a))): bad.append("range of " + k)
    return bad
def reference(mt, xv, th):
    M = mt.astype(np.int64).reshape(N, 8, 16, W); X = xv.astype(np.float32).astype(np.int64).reshape(N, 8, 16, W); T = th.astype(np.int64).reshape(N, 8, 1)
    pi = np.full((8, W), -1, np.int64); grp = np.arange(8).reshape(8, 1, 1); A = 0
    for t in range(RO):
        a = t % C; lanes, cand, has, cnt = [], [], [], []
        for r in range(N):
            v = N * C * np.arange(L) + N * a + r; alive = pi[:, v] < 0
            old = M[r][:, :, v]; m = old
            for h in range(H):
                p = pi[grp, m]; m = np.where(p >= 0, np.take_along_axis(M[r], np.maximum(p, 0), 2), m)
            M[r][:, :, v] = np.where(alive[:, None], m, old)
            ix = m.reshape(8, 1, 16 * L)
            n = np.sum(np.take_along_axis(M[r], ix, 2).reshape(8, 16, 16, L) == v, axis=1)
            D = np.sum(np.abs(np.take_along_axis(X[r], ix, 2).reshape(8, 16, 16, L) - X[r][:, :, v][:, :, None, :]), axis=1)
            may = alive[:, None] & (pi[grp, m] < 0) & (m // N % C != a)
            k = np.argmax(np.where(may, 4096 * n - D, -2 ** 20), axis=1)[:, None]
            lanes.append(v); has.append(np.any(may, axis=1)); cand.append(np.take_along_axis(m, k, 1)[:, 0]); cnt.append(np.take_along_axis(n, k, 1)[:, 0])
        yes = []
        for r in range(N):
            q = (r + 1 + t % (N - 1)) % N
            s = cnt[r] + np.sum(np.take_along_axis(M[q], cand[r][:, None, :], 2) == lanes[r], axis=1)
            y = has[r] & (s >= T[r] + (A & 3)); before = np.add.accumulate(y.astype(np.int64), axis=1) - y
            yes.append(y & (before < CAP))
        cc = np.concatenate(cand, axis=1); yy = np.concatenate(yes, axis=1); vv = np.concatenate(lanes)
        won = np.zeros((8, N * L), bool)
        for g in range(8):
            j = np.nonzero(yy[g])[0]; u, first = np.unique(cc[g, j], return_index=True); won[g, j[first]] = True
        for r in range(N):
            v = lanes[r]; lose = has[r] & ~won[:, r * L:r * L + L]; x = X[r][:, :, v]
            X[r][:, :, v] = np.where(lose[:, None], (x + np.take_along_axis(X[r], cand[r][:, None, :], 2)) >> 1, x)
        gg, jj = np.nonzero(won); pi[gg, vv[jj]] = cc[gg, jj]; pi[gg, cc[gg, jj]] = vv[jj]; A = int(np.sum(won))
    ym = np.stack([M[r].reshape(128, W)[:, r::N] for r in range(N)]); yx = np.stack([X[r].reshape(128, W)[:, r::N] for r in range(N)])
    return {"yp": np.stack([pi] * N).astype(np.float32), "ym": ym.astype(np.float32), "yx": yx.astype(np.float32).astype(BF)}

@@ -1,0 +1,629 @@
+import math
+from concourse.bass import DstId, RemoteDMATransfer
+from concourse.mybir import AluOpType as OP, AxisListType as AX, ActivationFunctionType as AF
+
+F32, BF, F16, I32, U16 = "float32", "bfloat16", "float16", "int32", "uint16"
+TW = 2560
+QW = 2056
+BIG = 8192.0
+HS = 524288.0
+FO = 64.0
+RND = 12582912.0
+CFG = {
+    "units": (("v", 0, 64), ("s", 64, 128), ("v", 128, 192), ("s", 192, 256)),
+    "abs0": (3, 5, 6, 7), "abs": (3, 4, 5, 6, 7),
+    "sint": True,
+    "gam": 1.56, "sig": 3.8, "pe": 0.42, "wake": 90.0, "hop": 3500.0, "look": 600.0, "slack": 60.0,
+    "keep": {}, "seed": 1, "turns": 90, "jit": 500.0,
+}
+
+
+def _sb(n, d):
+    return ("sbuf", [128, n], d)
+
+
+SCRATCH = {
+    "M": _sb(TW, I32), "Q0": _sb(QW, I32), "Q1": _sb(QW, I32), "Q2": _sb(QW, I32),
+    "F": _sb(TW, F32), "PI": _sb(TW, F32), "IO": _sb(TW, F32), "X0": _sb(TW, BF), "X1": _sb(TW, BF),
+    "VR0": _sb(4096, F16), "VR1": _sb(4096, F16), "o0": _sb(256, U16),
+    "E": _sb(4096, BF), "GX": _sb(4096, BF), "MX": _sb(4096, BF), "GF": _sb(4096, F16), "SK": _sb(2048, F16),
+    "Pi": _sb(8, I32), "Pf": _sb(16, F32), "I16": _sb(256, F32), "SEED": _sb(256, F32), "J": _sb(96, I32), "Jf": _sb(48, F32),
+    "SEG": _sb(256, F32), "DIAG": _sb(64, F32), "TB": _sb(128, BF), "ONE": _sb(320, BF), "SG2": _sb(640, BF),
+    "WE": _sb(144, BF), "WM": _sb(144, BF), "WG": _sb(144, BF), "WA": _sb(144, BF), "BC": _sb(512, BF),
+    "ID": _sb(128, BF), "NID": _sb(128, BF), "IDH": _sb(128, F16), "NIH": _sb(128, F16), "NIF": _sb(128, F32),
+    "BO": _sb(128, BF), "BO16": _sb(128, BF), "BOC": _sb(128, BF), "BON": _sb(128, BF), "O16": _sb(128, F32),
+    "M16": _sb(16, F32), "VL0": _sb(256, F32), "VL1": _sb(256, F32), "TC": _sb(16, F32), "B4": _sb(64, F32),
+    "L0": _sb(16, U16), "L1": _sb(16, U16), "PERM": _sb(16, U16), "ENDS": _sb(16, U16), "OW": _sb(16, U16),
+    "thi": _sb(8, I32), "thb": _sb(8, BF), "THR": _sb(8, F32), "Ai": _sb(8, I32), "CNT": _sb(8, F32),
+    "o1": _sb(256, U16), "o2": _sb(256, U16), "oc": _sb(256, U16), "cO": _sb(16, U16), "idx": _sb(8, U16),
+    "m2": _sb(256, F32), "mp": _sb(288, F32), "vF": _sb(256, F32), "mW": _sb(544, F32), "OM": _sb(512, F16),
+    "XN0": _sb(256, BF), "XN1": _sb(256, BF), "XT": _sb(256, BF), "DB": _sb(256, BF), "XTT": _sb(256, BF),
+    "pm": _sb(256, F32), "ks": _sb(256, F32), "oh": _sb(256, F32), "val": _sb(256, F32), "sc": _sb(256, F32),
+    "E1": _sb(256, BF), "E2": _sb(256, BF), "XC": _sb(256, BF), "cH": _sb(320, F32),
+    "yy": _sb(320, BF), "cum": _sb(320, BF), "le": _sb(640, F16), "les": _sb(640, F16), "junk": _sb(640, BF), "acc": _sb(8, F32),
+    "K": _sb(64, F32), "Mk": _sb(64, F32), "Ta": _sb(64, F32), "AB": _sb(256, F32), "U": _sb(8, F32), "nf": _sb(8, F32),
+    "LA0": _sb(512, U16), "LA1": _sb(512, U16), "LA2": _sb(512, U16),
+    "c1": _sb(48, U16), "c2": _sb(16, U16), "v1": _sb(48, U16),
+    "vR": _sb(256, F32), "cR": _sb(768, F16), "d1": _sb(256, F32), "d2": _sb(256, F16), "won": _sb(768, F32),
+    "w": _sb(256, F32), "w2": _sb(256, F32), "XG": _sb(256, BF), "wb": _sb(256, BF), "BG": _sb(64, BF),
+    "av": _sb(256, F16), "hb": _sb(256, BF), "xh": _sb(768, F16), "sh": _sb(768, F16),
+    "al": _sb(256, BF), "am": _sb(256, BF), "pr": _sb(256, BF), "ph": _sb(256, F16), "YM": _sb(512, F32), "YX": _sb(512, BF),
+    "KA": ("psum", [128, 512], F32), "KB": ("psum", [128, 512], F32), "XL": ("psum", [128, 512], F32),
+    "EA": ("psum", [128, 512], F32), "EB": ("psum", [128, 512], F32), "EC": ("psum", [128, 512], F32),
+    "VO": ("psum", [128, 512], F32), "MI": ("psum", [128, 512], F32),
+}
+DMAS = ["lm0", "lm1", "lx1", "lx0", "lth", "lp", "sp", "sm", "sx"]
+REMS = ["q0", "q1", "q2", "a0", "a1", "a2", "tq0", "tq1", "tq2", "ta0", "ta1", "ta2"]
+SEMAPHORES = ["sv", "ss", "st", "sg"] + DMAS + REMS
+
+
+def _masks(topo, src, dsts):
+    far = [d for d in dsts if d not in topo.cores_of(src)]
+    near = [d for d in dsts if d in topo.cores_of(src)]
+    out, used = {}, []
+    for n, d in enumerate(far):
+        e = topo.engines(src, d)
+        per = len(e) // len(far)
+        out[d] = e[n * per:(n + 1) * per]
+        used += e
+    for n, d in enumerate(near):
+        e = [x for x in topo.engines(src, d) if x not in used]
+        per = min([len(e) // len(near)] + [len(out[x]) for x in far])
+        out[d] = e[n * per:(n + 1) * per]
+    return out
+
+
+def _deps(ops):
+    hist, out = {}, []
+    for n, (q, fn, rd, wr, sem, inc, cost, lat) in enumerate(ops):
+        dep = {}
+        for mode, regs in (("r", rd), ("w", wr)):
+            for (name, lo, hi, st) in regs:
+                bank = SCRATCH[name][0] == "psum"
+                for (m, mo, l2, h2, st2) in hist.get(name, []):
+                    plain = ops[m][4] is None and sem is None
+                    same = ops[m][0] == q and plain
+                    if bank and (not same or q == "t"):
+                        hard = not same
+                    elif l2 >= hi or lo >= h2 or (mode == "r" and mo == "r") or (
+                            plain and (lo - l2) % (math.gcd(st * (hi - lo > 1), st2 * (h2 - l2 > 1)) or 1)):
+                        continue
+                    else:
+                        hard = not (same and mode == "w" and mo == "r")
+                    dep[m] = dep.get(m, False) or hard
+        out.append(dep)
+        for mode, regs in (("r", rd), ("w", wr)):
+            for (name, lo, hi, st) in regs:
+                hist.setdefault(name, []).append((n, mode, lo, hi, st))
+    return out
+
+
+def _graph(ops, soft, mid):
+    dep = _deps(ops)
+    for n in mid:
+        for m in [m for m in dep[n] if m in mid]:
+            del dep[n][m]
+    last = {}
+    for n, o in enumerate(ops):
+        if o[0] in ("g", "y"):
+            if o[0] in last:
+                dep[n].setdefault(last[o[0]], False)
+            last[o[0]] = n
+        if o[0] is None and o[1] is not None:
+            dep[n][[m for m in range(n) if ops[m][4] == o[1]][0]] = True
+    lev = [0.0] * len(ops)
+    hint = dict(soft)
+    for n in range(len(ops) - 1, -1, -1):
+        lev[n] += ops[n][6] + ops[n][7] + 1.0
+        for m, hard in dep[n].items():
+            lev[m] = max(lev[m], lev[n] + (CFG["wake"] if hard else -ops[m][7]))
+        if n in hint:
+            lev[hint[n]] = max(lev[hint[n]], lev[n])
+    return [{m: (ops[m][7] + CFG["wake"] if hard else 0.0) for m, hard in d.items()} for d in dep], lev
+
+
+def _plan(ops, dep, lev):
+    back = [{} for _o in ops]
+    for n, d in enumerate(dep):
+        for m, x in d.items():
+            back[m][n] = x
+    best, seed = None, CFG["seed"]
+    for it in range(CFG["turns"]):
+        out, end = _order(ops, dep, lev, [0.0] * len(ops))
+        span = max(end[n] + ops[n][7] for n in out)
+        if best is None or span < best[0]:
+            best = (span, out, end)
+        if it % 3 == 2:
+            end = best[2]
+        rank = []
+        for x in end:
+            seed = (seed * 1103515245 + 12345) % 2147483648
+            rank.append(x + CFG["jit"] * seed / 2147483648)
+        lev = _order(ops, back, rank, [0.0 if back[n] else o[7] for n, o in enumerate(ops)])[1]
+    return best
+
+
+def _order(ops, dep, lev, ready):
+    succ = [[] for _o in ops]
+    left = [len(d) for d in dep]
+    for n, d in enumerate(dep):
+        for m in d:
+            succ[m].append(n)
+    ends, free, pool, out = [0.0] * len(ops), {}, {}, []
+    for n in range(len(ops)):
+        if not left[n]:
+            pool.setdefault(ops[n][0], []).append(n)
+    while len(out) < len(ops):
+        best = None
+        for q, p in pool.items():
+            if p:
+                t0 = max(free.get(q, 0.0) if q else 0.0, min(ready[n] for n in p))
+                if best is None or t0 < best[0]:
+                    best = (t0, q)
+        t0, q = best
+        top = max((n for n in pool[q] if ready[n] <= t0 + CFG["look"]), key=lambda z: (lev[z], -z))
+        fit = [n for n in pool[q] if max(ready[n], t0) + ops[n][6] <= ready[top] + CFG["slack"]]
+        n = max(fit, key=lambda z: (lev[z], -z)) if fit and ready[top] > t0 else top
+        pool[q].remove(n)
+        end = max(ready[n], t0 if q else 0.0) + ops[n][6]
+        free[q] = ends[n] = end
+        out.append(n)
+        for k in succ[n]:
+            ready[k] = max(ready[k], end + dep[k][n])
+            left[k] -= 1
+            if not left[k]:
+                pool.setdefault(ops[k][0], []).append(k)
+    return out, ends
+
+
+def _emit(g, T, ops):
+    Q = {"v": g.vector, "s": g.scalar, "t": g.tensor, "g": g, "y": g.sync}
+    own = {"v": "sv", "s": "ss", "t": "st", "g": "sg"}
+    count = {k: 0 for k in SEMAPHORES}
+    known = {k: {} for k in Q}
+    done, dep = [], _deps(ops)
+    for n, (q, fn, rd, wr, sem, inc, cost, lat) in enumerate(ops):
+        if q is None:
+            count[sem] += inc
+            done.append((sem, count[sem], {}))
+            continue
+        need = {}
+        for m, hard in dep[n].items():
+            s, c, _k = done[m]
+            if hard and c > need.get(s, (0, 0))[0]:
+                need[s] = (c, m)
+        for s in sorted(need, key=lambda z: -need[z][1]):
+            c, m = need[s]
+            if known[q].get(s, 0) < c:
+                Q[q].wait_ge(T.sem[s], c)
+                known[q][s] = c
+                for s3, c3 in done[m][2].items():
+                    known[q][s3] = max(known[q].get(s3, 0), c3)
+        s = sem or own[q]
+        if s in REMS:
+            fn(Q[q])
+        else:
+            fn(Q[q]).then_inc(T.sem[s], inc)
+        count[s] += inc
+        done.append((s, count[s], dict(known[q])))
+    for s in SEMAPHORES:
+        if count[s] and max(known[q].get(s, 0) for q in Q) < count[s]:
+            g.wait_ge(T.sem[s], count[s])
+
+
+def rank_program(g, core, T, topo):
+    r = T.rank_of(core)
+    if r is None:
+        return
+    cores = list(T.cores)
+    N = len(cores)
+    ops, soft, tail, mid = [], [], {}, set()
+    sq = "s" if CFG["sint"] else "v"
+
+    def A(name, lo=0, hi=None, st=1, p=None):
+        hi = SCRATCH[name][1][1] if hi is None else hi
+        ps = slice(0, 128) if p is None else slice(*p)
+        return (T[name][ps, lo:hi:st] if st > 1 else T[name][ps, lo:hi], [(name, lo, hi, st)])
+
+    def C(name, c):
+        return A(name, c, c + 1)
+
+    def IN(win, off):
+        return (win[0].indirect(off[0]), win[1] + off[1], win[1], off[1])
+
+    def ap(x):
+        return x[0] if isinstance(x, tuple) else x
+
+    def size(x):
+        name, lo, hi, st = x[1][-1]
+        return (hi - lo + st - 1) // st * (16 if len(x) == 4 else 1)
+
+    def add(q, fn, out, ins, sem=None, inc=1, cost=None, lat=0.0, two=False):
+        rd, wr = [], []
+        full = [x for x in ins if isinstance(x, tuple)]
+        for x in full:
+            rd += x[1]
+        for x in out:
+            wr += x[2] if len(x) == 4 else x[1]
+            rd += x[3] if len(x) == 4 else []
+        if cost is None:
+            n = max(size(x) for x in full + out)
+            if len(out[0]) == 4:
+                cost = 50 + CFG["sig"] * 0.83 * size(out[0])
+            elif full and len(full[0]) == 4:
+                cost = 50 + CFG["gam"] * 0.83 * size(full[0])
+            else:
+                kinds = [SCRATCH[x[1][0][0]] for x in full + out if size(x) == n]
+                k = 0.5 if q == "v" and all(z[2] in (BF, F16, U16) for z in kinds) else 1.0
+                if two:
+                    k = 1.0 if any(z[0] == "psum" for z in kinds) else 2.0
+                cost = 30 + 0.83 * max(64, k * n)
+            cost *= 1.25
+        ops.append((q, fn, rd, wr, sem, inc, cost, lat))
+
+    def chain(key):
+        if key in tail:
+            soft.append((len(ops) - 1, tail[key]))
+        tail[key] = len(ops) - 1
+
+    def cp(o, i):
+        add("v", lambda e: e.tensor_copy(o[0], i[0]), [o], [i])
+
+    def tt(o, a, b, op):
+        add("v", lambda e: e.tensor_tensor(o[0], a[0], b[0], op), [o], [a, b], two=True)
+
+    def ts(o, a, s1, op0, s2=None, op1=None):
+        if op1 is None:
+            add("v", lambda e: e.tensor_scalar(o[0], a[0], ap(s1), None, op0), [o], [a, s1])
+        else:
+            add("v", lambda e: e.tensor_scalar(o[0], a[0], ap(s1), ap(s2), op0, op1), [o], [a, s1, s2])
+
+    def scan(o, a, b, op0, op1):
+        add("v", lambda e: e.tensor_tensor_scan(o[0], a[0], b[0], 0.0, op0, op1), [o], [a, b])
+
+    def ms(o, c):
+        add("v", lambda e: e.memset(o[0], c), [o], [])
+
+    def act(o, i, f=AF.Identity, bias=0.0, scale=1.0, acc=None):
+        if acc is None:
+            add("s", lambda e: e.activation(o[0], i[0], f, bias=ap(bias), scale=ap(scale)), [o], [i, bias, scale])
+        else:
+            add("s", lambda e: e.activation(o[0], i[0], f, bias=ap(bias), scale=scale, accum_out=acc[0]), [o, acc], [i, bias])
+
+    def fill(o, c):
+        act(o, A("SEED", 0, size(o)), bias=c, scale=0.0)
+
+    def lin(q, o, i, bias=0.0):
+        if q == "s":
+            act(o, i, bias=bias)
+        elif bias:
+            ts(o, i, bias, OP.add)
+        else:
+            cp(o, i)
+
+    def mm(o, l, x, a, b):
+        c = 1.25 * CFG["pe"] * max(64, size(x)) * (4 if SCRATCH[x[1][0][0]][2] == F32 else 1)
+        add("t", lambda e: e.matmul(o[0], l[0], x[0], a, b), [o], [l, x], cost=c, lat=100.0)
+        if not a and not b:
+            mid.add(len(ops) - 1)
+
+    def iota(o, pat, base, ch, fl=True):
+        c = 1.25 * (130 + 1.66 * size(o))
+        if fl:
+            add("g", lambda e: e.iota(o[0], pat, base, ch, allow_small_or_imprecise_dtypes=True), [o], [], cost=c)
+        else:
+            add("g", lambda e: e.iota(o[0], pat, base, ch), [o], [], cost=c)
+
+    def dma(q, o, i, out, ins, sem, lat):
+        add(q, lambda e: e.dma_start(o, i), out, ins, sem, 16, cost=60.0, lat=lat)
+
+    def send_table(t, after):
+        d = cores[(r - 1 - t) % N]
+        rid, pid = topo.addr(d, core)
+        src = A("M", 0, QW)
+        add("g", lambda e: e.remote_dma(T["Q%d" % t][:, :], src[0], T.sem["q%d" % t], T.sem["tq%d" % t], pid, rid, topo.mask(core, d)),
+            [], [src] + after, "tq%d" % t, len(topo.engines(core, d)), cost=500.0, lat=10000.0)
+        add(None, "tq%d" % t, [A("Q%d" % t)], [], "q%d" % t, len(topo.engines(cores[(r + 1 + t) % N], core)), cost=0.0)
+
+    def send_lists(t):
+        peers = [c for c in cores if c != core]
+        mk = _masks(topo, core, peers)
+        src = A("LA%d" % t, 128 * r, 128 * r + 128)
+        trs = []
+        for d in peers:
+            rid, pid = topo.addr(d, core)
+            trs.append(RemoteDMATransfer(dst_ids=[DstId(rid=rid, pnc=pid)], dma_engine_mask=sum(1 << x for x in mk[d]),
+                                         remote_sem=T.sem["a%d" % t], src=src[0], dst=src[0]))
+        add("g", lambda e: e.remote_dma_fused(trs, local_sem=T.sem["ta%d" % t]), [], [src], "ta%d" % t,
+            sum(len(mk[d]) for d in peers), cost=500.0, lat=CFG["hop"] - 500.0)
+        n = sum(len(_masks(topo, s, [c for c in cores if c != s])[core]) for s in peers)
+        add(None, "ta%d" % t, [A("LA%d" % t, 128 * j, 128 * j + 128) for j in range(N) if j != r], [], "a%d" % t, n, cost=0.0)
+
+    def own(name, a):
+        return A(name, 4 * a + r, 2048, 8)
+
+    ms(A("thi"), 0)
+    dma("y", T.M[:, 0:1024], T.mt[:, 0:1024], [A("M", 0, 1024)], [], "lm0", 4000.0)
+    dma("s", T.M[:, 1024:2048], T.mt[:, 1024:2048], [A("M", 1024, 2048)], [], "lm1", 4000.0)
+    dma("y", T.X1[:, 0:2048], T.xv[:, :], [A("X1", 0, 2048), C("Ai", 7)], [], "lx1", 4500.0)
+    dma("y", T.thi[0:128:16, 0:1], T.th[:], [A("thi")], [], "lth", 2500.0)
+    dma("y", T.X0[:, 0:2048], T.xv[:, :], [A("X0", 0, 2048)], [C("Ai", 7)], "lx0", 3500.0)
+
+    iota(A("SEED"), [[128, 16], [0, 16]], 0, 0)
+    iota(A("J", 0, 16), [[8, 16]], r, 128, False)
+    iota(C("Pi", 0), [[0, 1]], 0, 1, False)
+    iota(A("IO", 0, 256), [[1, 256]], 0, 0)
+    iota(A("J", 16, 32), [[1, 16]], 0, 16, False)
+    iota(A("I16"), [[0, 16], [1, 16]], 0, 0)
+    iota(A("J", 32, 48), [[16, 16]], 0, 1, False)
+    iota(A("M", 2048, TW), [[0, TW - 2048]], -1, 0, False)
+    send_table(0, [])
+    for o, c in ((A("mp", 0, 16), 0), (A("mp", 272, 288), 0), (A("X1", 2048, TW), 32768), (A("PI", 0, 256), -1)):
+        iota(o, [[0, size(o)]], c, 0)
+    iota(A("VL0"), [[8, 256]], r, 0)
+    iota(A("IO", 256, TW), [[1, TW - 256]], 256, 0)
+    iota(A("yy", 256, 320), [[0, 64]], 1, 0)
+    iota(A("B4"), [[4096, 64]], 0, 0)
+    iota(A("SG2"), [[0, 640]], 1, 0)
+    iota(A("SG2", 320, 321), [[0, 1]], 0, 0)
+    iota(A("X0", 2048, TW), [[0, TW - 2048]], 32768, 0)
+    iota(A("VL1"), [[8, 256]], r + 4, 0)
+    iota(A("BG"), [[0, 64]], int(BIG), 0)
+    ts(A("VR0", 0, 256), A("SEED"), float(r), OP.add)
+    for n in (256, 512, 1024):
+        ts(A("VR0", n, 2 * n), A("VR0", 0, n), n / 32.0, OP.add)
+    for p in range(8, 16):
+        act(A("VR0", 256 * p, 256 * p + 256), A("SEED"), bias=float(8 * p + r))
+    ts(A("J", 48, 64), A("J", 0, 16), 2047, OP.bitwise_and)
+    cp(A("L0"), A("J", 48, 64))
+    ts(A("L1"), A("J", 48, 64), 4.0, OP.add)
+    ts(A("J", 64, 80), A("J", 16, 32), 255, OP.bitwise_and)
+    cp(A("PERM"), A("J", 64, 80))
+    ts(C("Pi", 1), C("Pi", 0), 15, OP.bitwise_and)
+    ts(C("Pi", 2), C("Pi", 0), 4, OP.logical_shift_right)
+    ts(C("Pi", 3), C("Pi", 0), 31, OP.bitwise_and)
+    cp(A("Pf", 0, 4), A("Pi", 0, 4))
+    act(C("Pf", 6), C("Pf", 2), bias=15.0, scale=16.0)
+    act(C("Pf", 7), C("Pf", 2), scale=128.0)
+    act(C("Pf", 8), C("Pf", 2), scale=-16.0)
+    act(C("Pf", 9), C("Pf", 3), scale=128.0)
+    act(C("Pf", 10), C("Pf", 3), scale=128.0, bias=-2048.0)
+    ts(A("ID"), A("IO", 0, 128), C("Pf", 0), OP.is_equal)
+    ts(A("WE"), A("IO", 0, 144), C("Pf", 6), OP.is_equal, 65536.0, OP.mult)
+    ts(A("BO"), A("SEED", 0, 128), C("Pf", 7), OP.is_equal)
+    ts(A("BC", 0, 256), A("SEED"), C("Pf", 9), OP.is_equal)
+    ts(A("BC", 256, 512), A("SEED"), C("Pf", 10), OP.is_equal)
+    for nm, wt in (("WG", 16.0), ("WM", -32.0), ("WA", -16.0)):
+        act(A(nm), A("WE"), scale=wt / 65536.0)
+    for nm, wt in (("BO16", 0.0625), ("BOC", 8192.0), ("BON", -1.0 / 8192)):
+        act(A(nm), A("BO"), scale=wt)
+    for nm, wt in (("NID", -1.0), ("IDH", 1.0), ("NIH", -1.0), ("NIF", -1.0)):
+        act(A(nm), A("ID"), scale=wt)
+    ms(A("ONE"), 1.0)
+    act(A("TB"), A("I16", 0, 128), bias=16.0, scale=-1.0)
+    act(A("SEG"), A("I16"), AF.Sign)
+    ts(A("DIAG"), A("I16", 0, 64), C("Pf", 1), OP.is_equal)
+    ts(A("ENDS"), A("IO", 0, 16), 16.0, OP.mult, 15.0, OP.add)
+    ts(A("J", 80, 96), A("J", 32, 48), 4, OP.logical_shift_right, 1, OP.bitwise_and)
+    ts(A("Jf", 0, 16), A("J", 32, 48), C("Pf", 8), OP.add)
+    ts(A("Jf", 16, 32), A("J", 80, 96), 272.0, OP.mult)
+    tt(A("Jf", 32, 48), A("Jf", 0, 16), A("Jf", 16, 32), OP.add)
+    cp(A("OW"), A("Jf", 32, 48))
+    act(A("TC", 0, 4), A("IO", 0, 4), bias=C("Pf", 1), scale=16.0)
+    act(A("TC", 4, 8), A("TC", 0, 4), bias=0.5)
+    act(A("TC", 8, 12), A("TC", 0, 4), scale=4096.0)
+    act(A("TC", 12, 16), A("TC", 0, 4), AF.Silu, bias=float(QW))
+    ts(A("M16"), A("IO", 0, 16), C("Pf", 1), OP.is_equal)
+    for o, c in ((A("O16"), 0.0625), (A("cH", 256, 320), 4000.0 * HS)):
+        fill(o, c)
+    for t in range(3):
+        ms(A("LA%d" % t, 128 * r, 128 * r + 128, 2), 0)
+    for k in range(16):
+        act(A("SK", 128 * k, 128 * k + 128), A("ID"), scale=C("M16", k))
+    for n in range(1, TW // 256):
+        dma("y", T.PI[:, 256 * n:256 * n + 256], T.PI[:, 0:256], [A("PI", 256 * n, 256 * n + 256)], [A("PI", 0, 256)], "lp", 2500.0)
+    iota(A("F"), [[1, TW]], int(FO), 0)
+    cp(C("thb", 0), C("thi", 0))
+
+    def choose(a, blocks, oc):
+        for h in range(2):
+            mm(A("MI", 128 * h, 128 * h + 128), A("XT", 128 * h, 128 * h + 128), A("ID"), True, a is None)
+            if a is not None:
+                mm(A("MI", 128 * h, 128 * h + 128), A("DB", 128 * h, 128 * h + 128), A("ID"), False, True)
+        act(A("XTT"), A("MI", 0, 256))
+        a = a or 0
+        for kb in ("KA", "KB"):
+            mm(A(kb, 0, 128), A("BO16"), A("TB"), True, False)
+        for n in range(8):
+            lo, hi = 512 * n, 512 * n + 512
+            tt(A("E", lo, hi), IN(A("M", 0, 2048), A(oc, 32 * n, 32 * n + 32)), A("VR%d" % a, lo, hi), OP.is_equal)
+            chain("v")
+            act(A("GX", lo, hi), IN(A("X%d" % (1 - a), 0, 2048), A(oc, 32 * n, 32 * n + 32)))
+            chain("s")
+            bank, ps = A(("XL", "MI")[n % 2]), (32 * (n % 4), 32 * (n % 4) + 32)
+            mm(bank, A("XTT", 128 * (n // 4), 128 * (n // 4) + 128, p=ps), A("BC", p=ps), True, n not in blocks)
+            if n in blocks:
+                mm(bank, A("NID"), A("GX", lo, hi), False, True)
+                act(A("MX", lo, hi), bank, AF.Abs)
+                use = (("E", "WE"), ("MX", "WA"))
+            else:
+                tt(A("MX", lo, hi), A("GX", lo, hi), bank, OP.max)
+                use = (("E", "WE"), ("GX", "WG"), ("MX", "WM"))
+            for src, wn in use:
+                for p in (2 * n, 2 * n + 1):
+                    for b, kb in enumerate(("KA", "KB")):
+                        c = 256 * p + 128 * b
+                        mm(A(kb, 0, 128), A(wn, 15 - p, 143 - p), A(src, c, c + 128), False, False)
+        for kb in ("KA", "KB"):
+            mm(A(kb, 0, 128), A("BOC"), A("ONE", 0, 128), False, True)
+
+    def follow(src, dst, col):
+        for (q, lo, hi), bank in zip(CFG["units"], ("EA", "EB", "EC", "VO")):
+            lin(q, A("GF", 16 * lo, 16 * hi), IN(A("F", 0, 2048), A(src, lo, hi)), -FO)
+            chain(q)
+            o = A(bank, col, col + hi - lo)
+            for k in range(16):
+                mm(o, A("SK", 128 * k, 128 * k + 128), A("GF", 16 * lo + k, 16 * hi, 16), k == 0, k == 15)
+            cp(A(dst, lo, hi), o)
+            if col:
+                act(A("m2", lo, hi), o, bias=RND)
+
+    def marks(t):
+        a, z = t % 2, (256 * t, 256 * t + 256)
+        mm(A("EB", 0, 256), A("IDH"), A("cR", *z), True, True)
+        mm(A("EC", 0, 256), A("IDH"), A("sh", *z), True, False)
+        mm(A("EC", 0, 256), A("NIH"), A("xh", *z), False, True)
+        tt(A("w2"), A("won", *z), A("EB", 0, 256), OP.mult)
+        ts(IN(A("PI"), A("v1", 16 * t, 16 * t + 16)), A("w2"), 1.0, OP.mult, -1.0, OP.add)
+        if t == 2:
+            dma("y", T.yp[:, :], T.PI[0:128:16, 0:2048], [], [A("PI")], "sp", 2200.0)
+        else:
+            act(A("al"), own("PI", a), AF.Relu, scale=-1.0)
+        tt(A("pr"), A("al"), A("EC", 0, 256), OP.mult)
+        mm(A("EB", 256, 512), A("ID"), A("XN%d" % a), True, False)
+        mm(A("EB", 256, 512), A("ID"), A("pr"), False, True)
+        act(A("XN0") if t == 0 else A("YX", a, 512, 2), A("EB", 256, 512))
+
+    for t in range(3):
+        a = t % 2
+        off = 4 * a + r
+        z = (256 * t, 256 * t + 256)
+        if t == 0:
+            cp(A("o0"), IN(A("M", 0, 2048), A("L0")))
+            act(A("XN0"), own("X1", 0))
+            act(A("XT"), IN(A("XN0"), A("PERM")))
+            for j in range(4):
+                ms(A("X1", j, 2048, 8), BIG)
+            act(A("XN1"), own("X1", 1))
+            lin(sq, A("mp", 16, 272), own("M", 0), -2048.0)
+            for b in range(2):
+                lin(sq, A("OM", 256 * b, 256 * b + 256), own("M", b), -2048.0)
+            mm(A("VO", 0, 1), A("BO"), C("thb", 0), True, True)
+            act(C("THR", 0), A("VO", 0, 1), bias=-0.5)
+            choose(None, CFG["abs0"], "o0")
+        else:
+            act(A("DB"), IN(A("PI", 0, 2048), A("L%d" % a)), AF.Relu, bias=32768.0, scale=32768.0)
+            act(A("am"), own("PI", a), AF.Relu, scale=-1.0)
+            mm(A("XL", 0, 1), A("O16"), C("CNT", 0), True, True)
+            cp(C("Ai", 0), A("XL", 0, 1))
+            ts(C("Ai", 1), C("Ai", 0), 3, OP.bitwise_and)
+            ts(C("THR", t), C("Ai", 1), C("THR", 0), OP.add)
+            follow("o%d" % a, "o2", 0)
+            follow("o2", "oc", 256)
+            act(A("mp", 16, 272), IN(A("m2"), A("PERM")), bias=-2048.0 - RND)
+            choose(a, CFG["abs"], "oc")
+        add("v", lambda e: e.transpose(T.mW[:, 0:256], T.mp[:, 16:272]), [A("mW", 0, 256)], [A("mp", 16, 272)])
+        add("v", lambda e: e.transpose(T.mW[:, 256:544], T.mp[:, 0:288]), [A("mW", 256, 544)], [A("mp")])
+
+        scan(A("pm", 0, 128), A("SEG", 0, 128), A("KA", 0, 128), OP.mult, OP.max)
+        act(A("ks", 128, 256), A("KB", 0, 128))
+        scan(A("pm", 128, 256), A("SEG", 0, 128), A("KB", 0, 128), OP.mult, OP.max)
+        act(A("ks", 0, 128), A("KA", 0, 128))
+        tt(A("oh"), IN(A("pm"), A("ENDS")), A("ks"), OP.is_equal)
+        tt(A("val"), IN(A("mW"), A("OW")), A("oh"), OP.mult)
+        scan(A("sc"), A("SEG"), A("val"), OP.mult, OP.add)
+        ts(A("cO"), A("sc", 15, 256, 16), 2048.0, OP.add)
+        act(A("XC"), IN(A("X%d" % (1 - a), 0, 2064), A("cO")))
+        tt(A("E1"), IN(A("M", 0, QW), A("cO")), A("VL%d" % a), OP.is_equal)
+        tt(A("E2"), IN(A("Q%d" % t), A("cO")), A("VL%d" % a), OP.is_equal)
+        act(A("cH", 0, 256), IN(A("IO", 0, QW), A("cO")), scale=HS)
+        mm(A("VO", 0, 256), A("BO"), A("E1"), True, False)
+        mm(A("VO", 0, 256), A("BON"), A("XC"), False, False)
+        mm(A("VO", 0, 256), A("BO"), A("E2"), False, True)
+        ts(A("yy", 0, 256), A("VO", 0, 256), C("THR", t), OP.is_ge)
+        scan(A("cum"), A("ONE"), A("yy"), OP.mult, OP.add)
+        for s in (2, 3):
+            act(A("junk", 320 * s - 640, 320 * s - 320), A("cum"), AF.Sign, bias=C("TC", 4 + s), scale=-1.0, acc=C("acc", s))
+        for s in (0, 1):
+            ts(A("le", 320 * s, 320 * s + 320), A("cum"), C("TC", s), OP.is_le)
+        scan(A("les"), A("SG2"), A("le"), OP.mult, OP.add)
+        cp(A("idx", 0, 2), A("les", 319, 640, 320))
+        ts(A("idx", 2, 4), A("acc", 2, 4), 0.5, OP.mult, 160.0, OP.add)
+        la, b0 = "LA%d" % t, 128 * r
+        ts(A(la, b0 + 1, b0 + 128, 2), IN(A("IO", 0, 320), A("idx", 0, 4)), 8.0, OP.mult, float(off), OP.add)
+        tt(A("Mk"), IN(A("cH"), A("idx", 0, 4)), A("DIAG"), OP.mult)
+        tt(A("K"), IN(A("cH"), A("idx", 0, 4)), A("B4"), OP.subtract)
+        scan(A("Ta"), A("SEG", 0, 64), A("Mk"), OP.mult, OP.add)
+        for s in range(4):
+            act(A("AB", 64 * s, 64 * s + 64), A("K"), AF.Abs, bias=C("Ta", 16 * s + 15), scale=-1.0)
+        ts(A("U", 0, 4), A("Ta", 15, 64, 16), 1.0 / HS, OP.mult)
+        ts(A(la, b0 + 4, b0 + 128, 32), A("idx", 0, 4), 8.0, OP.mult, float(off), OP.add)
+        tt(A("U", 4, 8), A("U", 0, 4), A("TC", 8, 12), OP.add)
+        ts(A(la, b0 + 2, b0 + 128, 32), A("U", 0, 4), 2048.0, OP.min)
+        for s in range(4):
+            add("v", lambda e, s=s: e.tensor_reduce(T.nf[:, s:s + 1], T.AB[:, 64 * s:64 * s + 64], AX.X, OP.min, negate=True),
+                [C("nf", s)], [A("AB", 64 * s, 64 * s + 64)])
+        for s in range(4):
+            ts(C(la, b0 + 32 * s), C("nf", s), C("U", 4 + s), OP.add, C("TC", 12 + s), OP.min)
+        send_lists(t)
+
+        mm(A("MI", 0, 256), A("ID"), A("XC"), True, False)
+        mm(A("MI", 0, 256), A("ID"), A("XN%d" % a), False, True)
+        act(A("av"), A("MI", 0, 256), bias=1535.75, scale=0.5)
+        act(A("hb"), A("XC"), AF.Relu, bias=1024.0, scale=-1.0)
+        act(A("xh", *z), A("XN%d" % a), bias=1536.0)
+        mm(A("XL", 0, 256), A("IDH"), A("xh", *z), True, False)
+        mm(A("XL", 0, 256), A("ID"), A("hb"), False, True)
+        tt(A("sh", *z), A("av"), A("XL", 0, 256), OP.min)
+        if t < 2:
+            act(own("X%d" % a, a), A("sh", *z), bias=-1536.0)
+        if t == 0:
+            cp(A("o1"), IN(A("M", 0, 2048), A("L1")))
+            ops[-1][2].extend(A(la, b0, b0 + 16)[1])
+            for h in range(2):
+                ts(A("VR1", 2048 * h, 2048 * h + 2048), A("VR0", 2048 * h, 2048 * h + 2048), 4.0, OP.add)
+                ops[-1][2].extend(A(la, b0, b0 + 16)[1])
+            for j in range(4):
+                ms(A("X0", 4 + j, 2048, 8), BIG)
+                ops[-1][2].extend(A(la, b0, b0 + 16)[1])
+        if t > 0:
+            om = A("OM", 256 * a, 256 * a + 256)
+            mm(A("EA", 0, 256), A("NIF"), A("mp", 16, 272), True, False)
+            mm(A("EA", 0, 256), A("IDH"), om, False, True)
+            tt(A("ph"), A("am"), A("EA", 0, 256), OP.mult)
+            mm(A("EA", 256, 512), A("IDH"), om, True, False)
+            mm(A("EA", 256, 512), A("NIH"), A("ph"), False, True)
+            act(A("YM", a, 512, 2), A("EA", 256, 512), bias=2048.0)
+            marks(t - 1)
+        if t == 1:
+            cp(own("M", 1), A("YM", 1, 512, 2))
+            for j in range(N):
+                cp(IN(A("X1"), A("c1", 4 * j, 4 * j + 4)), A("BG"))
+        if t == 2:
+            dma("y", T.ym[:, :], T.YM[:, :], [], [A("YM")], "sm", 2500.0)
+        if t < 2:
+            act(A("XT"), IN(A("XN%d" % (1 - a)), A("PERM")))
+            send_table(t + 1, [A(la)])
+
+        v1, c0 = A("v1", 16 * t, 16 * t + 16), 16 * t
+        cp(v1, A(la, 4, 512, 32))
+        cp(A("c1", c0, c0 + 16), A(la, 0, 512, 32))
+        cp(A("c2"), A(la, 2, 512, 32))
+        act(A("vR"), IN(A("IO"), v1))
+        act(A("cR", *z), IN(A("IO", 0, QW), A("c2")), bias=1.0)
+        for j in range(N - 1, -1, -1):
+            cp(IN(A("PI"), A("c1", c0 + 4 * j, c0 + 4 * j + 4)), A(la, 128 * j + 1, 128 * j + 128, 2))
+        tt(A("won", *z), IN(A("PI"), A("c2")), A("vR"), OP.is_equal)
+        if t == 2:
+            tt(A("al"), IN(A("PI", 0, QW), A("cO")), A("VL0"), OP.not_equal)
+        if t < 2:
+            lin(sq, A("d2"), IN(A("M", 0, QW), A("c2")))
+            lin(sq, A("d1"), IN(A("M"), v1), FO)
+            ts(A("vF"), A("vR"), FO, OP.add)
+            mm(A("EA", 0, 256), A("NIF"), A("vR"), True, False)
+            mm(A("EA", 0, 256), A("IDH"), A("d2"), False, True)
+            for j in range(N - 1, -1, -1):
+                o, i = IN(A("F"), A("c1", c0 + 4 * j, c0 + 4 * j + 4)), A("d1", 64 * j, 64 * j + 64)
+                add("s", lambda e, o=o, i=i: e.activation(o[0], i[0], AF.Silu), [o], [i])
+            tt(A("w"), A("won", *z), A("EA", 0, 256), OP.mult)
+            tt(IN(A("F"), v1), A("vF"), A("w"), OP.add)
+            act(A("junk", 0, 256), A("won", *z), acc=C("CNT", 0))
+            act(A("XG"), IN(A("X%d" % a), v1))
+            act(A("wb"), A("won", *z), scale=BIG)
+            tt(IN(A("X%d" % a), v1), A("XG"), A("wb"), OP.add)
+    marks(2)
+    dma("s", T.yx[:, :], T.YX[:, :], [], [A("YX")], "sx", 2200.0)
+    if r not in CFG["keep"]:
+        dep, lev = _graph(ops, soft, mid)
+        CFG["keep"][r] = _plan(ops, dep, lev)
+    _emit(g, T, [ops[n] for n in CFG["keep"][r][1]])

@@ -3,18 +3,24 @@ from concourse.bass import DstId, RemoteDMATransfer
 from concourse.mybir import AluOpType as OP, AxisListType as AX, ActivationFunctionType as AF
 
 F32, BF, F16, I32, U16 = "float32", "bfloat16", "float16", "int32", "uint16"
-TW = 2560
-QW = 2056
-BIG = 8192.0
+TW = 2320
+SP = 2064
+LW = 72
+NS = 4
+BIG = 32768.0
+KU = 4096.0
 HS = 524288.0
-FO = 64.0
+FO = 65.0
 RND = 12582912.0
 CFG = {
-    "units": (("v", 0, 64), ("s", 64, 128), ("v", 128, 192), ("s", 192, 256)),
-    "abs0": (3, 5, 6, 7), "abs": (3, 4, 5, 6, 7),
-    "sint": True,
-    "gam": 1.56, "sig": 3.8, "pe": 0.42, "wake": 90.0, "hop": 3500.0, "look": 600.0, "slack": 60.0,
-    "keep": {}, "seed": 1, "turns": 90, "jit": 500.0,
+    "f1": tuple(("vs"[n % 2], 32 * n, 32 * n + 32) for n in range(8)),
+    "f2": tuple(("vs"[n % 2], 32 * n, 32 * n + 32) for n in range(8)),
+    "fg": ((0, 64), (64, 128), (128, 192), (192, 256)),
+    "sel": ((0, 128), (128, 192), (192, 256)),
+    "gb": 64, "mk": "vvss",
+    "abs0": (1, 3, 5, 6), "abs": (1, 2, 3, 4, 5, 6),
+    "gam": 1.56, "sig": 3.8, "pe": 0.42, "wake": 90.0, "hop": 3500.0, "look": 600.0, "slack": 60.0, "fac": 1.25, "gfac": 1.05,
+    "keep": {}, "seed": 1, "turns": 10, "jit": 500.0, "moves": 120000, "heat": 200.0, "mean": 0.3,
 }
 
 
@@ -23,36 +29,37 @@ def _sb(n, d):
 
 
 SCRATCH = {
-    "M": _sb(TW, I32), "Q0": _sb(QW, I32), "Q1": _sb(QW, I32), "Q2": _sb(QW, I32),
-    "F": _sb(TW, F32), "PI": _sb(TW, F32), "IO": _sb(TW, F32), "X0": _sb(TW, BF), "X1": _sb(TW, BF),
-    "VR0": _sb(4096, F16), "VR1": _sb(4096, F16), "o0": _sb(256, U16),
+    "M": _sb(TW, I32), "Q0": _sb(2048, I32), "Q1": _sb(2048, I32), "Q2": _sb(2048, I32),
+    "F": _sb(TW, F32), "PI": _sb(TW, F32), "IO": _sb(TW + 64, F32), "X0": _sb(TW, BF), "X1": _sb(TW, BF),
+    "VRH": _sb(2048, F16), "VR0": _sb(4096, F32), "VR1": _sb(4096, F32), "BC": _sb(2048, BF),
     "E": _sb(4096, BF), "GX": _sb(4096, BF), "MX": _sb(4096, BF), "GF": _sb(4096, F16), "SK": _sb(2048, F16),
-    "Pi": _sb(8, I32), "Pf": _sb(16, F32), "I16": _sb(256, F32), "SEED": _sb(256, F32), "J": _sb(96, I32), "Jf": _sb(48, F32),
-    "SEG": _sb(256, F32), "DIAG": _sb(64, F32), "TB": _sb(128, BF), "ONE": _sb(320, BF), "SG2": _sb(640, BF),
-    "WE": _sb(144, BF), "WM": _sb(144, BF), "WG": _sb(144, BF), "WA": _sb(144, BF), "BC": _sb(512, BF),
-    "ID": _sb(128, BF), "NID": _sb(128, BF), "IDH": _sb(128, F16), "NIH": _sb(128, F16), "NIF": _sb(128, F32),
-    "BO": _sb(128, BF), "BO16": _sb(128, BF), "BOC": _sb(128, BF), "BON": _sb(128, BF), "O16": _sb(128, F32),
-    "M16": _sb(16, F32), "VL0": _sb(256, F32), "VL1": _sb(256, F32), "TC": _sb(16, F32), "B4": _sb(64, F32),
-    "L0": _sb(16, U16), "L1": _sb(16, U16), "PERM": _sb(16, U16), "ENDS": _sb(16, U16), "OW": _sb(16, U16),
+    "Pi": _sb(8, I32), "Pf": _sb(16, F32), "I16": _sb(64, F32), "G16": _sb(128, F32), "SEED": _sb(256, F32),
+    "J": _sb(32, I32), "Jf": _sb(96, F32), "RS": _sb(256, F32), "DIAG": _sb(64, F32), "TB": _sb(128, BF),
+    "ONE": _sb(512, BF), "C15": _sb(256, BF),
+    "WE": _sb(144, BF), "WM": _sb(144, BF), "WG": _sb(144, BF), "WA": _sb(144, BF),
+    "ID": _sb(128, BF), "NID": _sb(128, BF), "NIH": _sb(128, F16), "IDF": _sb(128, F32), "IDB": _sb(128, BF), "IDN": _sb(128, BF),
+    "BO": _sb(128, BF), "BON": _sb(128, BF), "O16": _sb(128, F32),
+    "VL0": _sb(272, F32), "VL1": _sb(272, F32), "TC": _sb(24, F32), "B4": _sb(64, F32),
+    "L0": _sb(16, U16), "L1": _sb(16, U16), "PERM": _sb(16, U16), "OW": _sb(16, U16),
     "thi": _sb(8, I32), "thb": _sb(8, BF), "THR": _sb(8, F32), "Ai": _sb(8, I32), "CNT": _sb(8, F32),
-    "o1": _sb(256, U16), "o2": _sb(256, U16), "oc": _sb(256, U16), "cO": _sb(16, U16), "idx": _sb(8, U16),
-    "m2": _sb(256, F32), "mp": _sb(288, F32), "vF": _sb(256, F32), "mW": _sb(544, F32), "OM": _sb(512, F16),
-    "XN0": _sb(256, BF), "XN1": _sb(256, BF), "XT": _sb(256, BF), "DB": _sb(256, BF), "XTT": _sb(256, BF),
-    "pm": _sb(256, F32), "ks": _sb(256, F32), "oh": _sb(256, F32), "val": _sb(256, F32), "sc": _sb(256, F32),
-    "E1": _sb(256, BF), "E2": _sb(256, BF), "XC": _sb(256, BF), "cH": _sb(320, F32),
-    "yy": _sb(320, BF), "cum": _sb(320, BF), "le": _sb(640, F16), "les": _sb(640, F16), "junk": _sb(640, BF), "acc": _sb(8, F32),
-    "K": _sb(64, F32), "Mk": _sb(64, F32), "Ta": _sb(64, F32), "AB": _sb(256, F32), "U": _sb(8, F32), "nf": _sb(8, F32),
-    "LA0": _sb(512, U16), "LA1": _sb(512, U16), "LA2": _sb(512, U16),
-    "c1": _sb(48, U16), "c2": _sb(16, U16), "v1": _sb(48, U16),
-    "vR": _sb(256, F32), "cR": _sb(768, F16), "d1": _sb(256, F32), "d2": _sb(256, F16), "won": _sb(768, F32),
-    "w": _sb(256, F32), "w2": _sb(256, F32), "XG": _sb(256, BF), "wb": _sb(256, BF), "BG": _sb(64, BF),
-    "av": _sb(256, F16), "hb": _sb(256, BF), "xh": _sb(768, F16), "sh": _sb(768, F16),
-    "al": _sb(256, BF), "am": _sb(256, BF), "pr": _sb(256, BF), "ph": _sb(256, F16), "YM": _sb(512, F32), "YX": _sb(512, BF),
-    "KA": ("psum", [128, 512], F32), "KB": ("psum", [128, 512], F32), "XL": ("psum", [128, 512], F32),
-    "EA": ("psum", [128, 512], F32), "EB": ("psum", [128, 512], F32), "EC": ("psum", [128, 512], F32),
+    "o0": _sb(256, U16), "o1": _sb(256, U16), "o2": _sb(256, U16), "oc": _sb(256, U16), "cO": _sb(16, U16), "idx": _sb(8, U16),
+    "m2": _sb(256, F32), "mp": _sb(288, F32), "mW": _sb(544, F32), "OM": _sb(512, F16),
+    "XN0": _sb(256, BF), "XN1": _sb(256, BF), "XTT": _sb(256, BF), "dead": _sb(256, BF),
+    "pm": _sb(256, F32), "df": _sb(256, F32), "dn": _sb(256, F32), "sc": _sb(256, F32),
+    "E1": _sb(256, BF), "E2": _sb(256, BF), "XC": _sb(256, BF), "cH": _sb(272, F32),
+    "yy": _sb(256, BF), "cum": _sb(256, BF), "le": _sb(512, F16), "les": _sb(512, F16), "junk": _sb(512, BF), "acc": _sb(8, F32),
+    "K": _sb(64, F32), "Mk": _sb(64, F32), "Ta": _sb(64, F32), "AB": _sb(260, BF), "RB": _sb(260, BF), "U": _sb(8, F32), "nf": _sb(260, F32),
+    "LA0": ("sbuf", [128, 4, LW], U16), "LA1": ("sbuf", [128, 4, LW], U16), "LA2": ("sbuf", [128, 4, LW], U16),
+    "c1": _sb(48, U16), "v1": _sb(48, U16),
+    "vF": _sb(256, F32), "cR": _sb(256, F32), "d1": _sb(256, F32), "d2": _sb(256, F16), "won": _sb(768, F32),
+    "w": _sb(256, F32), "w2": _sb(256, F32), "XG": _sb(256, BF), "wb": _sb(256, BF), "van": _sb(768, BF), "IDH": _sb(128, F16),
+    "av": _sb(256, F16), "hb": _sb(256, BF), "sh": _sb(768, F16),
+    "al": _sb(256, BF), "pr": _sb(256, BF), "ph": _sb(256, F16), "YM": _sb(512, F32), "YX": _sb(512, BF),
+    "KA": ("psum", [128, 512], F32), "KB": ("psum", [128, 512], F32), "XA": ("psum", [128, 512], F32),
+    "XB": ("psum", [128, 512], F32), "FA": ("psum", [128, 512], F32), "FB": ("psum", [128, 512], F32),
     "VO": ("psum", [128, 512], F32), "MI": ("psum", [128, 512], F32),
 }
-DMAS = ["lm0", "lm1", "lx1", "lx0", "lth", "lp", "sp", "sm", "sx"]
+DMAS = ["lm0", "lm1", "lx1", "lx0", "lth", "lp", "lf", "sp", "sm", "sx"]
 REMS = ["q0", "q1", "q2", "a0", "a1", "a2", "tq0", "tq1", "tq2", "ta0", "ta1", "ta2"]
 SEMAPHORES = ["sv", "ss", "st", "sg"] + DMAS + REMS
 
@@ -89,7 +96,7 @@ def _deps(ops):
                             plain and (lo - l2) % (math.gcd(st * (hi - lo > 1), st2 * (h2 - l2 > 1)) or 1)):
                         continue
                     else:
-                        hard = not (same and mode == "w" and mo == "r")
+                        hard = True
                     dep[m] = dep.get(m, False) or hard
         out.append(dep)
         for mode, regs in (("r", rd), ("w", wr)):
@@ -98,10 +105,10 @@ def _deps(ops):
     return out
 
 
-def _graph(ops, soft, mid):
+def _graph(ops, soft, mid, spare):
     dep = _deps(ops)
     for n in mid:
-        for m in [m for m in dep[n] if m in mid]:
+        for m in [m for m in dep[n] if mid.get(m) == mid[n]]:
             del dep[n][m]
     last = {}
     for n, o in enumerate(ops):
@@ -111,18 +118,28 @@ def _graph(ops, soft, mid):
             last[o[0]] = n
         if o[0] is None and o[1] is not None:
             dep[n][[m for m in range(n) if ops[m][4] == o[1]][0]] = True
+    full = [{m: (ops[m][7] + CFG["wake"] if hard else 0.0) for m, hard in d.items()} for d in dep]
+    anc = []
+    for n, d in enumerate(full):
+        keep, mask = {}, 0
+        for m in sorted(d, reverse=True):
+            if not any(anc[k] >> m & 1 and k not in spare and ops[k][6] + d[k] >= d[m] for k in keep):
+                keep[m] = d[m]
+            mask |= anc[m] | 1 << m
+        full[n] = keep
+        anc.append(mask)
     lev = [0.0] * len(ops)
     hint = dict(soft)
     for n in range(len(ops) - 1, -1, -1):
         lev[n] += ops[n][6] + ops[n][7] + 1.0
-        for m, hard in dep[n].items():
-            lev[m] = max(lev[m], lev[n] + (CFG["wake"] if hard else -ops[m][7]))
+        for m, x in full[n].items():
+            lev[m] = max(lev[m], lev[n] + x - ops[m][7])
         if n in hint:
             lev[hint[n]] = max(lev[hint[n]], lev[n])
-    return [{m: (ops[m][7] + CFG["wake"] if hard else 0.0) for m, hard in d.items()} for d in dep], lev
+    return full, lev
 
 
-def _plan(ops, dep, lev):
+def _plan(ops, dep, lev, alts):
     back = [{} for _o in ops]
     for n, d in enumerate(dep):
         for m, x in d.items():
@@ -140,7 +157,93 @@ def _plan(ops, dep, lev):
             seed = (seed * 1103515245 + 12345) % 2147483648
             rank.append(x + CFG["jit"] * seed / 2147483648)
         lev = _order(ops, back, rank, [0.0 if back[n] else o[7] for n, o in enumerate(ops)])[1]
-    return best
+    return _polish(ops, dep, back, best, alts)
+
+
+def _times(ops, dep, out, start=0, end=None, why=None):
+    end, why = list(end or [0.0] * len(ops)), list(why or [-1] * len(ops))
+    last = {ops[n][0]: n for n in out[:start]}
+    free = {q: end[n] for q, n in last.items()}
+    for n in out[start:]:
+        q, c = ops[n][0], ops[n][6]
+        t, w = (free.get(q, 0.0), last.get(q, -1)) if q else (0.0, -1)
+        for m, x in dep[n]:
+            if end[m] + x > t:
+                t, w = end[m] + x, m
+        end[n] = free[q] = t + c if c >= 0 else t - ops[n][7] - CFG["wake"]
+        last[q], why[n] = n, w
+    return end, why
+
+
+def _polish(ops, dep, back, best, alts):
+    out, side = best[1], [0] * len(alts)
+    pre, seed = [list(d.items()) for d in dep], [CFG["seed"]]
+    tails = [n for n in out if not back[n]]
+
+    def draw(k):
+        seed[0] = (seed[0] * 1103515245 + 12345) % 2147483648
+        return (seed[0] >> 8) % k
+
+    def worth(e):
+        return max(e[n] + ops[n][7] for n in tails) + CFG["mean"] * sum(e) / len(e)
+
+    def flip(c):
+        side[c] ^= 1
+        for n, o in alts[c][side[c]]:
+            ops[n] = o
+
+    end, why = _times(ops, pre, out)
+    cur = worth(end)
+    best = (cur, out, end, list(side))
+    for it in range(CFG["moves"]):
+        kind, c = draw(10), -1
+        if kind == 0 and alts:
+            c = draw(len(alts))
+            flip(c)
+            new, i = out, min(out.index(n) for n, o in alts[c][0])
+        else:
+            ahead, far = draw(2), draw(5)
+            if kind < 6:
+                n, pairs = max(tails, key=lambda z: end[z] + ops[z][7]), []
+                while why[n] >= 0:
+                    if why[n] not in dep[n]:
+                        pairs.append((why[n], n))
+                    n = why[n]
+                y, x = pairs[draw(len(pairs))]
+                i, j = out.index(y), out.index(x)
+            else:
+                i = j = draw(len(out))
+                x = y = out[i]
+                far += 1
+            q, k, step = ops[x][0], (i if ahead else j), (-1 if ahead else 1)
+            while far and 0 <= k + step < len(out):
+                k += step
+                if ops[out[k]][0] == q:
+                    far -= 1
+                    i, j = (k, j) if ahead else (i, k)
+            if i == j or q is None:
+                continue
+            rel = dep if ahead else back
+            move, need = {x if ahead else y}, set(rel[x if ahead else y])
+            for k in (range(j - 1, i - 1, -1) if ahead else range(i + 1, j + 1)):
+                if out[k] in need:
+                    move.add(out[k])
+                    need.update(rel[out[k]])
+            part = out[i:j + 1]
+            a, b = [k for k in part if k in move], [k for k in part if k not in move]
+            new = out[:i] + (a + b if ahead else b + a) + out[j + 1:]
+        e2, w2 = _times(ops, pre, new, i, end, why)
+        s2 = worth(e2)
+        if s2 <= cur + CFG["heat"] * (1.0 - it / CFG["moves"]) * draw(64) / 64.0:
+            cur, out, end, why = s2, new, e2, w2
+            if cur < best[0]:
+                best = (cur, out, end, list(side))
+        elif c >= 0:
+            flip(c)
+    for c in range(len(alts)):
+        if side[c] != best[3][c]:
+            flip(c)
+    return (max(best[2][n] + ops[n][7] for n in tails),) + best[1:]
 
 
 def _order(ops, dep, lev, ready):
@@ -202,6 +305,9 @@ def _emit(g, T, ops):
         s = sem or own[q]
         if s in REMS:
             fn(Q[q])
+        elif q == "t":
+            for i in fn(Q[q]):
+                i.then_inc(T.sem[s], 1)
         else:
             fn(Q[q]).then_inc(T.sem[s], inc)
         count[s] += inc
@@ -217,8 +323,9 @@ def rank_program(g, core, T, topo):
         return
     cores = list(T.cores)
     N = len(cores)
-    ops, soft, tail, mid = [], [], {}, set()
-    sq = "s" if CFG["sint"] else "v"
+    ops, soft, tail, mid, grp, alts, spare = [], [], {}, {}, {}, [], set()
+    SEL, FG, GB, fac = CFG["sel"], CFG["fg"], CFG["gb"], CFG["fac"]
+    WM = max(hi - lo for lo, hi in SEL)
 
     def A(name, lo=0, hi=None, st=1, p=None):
         hi = SCRATCH[name][1][1] if hi is None else hi
@@ -227,6 +334,12 @@ def rank_program(g, core, T, topo):
 
     def C(name, c):
         return A(name, c, c + 1)
+
+    def LA(t, j, lo, hi, st=1):
+        name = "LA%d" % t
+        if j is None:
+            return (T[name][:, :, lo:hi], [(name, LW * i + lo, LW * i + hi, 1) for i in range(N)])
+        return (T[name][:, j, lo:hi:st] if st > 1 else T[name][:, j, lo:hi], [(name, LW * j + lo, LW * j + hi, st)])
 
     def IN(win, off):
         return (win[0].indirect(off[0]), win[1] + off[1], win[1], off[1])
@@ -238,7 +351,7 @@ def rank_program(g, core, T, topo):
         name, lo, hi, st = x[1][-1]
         return (hi - lo + st - 1) // st * (16 if len(x) == 4 else 1)
 
-    def add(q, fn, out, ins, sem=None, inc=1, cost=None, lat=0.0, two=False):
+    def add(q, fn, out, ins, sem=None, inc=1, cost=None, lat=0.0, two=False, more=0.0):
         rd, wr = [], []
         full = [x for x in ins if isinstance(x, tuple)]
         for x in full:
@@ -248,18 +361,39 @@ def rank_program(g, core, T, topo):
             rd += x[3] if len(x) == 4 else []
         if cost is None:
             n = max(size(x) for x in full + out)
+            c0 = 50 if q == "v" else 65
             if len(out[0]) == 4:
-                cost = 50 + CFG["sig"] * 0.83 * size(out[0])
+                cost = (c0 + CFG["sig"] * 0.83 * size(out[0])) * CFG["gfac"] / fac
             elif full and len(full[0]) == 4:
-                cost = 50 + CFG["gam"] * 0.83 * size(full[0])
+                cost = (c0 + CFG["gam"] * 0.83 * size(full[0])) * CFG["gfac"] / fac
             else:
                 kinds = [SCRATCH[x[1][0][0]] for x in full + out if size(x) == n]
                 k = 0.5 if q == "v" and all(z[2] in (BF, F16, U16) for z in kinds) else 1.0
                 if two:
                     k = 1.0 if any(z[0] == "psum" for z in kinds) else 2.0
                 cost = 30 + 0.83 * max(64, k * n)
-            cost *= 1.25
+            cost = (cost + more) * fac
         ops.append((q, fn, rd, wr, sem, inc, cost, lat))
+
+    def after(*regs):
+        for x in regs:
+            ops[-1][2].extend(x[1])
+
+    def either(first, steps):
+        forms = ([], [])
+        for step in steps:
+            n, made = len(ops), []
+            for f in step:
+                if f:
+                    f()
+                made.append(ops.pop() if f else None)
+            whole = [o for o in made if o]
+            ops.append(whole[0][:2] + (sum((o[2] for o in whole), []),) + whole[0][3:])
+            for side in (0, 1):
+                forms[side].append((n, made[side] or (None, None, [], [], None, 0, -1.0, whole[0][7])))
+            if len(whole) < 2:
+                spare.add(n)
+        alts.append(forms if first else forms[::-1])
 
     def chain(key):
         if key in tail:
@@ -278,20 +412,20 @@ def rank_program(g, core, T, topo):
         else:
             add("v", lambda e: e.tensor_scalar(o[0], a[0], ap(s1), ap(s2), op0, op1), [o], [a, s1, s2])
 
-    def scan(o, a, b, op0, op1):
-        add("v", lambda e: e.tensor_tensor_scan(o[0], a[0], b[0], 0.0, op0, op1), [o], [a, b])
+    def scan(o, a, b, op0, op1, init=0.0):
+        add("v", lambda e: e.tensor_tensor_scan(o[0], a[0], b[0], ap(init), op0, op1), [o], [a, b, init])
+
+    def tr(o, i):
+        add("v", lambda e: e.transpose(o[0], i[0]), [o], [i])
 
     def ms(o, c):
         add("v", lambda e: e.memset(o[0], c), [o], [])
 
-    def act(o, i, f=AF.Identity, bias=0.0, scale=1.0, acc=None):
+    def act(o, i, f=AF.Identity, bias=0.0, scale=1.0, acc=None, more=0.0):
         if acc is None:
-            add("s", lambda e: e.activation(o[0], i[0], f, bias=ap(bias), scale=ap(scale)), [o], [i, bias, scale])
+            add("s", lambda e: e.activation(o[0], i[0], f, bias=ap(bias), scale=ap(scale)), [o], [i, bias, scale], more=more)
         else:
-            add("s", lambda e: e.activation(o[0], i[0], f, bias=ap(bias), scale=scale, accum_out=acc[0]), [o, acc], [i, bias])
-
-    def fill(o, c):
-        act(o, A("SEED", 0, size(o)), bias=c, scale=0.0)
+            add("s", lambda e: e.activation(o[0], i[0], f, bias=ap(bias), scale=scale, accum_out=acc[0]), [o, acc], [i, bias], more=20.0)
 
     def lin(q, o, i, bias=0.0):
         if q == "s":
@@ -301,34 +435,53 @@ def rank_program(g, core, T, topo):
         else:
             cp(o, i)
 
-    def mm(o, l, x, a, b):
-        c = 1.25 * CFG["pe"] * max(64, size(x)) * (4 if SCRATCH[x[1][0][0]][2] == F32 else 1)
-        add("t", lambda e: e.matmul(o[0], l[0], x[0], a, b), [o], [l, x], cost=c, lat=100.0)
+    def mms(o, terms, a, b):
+        c = sum(fac * CFG["pe"] * max(64, size(x)) * (4 if SCRATCH[x[1][0][0]][2] == F32 else 1) for l, x in terms)
+        z = len(terms) - 1
+        add("t", lambda e: [e.matmul(o[0], l[0], x[0], a and n == 0, b and n == z) for n, (l, x) in enumerate(terms)],
+            [o], [y for lx in terms for y in lx], inc=z + 1, cost=c, lat=100.0)
+        bank = o[1][0][0]
+        if a:
+            grp[bank] = len(ops)
         if not a and not b:
-            mid.add(len(ops) - 1)
+            mid[len(ops) - 1] = grp[bank]
 
-    def iota(o, pat, base, ch, fl=True):
-        c = 1.25 * (130 + 1.66 * size(o))
-        if fl:
+    def mm(o, l, x, a, b):
+        mms(o, [(l, x)], a, b)
+
+    def lc(o, *terms):
+        for n, (l, x) in enumerate(terms):
+            mm(o, l, x, n == 0, n == len(terms) - 1)
+
+    def iota(o, pat, base, ch=0):
+        c = fac * (130 + 1.66 * size(o))
+        if SCRATCH[o[1][0][0]][2] != I32:
             add("g", lambda e: e.iota(o[0], pat, base, ch, allow_small_or_imprecise_dtypes=True), [o], [], cost=c)
         else:
             add("g", lambda e: e.iota(o[0], pat, base, ch), [o], [], cost=c)
 
+    def const(o, c):
+        iota(o, [[0, size(o)]], int(c))
+
+    def ends(name, a, first):
+        for c in range(first, 16 // NS):
+            iota(A(name, 256 * NS * c, 256 * NS * (c + 1)), [[8, 16], [128, NS], [0, 16]], 128 * NS * c + 4 * a + r)
+
     def dma(q, o, i, out, ins, sem, lat):
         add(q, lambda e: e.dma_start(o, i), out, ins, sem, 16, cost=60.0, lat=lat)
 
-    def send_table(t, after):
+    def send_table(t, wait):
         d = cores[(r - 1 - t) % N]
         rid, pid = topo.addr(d, core)
-        src = A("M", 0, QW)
+        src = A("M", 0, 2048)
         add("g", lambda e: e.remote_dma(T["Q%d" % t][:, :], src[0], T.sem["q%d" % t], T.sem["tq%d" % t], pid, rid, topo.mask(core, d)),
-            [], [src] + after, "tq%d" % t, len(topo.engines(core, d)), cost=500.0, lat=10000.0)
+            [], [src] + wait, "tq%d" % t, len(topo.engines(core, d)), cost=500.0, lat=10000.0)
         add(None, "tq%d" % t, [A("Q%d" % t)], [], "q%d" % t, len(topo.engines(cores[(r + 1 + t) % N], core)), cost=0.0)
 
     def send_lists(t):
         peers = [c for c in cores if c != core]
         mk = _masks(topo, core, peers)
-        src = A("LA%d" % t, 128 * r, 128 * r + 128)
+        src = LA(t, r, 0, LW)
         trs = []
         for d in peers:
             rid, pid = topo.addr(d, core)
@@ -337,10 +490,15 @@ def rank_program(g, core, T, topo):
         add("g", lambda e: e.remote_dma_fused(trs, local_sem=T.sem["ta%d" % t]), [], [src], "ta%d" % t,
             sum(len(mk[d]) for d in peers), cost=500.0, lat=CFG["hop"] - 500.0)
         n = sum(len(_masks(topo, s, [c for c in cores if c != s])[core]) for s in peers)
-        add(None, "ta%d" % t, [A("LA%d" % t, 128 * j, 128 * j + 128) for j in range(N) if j != r], [], "a%d" % t, n, cost=0.0)
+        add(None, "ta%d" % t, [LA(t, j, 0, LW) for j in range(N) if j != r], [], "a%d" % t, n, cost=0.0)
 
-    def own(name, a):
-        return A(name, 4 * a + r, 2048, 8)
+    def own(name, a, lo=0, hi=256, j=r):
+        return (A(name, 4 * a + j + 8 * lo, 8 * hi, 8)[0], [(name, 4 * a + i + 8 * lo, 8 * hi, 8) for i in range(N)])
+
+    mp = A("mp", 16, 272)
+
+    def key(n, lo, hi):
+        return A(("KA", "KB")[n % 2], lo % 256, (hi - 1) % 256 + 1)
 
     ms(A("thi"), 0)
     dma("y", T.M[:, 0:1024], T.mt[:, 0:1024], [A("M", 0, 1024)], [], "lm0", 4000.0)
@@ -349,281 +507,315 @@ def rank_program(g, core, T, topo):
     dma("y", T.thi[0:128:16, 0:1], T.th[:], [A("thi")], [], "lth", 2500.0)
     dma("y", T.X0[:, 0:2048], T.xv[:, :], [A("X0", 0, 2048)], [C("Ai", 7)], "lx0", 3500.0)
 
-    iota(A("SEED"), [[128, 16], [0, 16]], 0, 0)
-    iota(A("J", 0, 16), [[8, 16]], r, 128, False)
-    iota(C("Pi", 0), [[0, 1]], 0, 1, False)
-    iota(A("IO", 0, 256), [[1, 256]], 0, 0)
-    iota(A("J", 16, 32), [[1, 16]], 0, 16, False)
-    iota(A("I16"), [[0, 16], [1, 16]], 0, 0)
-    iota(A("J", 32, 48), [[16, 16]], 0, 1, False)
-    iota(A("M", 2048, TW), [[0, TW - 2048]], -1, 0, False)
+    iota(A("SEED"), [[8, 16 // NS], [128, NS], [0, 16]], r)
+    iota(C("Pi", 0), [[0, 1]], 0, 1)
+    iota(A("Jf", 0, 16), [[128 * NS, 16 // NS], [128 // NS, NS]], r)
+    iota(A("IO", 0, 256), [[1, 256]], 1)
+    iota(A("G16"), [[1, 8], [0, 16]], 0)
+    iota(A("TB", 0, 16 * NS), [[0, NS], [-int(KU), 16]], int(16 * KU))
+    iota(A("J", 0, 16), [[16, 16]], 0, 1)
+    iota(A("I16"), [[0, 4], [1, 16]], 0)
+    iota(A("Jf", 16, 32), [[16 * NS, 16 // NS], [1, NS]], 0)
+    const(A("mp", 0, 16), 0)
+    const(A("mp", 272, 288), 0)
     send_table(0, [])
-    for o, c in ((A("mp", 0, 16), 0), (A("mp", 272, 288), 0), (A("X1", 2048, TW), 32768), (A("PI", 0, 256), -1)):
-        iota(o, [[0, size(o)]], c, 0)
-    iota(A("VL0"), [[8, 256]], r, 0)
-    iota(A("IO", 256, TW), [[1, TW - 256]], 256, 0)
-    iota(A("yy", 256, 320), [[0, 64]], 1, 0)
-    iota(A("B4"), [[4096, 64]], 0, 0)
-    iota(A("SG2"), [[0, 640]], 1, 0)
-    iota(A("SG2", 320, 321), [[0, 1]], 0, 0)
-    iota(A("X0", 2048, TW), [[0, TW - 2048]], 32768, 0)
-    iota(A("VL1"), [[8, 256]], r + 4, 0)
-    iota(A("BG"), [[0, 64]], int(BIG), 0)
-    ts(A("VR0", 0, 256), A("SEED"), float(r), OP.add)
+    ends("VR0", 0, 8 // NS)
+    iota(A("VL0", 0, 256), [[8, 256]], r)
+    iota(A("IO", 256, 2048), [[1, 1792]], 257)
+    iota(A("B4"), [[int(KU), 64]], 0)
+    const(A("VL0", 256, 272), 5000)
+    iota(A("IO", 2048, TW + 64), [[1, TW - 1984]], 2049)
+    const(A("PI", 0, 256), FO - 1)
+    const(A("RB"), 0)
+    const(A("C15"), 1536)
+    cp(A("VRH", 0, 256), A("SEED"))
     for n in (256, 512, 1024):
-        ts(A("VR0", n, 2 * n), A("VR0", 0, n), n / 32.0, OP.add)
-    for p in range(8, 16):
-        act(A("VR0", 256 * p, 256 * p + 256), A("SEED"), bias=float(8 * p + r))
-    ts(A("J", 48, 64), A("J", 0, 16), 2047, OP.bitwise_and)
-    cp(A("L0"), A("J", 48, 64))
-    ts(A("L1"), A("J", 48, 64), 4.0, OP.add)
-    ts(A("J", 64, 80), A("J", 16, 32), 255, OP.bitwise_and)
-    cp(A("PERM"), A("J", 64, 80))
+        ts(A("VRH", n, 2 * n), A("VRH", 0, n), n / 2.0 / (NS if n < 256 * NS else 1), OP.add)
     ts(C("Pi", 1), C("Pi", 0), 15, OP.bitwise_and)
     ts(C("Pi", 2), C("Pi", 0), 4, OP.logical_shift_right)
-    ts(C("Pi", 3), C("Pi", 0), 31, OP.bitwise_and)
-    cp(A("Pf", 0, 4), A("Pi", 0, 4))
-    act(C("Pf", 6), C("Pf", 2), bias=15.0, scale=16.0)
-    act(C("Pf", 7), C("Pf", 2), scale=128.0)
-    act(C("Pf", 8), C("Pf", 2), scale=-16.0)
-    act(C("Pf", 9), C("Pf", 3), scale=128.0)
-    act(C("Pf", 10), C("Pf", 3), scale=128.0, bias=-2048.0)
-    ts(A("ID"), A("IO", 0, 128), C("Pf", 0), OP.is_equal)
-    ts(A("WE"), A("IO", 0, 144), C("Pf", 6), OP.is_equal, 65536.0, OP.mult)
-    ts(A("BO"), A("SEED", 0, 128), C("Pf", 7), OP.is_equal)
-    ts(A("BC", 0, 256), A("SEED"), C("Pf", 9), OP.is_equal)
-    ts(A("BC", 256, 512), A("SEED"), C("Pf", 10), OP.is_equal)
+    ts(C("Pi", 3), C("Pi", 0), NS - 1, OP.bitwise_and)
+    ts(C("Pi", 4), C("Pi", 0), 15, OP.bitwise_and, NS.bit_length() - 1, OP.logical_shift_right)
+    cp(A("Pf", 0, 5), A("Pi", 0, 5))
+    ms(A("ONE"), 1.0)
+    ms(C("ONE", 256), 0.0)
+    act(A("AB", 64, 260, 65), A("IO", 0, 4), bias=1e29, scale=0.0)
+    act(C("Pf", 5), C("Pf", 0), bias=1.0)
+    act(C("Pf", 6), C("Pf", 2), bias=16.0, scale=16.0)
+    act(C("Pf", 8), C("Pf", 4), scale=8.0)
+    act(C("Pf", 7), C("Pf", 3), bias=C("Pf", 8), scale=128.0)
+    act(C("Pf", 9), C("Pf", 1), scale=float(NS))
+    act(C("Pf", 10), C("Pf", 0), bias=float(r), scale=8.0)
+    act(C("Pf", 11), C("Pf", 1), bias=C("Pf", 5), scale=128.0)
+    act(C("Pf", 12), C("Pf", 2), scale=-16.0)
+    ts(A("L0"), A("Jf", 0, 16), C("Pf", 7), OP.add)
+    ts(A("L1"), A("Jf", 0, 16), C("Pf", 7), OP.add, 4.0, OP.add)
+    ts(A("PERM"), A("Jf", 16, 32), C("Pf", 9), OP.add)
+    ts(A("ID"), A("IO", 0, 128), C("Pf", 5), OP.is_equal)
+    ts(A("WE"), A("IO", 0, 144), C("Pf", 6), OP.is_equal, 65536.0 * KU, OP.mult)
+    ts(A("BO"), A("G16"), C("Pf", 2), OP.is_equal)
+    for n in range(0, 2048, 1024):
+        ts(A("BC", n, n + 1024), A("VRH", n, n + 1024), C("Pf", 10), OP.is_equal)
     for nm, wt in (("WG", 16.0), ("WM", -32.0), ("WA", -16.0)):
         act(A(nm), A("WE"), scale=wt / 65536.0)
-    for nm, wt in (("BO16", 0.0625), ("BOC", 8192.0), ("BON", -1.0 / 8192)):
-        act(A(nm), A("BO"), scale=wt)
-    for nm, wt in (("NID", -1.0), ("IDH", 1.0), ("NIH", -1.0), ("NIF", -1.0)):
+    act(A("BON"), A("BO"), scale=-1.0 / 8192)
+    for nm, wt in (("NID", -1.0), ("IDF", 1.0), ("NIH", -1.0), ("IDH", 1.0), ("IDB", BIG), ("IDN", -64.0)):
         act(A(nm), A("ID"), scale=wt)
-    ms(A("ONE"), 1.0)
-    act(A("TB"), A("I16", 0, 128), bias=16.0, scale=-1.0)
-    act(A("SEG"), A("I16"), AF.Sign)
-    ts(A("DIAG"), A("I16", 0, 64), C("Pf", 1), OP.is_equal)
-    ts(A("ENDS"), A("IO", 0, 16), 16.0, OP.mult, 15.0, OP.add)
-    ts(A("J", 80, 96), A("J", 32, 48), 4, OP.logical_shift_right, 1, OP.bitwise_and)
-    ts(A("Jf", 0, 16), A("J", 32, 48), C("Pf", 8), OP.add)
-    ts(A("Jf", 16, 32), A("J", 80, 96), 272.0, OP.mult)
-    tt(A("Jf", 32, 48), A("Jf", 0, 16), A("Jf", 16, 32), OP.add)
-    cp(A("OW"), A("Jf", 32, 48))
+    ms(A("RS", 0, WM), 0.0)
+    ms(A("RS", 0, WM, 16), -1e29)
+    ts(A("DIAG"), A("I16"), C("Pf", 1), OP.is_equal)
+    ts(A("J", 16, 32), A("J", 0, 16), 4, OP.logical_shift_right, 1, OP.bitwise_and)
+    ts(A("Jf", 32, 48), A("J", 0, 16), C("Pf", 12), OP.add)
+    ts(A("Jf", 48, 64), A("J", 16, 32), 272.0, OP.mult)
+    tt(A("Jf", 64, 80), A("Jf", 32, 48), A("Jf", 48, 64), OP.add)
+    cp(A("OW"), A("Jf", 64, 80))
     act(A("TC", 0, 4), A("IO", 0, 4), bias=C("Pf", 1), scale=16.0)
-    act(A("TC", 4, 8), A("TC", 0, 4), bias=0.5)
-    act(A("TC", 8, 12), A("TC", 0, 4), scale=4096.0)
-    act(A("TC", 12, 16), A("TC", 0, 4), AF.Silu, bias=float(QW))
-    ts(A("M16"), A("IO", 0, 16), C("Pf", 1), OP.is_equal)
-    for o, c in ((A("O16"), 0.0625), (A("cH", 256, 320), 4000.0 * HS)):
-        fill(o, c)
-    for t in range(3):
-        ms(A("LA%d" % t, 128 * r, 128 * r + 128, 2), 0)
-    for k in range(16):
-        act(A("SK", 128 * k, 128 * k + 128), A("ID"), scale=C("M16", k))
-    for n in range(1, TW // 256):
-        dma("y", T.PI[:, 256 * n:256 * n + 256], T.PI[:, 0:256], [A("PI", 256 * n, 256 * n + 256)], [A("PI", 0, 256)], "lp", 2500.0)
-    iota(A("F"), [[1, TW]], int(FO), 0)
+    act(A("TC", 4, 8), A("TC", 0, 4), bias=-32.0, scale=2.0)
+    act(A("TC", 8, 12), A("TC", 0, 4), bias=-31.0, scale=2.0)
+    act(A("TC", 12, 16), A("TC", 0, 4), bias=float(SP + 64 * r - 16))
+    for n, c in ((13, 0), (14, r), (15, r + 4)):
+        act(C("Pf", n), C("Pf", 1), bias=float(c), scale=KU)
+    act(A("RB", 64, 260, 65), A("IO", 0, 4), bias=16.0 * KU, scale=-16.0 * KU)
+    act(A("RB", 0, 260, 65), A("IO", 0, 4), bias=1e29, scale=0.0)
+    act(C("CNT", 1), C("ONE", 0), scale=-1.5 * BIG / 8)
+    act(A("O16"), A("G16"), bias=0.0625 / BIG, scale=0.0)
+    act(A("cH", 256, 272), A("G16", 0, 16), bias=4000.0 * HS, scale=0.0)
     cp(C("thb", 0), C("thi", 0))
 
-    def choose(a, blocks, oc):
-        for h in range(2):
-            mm(A("MI", 128 * h, 128 * h + 128), A("XT", 128 * h, 128 * h + 128), A("ID"), True, a is None)
-            if a is not None:
-                mm(A("MI", 128 * h, 128 * h + 128), A("DB", 128 * h, 128 * h + 128), A("ID"), False, True)
-        act(A("XTT"), A("MI", 0, 256))
-        a = a or 0
-        for kb in ("KA", "KB"):
-            mm(A(kb, 0, 128), A("BO16"), A("TB"), True, False)
+    def choose(t, blocks, oc):
+        a = t % 2
         for n in range(8):
             lo, hi = 512 * n, 512 * n + 512
-            tt(A("E", lo, hi), IN(A("M", 0, 2048), A(oc, 32 * n, 32 * n + 32)), A("VR%d" % a, lo, hi), OP.is_equal)
-            chain("v")
-            act(A("GX", lo, hi), IN(A("X%d" % (1 - a), 0, 2048), A(oc, 32 * n, 32 * n + 32)))
-            chain("s")
-            bank, ps = A(("XL", "MI")[n % 2]), (32 * (n % 4), 32 * (n % 4) + 32)
-            mm(bank, A("XTT", 128 * (n // 4), 128 * (n // 4) + 128, p=ps), A("BC", p=ps), True, n not in blocks)
-            if n in blocks:
-                mm(bank, A("NID"), A("GX", lo, hi), False, True)
-                act(A("MX", lo, hi), bank, AF.Abs)
-                use = (("E", "WE"), ("MX", "WA"))
-            else:
-                tt(A("MX", lo, hi), A("GX", lo, hi), bank, OP.max)
-                use = (("E", "WE"), ("GX", "WG"), ("MX", "WM"))
-            for src, wn in use:
-                for p in (2 * n, 2 * n + 1):
-                    for b, kb in enumerate(("KA", "KB")):
-                        c = 256 * p + 128 * b
-                        mm(A(kb, 0, 128), A(wn, 15 - p, 143 - p), A(src, c, c + 128), False, False)
-        for kb in ("KA", "KB"):
-            mm(A(kb, 0, 128), A("BOC"), A("ONE", 0, 128), False, True)
+            if 32 * n % GB == 0:
+                o = A(oc, 32 * n, 32 * n + GB)
+                tt(A("E", lo, lo + 16 * GB), IN(A("M", 0, 2048), o), A("VR%d" % a if a or lo >= 2048 else "VRH", lo, lo + 16 * GB), OP.is_equal)
+                chain("v")
+                act(A("GX", lo, lo + 16 * GB), IN(A("X%d" % (1 - a), 0, 2048), o))
+                chain("s")
+            c0 = 32 * n // (16 * NS) * 16 * NS
+            sel = [i for i, (x, y) in enumerate(SEL) if x <= c0 < y][0]
+            kb = key(sel, c0, c0 + 16 * NS)
+            if 32 * n == c0:
+                mm(kb, A("ID"), A("TB", 0, 16 * NS), True, False)
+            bank = A(("XA", "XB")[n % 2])
+            def keys(src, wn):
+                mms(kb, [(A(wn, 15 - (x - c0) // NS, 143 - (x - c0) // NS), A(src, 16 * x, 16 * x + 16 * NS))
+                         for x in range(32 * n, 32 * n + 32, NS)], False, src == "MX" and 32 * n + 32 == c0 + 16 * NS)
 
-    def follow(src, dst, col):
-        for (q, lo, hi), bank in zip(CFG["units"], ("EA", "EB", "EC", "VO")):
-            lin(q, A("GF", 16 * lo, 16 * hi), IN(A("F", 0, 2048), A(src, lo, hi)), -FO)
-            chain(q)
-            o = A(bank, col, col + hi - lo)
-            for k in range(16):
-                mm(o, A("SK", 128 * k, 128 * k + 128), A("GF", 16 * lo + k, 16 * hi, 16), k == 0, k == 15)
+            def spread(stop):
+                mm(bank, A("XTT", 128 * (n // 4), 128 * (n // 4) + 128), A("BC", lo % 2048, lo % 2048 + 512), True, stop)
+
+            keys("E", "WE")
+            either(n in blocks, (
+                (lambda: spread(False), lambda: spread(True)),
+                (lambda: mm(bank, A("NID"), A("GX", lo, hi), False, True), None),
+                (lambda: act(A("MX", lo, hi), bank, AF.Abs), lambda: tt(A("MX", lo, hi), A("GX", lo, hi), bank, OP.max)),
+                (None, lambda: keys("GX", "WG")),
+                (lambda: keys("MX", "WA"), lambda: keys("MX", "WM"))))
+            if 32 * n + 32 == SEL[sel][1]:
+                vote(t, sel)
+
+    def turn(a):
+        for h in range(2):
+            mm(A("XB", 128 * h, 128 * h + 128), A("XN%d" % a, 128 * h, 128 * h + 128), A("ID"), True, True)
+        act(A("XTT"), A("XB", 0, 256))
+
+    def vote(t, n):
+        a, (lo, hi) = t % 2, SEL[n]
+        w, kb = hi - lo, key(n, lo, hi)
+        if n == 0:
+            tr(A("mW", 0, 256), A("mp", 16, 272))
+            tr(A("mW", 256, 544), A("mp"))
+        scan(A("pm", lo, hi), A("RS", 0, w), kb, OP.add, OP.max)
+        tt(A("df", lo, hi), A("pm", lo, hi), kb, OP.subtract)
+        tt(A("dn", lo, hi), IN(A("mW"), A("OW", lo // 16, hi // 16)), A("df", lo, hi), OP.subtract)
+        scan(A("sc", lo, hi), A("df", lo, hi), A("dn", lo, hi), OP.min, OP.max)
+        c = A("cO", lo // 16, hi // 16)
+        cp(c, A("sc", lo + 15, hi, 16))
+        act(A("XC", lo, hi), IN(A("X%d" % (1 - a), 0, 2048), c))
+        tt(A("E2", lo, hi), IN(A("Q%d" % t), c), A("VL%d" % a, lo, hi), OP.is_equal)
+        tt(A("E1", lo, hi), IN(A("M", 0, 2048), c), A("VL%d" % a, lo, hi), OP.is_equal)
+        act(A("cH", lo, hi), IN(A("IO", 0, 2048), c), scale=HS, bias=-HS)
+        vo = A("VO", lo, hi)
+        lc(vo, *([(A("IDN"), A("dead", lo, hi))] * (t > 0) +
+                 [(A("BON"), A("XC", lo, hi)), (A("BO"), A("E2", lo, hi)), (A("BO"), A("E1", lo, hi))]))
+        act(A("yy", lo, hi), vo, AF.Sign, bias=C("THR", t))
+        scan(A("cum", lo, hi), A("yy", lo, hi), A("ONE", 0, w), OP.add, OP.add, C("cum", lo - 1) if lo else 0.0)
+
+    def follow(units, src, dst, col):
+        for q, lo, hi in units:
+            o, i = A("GF", 16 * lo, 16 * hi), IN(A("F", 0, 2048), A(src, lo, hi))
+            either(q == "s", ((lambda: lin("s", o, i, -FO), lambda: lin("v", o, i, -FO)),))
+            chain(q + dst)
+        for n, (lo, hi) in enumerate(FG):
+            o = A("FB" if col else "FA", lo, hi)
+            mms(o, [(A("SK", 128 * k, 128 * k + 128), A("GF", 16 * lo + k, 16 * hi, 16)) for k in range(16)], True, True)
             cp(A(dst, lo, hi), o)
             if col:
                 act(A("m2", lo, hi), o, bias=RND)
 
     def marks(t):
         a, z = t % 2, (256 * t, 256 * t + 256)
-        mm(A("EB", 0, 256), A("IDH"), A("cR", *z), True, True)
-        mm(A("EC", 0, 256), A("IDH"), A("sh", *z), True, False)
-        mm(A("EC", 0, 256), A("NIH"), A("xh", *z), False, True)
-        tt(A("w2"), A("won", *z), A("EB", 0, 256), OP.mult)
-        ts(IN(A("PI"), A("v1", 16 * t, 16 * t + 16)), A("w2"), 1.0, OP.mult, -1.0, OP.add)
+        cw = IN(A("IO", 0, TW), A("c1", 16 * t, 16 * t + 16))
+        if t == 2:
+            act(A("cR"), cw)
+            mm(A("FB", 0, 256), A("IDF"), A("cR"), True, True)
+            tt(A("w2"), A("won", *z), A("FB", 0, 256), OP.mult)
+        else:
+            tt(A("w2"), cw, A("won", *z), OP.mult)
+            after(LA(t + 1, r, 64, LW))
+        ts(IN(A("PI"), A("v1", 16 * t, 16 * t + 16)), A("w2"), 1.0, OP.mult, FO * (t == 0) - 1.0, OP.add)
         if t == 2:
             dma("y", T.yp[:, :], T.PI[0:128:16, 0:2048], [], [A("PI")], "sp", 2200.0)
         else:
-            act(A("al"), own("PI", a), AF.Relu, scale=-1.0)
-        tt(A("pr"), A("al"), A("EC", 0, 256), OP.mult)
-        mm(A("EB", 256, 512), A("ID"), A("XN%d" % a), True, False)
-        mm(A("EB", 256, 512), A("ID"), A("pr"), False, True)
-        act(A("XN0") if t == 0 else A("YX", a, 512, 2), A("EB", 256, 512))
+            act(A("al"), own("PI", a), AF.Relu, scale=-1.0, bias=FO * (t == 0))
+        lc(A("KA", 0, 256), (A("ID"), A("XN%d" % a)), (A("ID"), A("C15")), (A("NIH"), A("sh", *z)))
+        tt(A("pr"), A("al"), A("KA", 0, 256), OP.mult)
+        lc(A("KB", 0, 256), (A("ID"), A("XN%d" % a)), (A("NID"), A("pr")))
+        act(A("XN0") if t == 0 else A("YX", a, 512, 2), A("KB", 0, 256))
 
     for t in range(3):
         a = t % 2
         off = 4 * a + r
         z = (256 * t, 256 * t + 256)
         if t == 0:
-            cp(A("o0"), IN(A("M", 0, 2048), A("L0")))
+            for lo, hi in ((0, 64), (64, 256)):
+                cp(A("o0", lo, hi), IN(A("M", 0, 2048), A("L0", lo // 16, hi // 16)))
             act(A("XN0"), own("X1", 0))
-            act(A("XT"), IN(A("XN0"), A("PERM")))
             for j in range(4):
-                ms(A("X1", j, 2048, 8), BIG)
+                if CFG["mk"][j] == "v":
+                    ms(A("X1", j, 2048, 8), BIG)
+                else:
+                    act(A("X1", j, 2048, 8), A("SEED"), bias=BIG, scale=0.0)
             act(A("XN1"), own("X1", 1))
-            lin(sq, A("mp", 16, 272), own("M", 0), -2048.0)
+            act(mp, own("M", 0))
             for b in range(2):
-                lin(sq, A("OM", 256 * b, 256 * b + 256), own("M", b), -2048.0)
-            mm(A("VO", 0, 1), A("BO"), C("thb", 0), True, True)
-            act(C("THR", 0), A("VO", 0, 1), bias=-0.5)
-            choose(None, CFG["abs0"], "o0")
+                act(A("OM", 256 * b, 256 * b + 256), own("M", b))
+            mm(A("VO", 256, 257), A("BO"), C("thb", 0), True, True)
+            act(C("THR", 0), A("VO", 256, 257), bias=0.5, scale=-1.0)
+            act(C("THR", 6), C("THR", 0), bias=-1.5)
+            turn(0)
+            choose(0, CFG["abs0"], "o0")
         else:
-            act(A("DB"), IN(A("PI", 0, 2048), A("L%d" % a)), AF.Relu, bias=32768.0, scale=32768.0)
-            act(A("am"), own("PI", a), AF.Relu, scale=-1.0)
-            mm(A("XL", 0, 1), A("O16"), C("CNT", 0), True, True)
-            cp(C("Ai", 0), A("XL", 0, 1))
-            ts(C("Ai", 1), C("Ai", 0), 3, OP.bitwise_and)
-            ts(C("THR", t), C("Ai", 1), C("THR", 0), OP.add)
-            follow("o%d" % a, "o2", 0)
-            follow("o2", "oc", 256)
-            act(A("mp", 16, 272), IN(A("m2"), A("PERM")), bias=-2048.0 - RND)
-            choose(a, CFG["abs"], "oc")
-        add("v", lambda e: e.transpose(T.mW[:, 0:256], T.mp[:, 16:272]), [A("mW", 0, 256)], [A("mp", 16, 272)])
-        add("v", lambda e: e.transpose(T.mW[:, 256:544], T.mp[:, 0:288]), [A("mW", 256, 544)], [A("mp")])
+            act(A("dead"), own("PI", a), AF.Sign, bias=1.0 - FO)
+            if t == 2:
+                for n in range(0, TW, 580):
+                    act(A("PI", n, n + 580), A("PI", n, n + 580), bias=-FO)
+            lc(A("VO", 256, 257), (A("O16"), C("CNT", 1)), (A("O16"), C("CNT", 0)))
+            act(C("THR", 3), A("VO", 256, 257), bias=C("THR", 6), scale=-1.0)
+            act(C("THR", 4), A("VO", 256, 257), bias=RND, scale=0.25)
+            act(C("THR", 5), C("THR", 4), bias=-RND)
+            act(C("THR", t), C("THR", 5), bias=C("THR", 3), scale=4.0)
+            follow(CFG["f1"], "o%d" % a, "o2", 0)
+            follow(CFG["f2"], "o2", "oc", 256)
+            act(mp, IN(A("m2"), A("PERM")), bias=-RND)
+            choose(t, CFG["abs"], "oc")
 
-        scan(A("pm", 0, 128), A("SEG", 0, 128), A("KA", 0, 128), OP.mult, OP.max)
-        act(A("ks", 128, 256), A("KB", 0, 128))
-        scan(A("pm", 128, 256), A("SEG", 0, 128), A("KB", 0, 128), OP.mult, OP.max)
-        act(A("ks", 0, 128), A("KA", 0, 128))
-        tt(A("oh"), IN(A("pm"), A("ENDS")), A("ks"), OP.is_equal)
-        tt(A("val"), IN(A("mW"), A("OW")), A("oh"), OP.mult)
-        scan(A("sc"), A("SEG"), A("val"), OP.mult, OP.add)
-        ts(A("cO"), A("sc", 15, 256, 16), 2048.0, OP.add)
-        act(A("XC"), IN(A("X%d" % (1 - a), 0, 2064), A("cO")))
-        tt(A("E1"), IN(A("M", 0, QW), A("cO")), A("VL%d" % a), OP.is_equal)
-        tt(A("E2"), IN(A("Q%d" % t), A("cO")), A("VL%d" % a), OP.is_equal)
-        act(A("cH", 0, 256), IN(A("IO", 0, QW), A("cO")), scale=HS)
-        mm(A("VO", 0, 256), A("BO"), A("E1"), True, False)
-        mm(A("VO", 0, 256), A("BON"), A("XC"), False, False)
-        mm(A("VO", 0, 256), A("BO"), A("E2"), False, True)
-        ts(A("yy", 0, 256), A("VO", 0, 256), C("THR", t), OP.is_ge)
-        scan(A("cum"), A("ONE"), A("yy"), OP.mult, OP.add)
         for s in (2, 3):
-            act(A("junk", 320 * s - 640, 320 * s - 320), A("cum"), AF.Sign, bias=C("TC", 4 + s), scale=-1.0, acc=C("acc", s))
+            act(A("junk", 256 * s - 512, 256 * s - 256), A("cum"), AF.Sign, bias=C("TC", 8 + s), scale=-1.0, acc=C("acc", s))
         for s in (0, 1):
-            ts(A("le", 320 * s, 320 * s + 320), A("cum"), C("TC", s), OP.is_le)
-        scan(A("les"), A("SG2"), A("le"), OP.mult, OP.add)
-        cp(A("idx", 0, 2), A("les", 319, 640, 320))
-        ts(A("idx", 2, 4), A("acc", 2, 4), 0.5, OP.mult, 160.0, OP.add)
-        la, b0 = "LA%d" % t, 128 * r
-        ts(A(la, b0 + 1, b0 + 128, 2), IN(A("IO", 0, 320), A("idx", 0, 4)), 8.0, OP.mult, float(off), OP.add)
-        tt(A("Mk"), IN(A("cH"), A("idx", 0, 4)), A("DIAG"), OP.mult)
-        tt(A("K"), IN(A("cH"), A("idx", 0, 4)), A("B4"), OP.subtract)
-        scan(A("Ta"), A("SEG", 0, 64), A("Mk"), OP.mult, OP.add)
+            ts(A("le", 256 * s, 256 * s + 256), A("cum"), C("TC", 4 + s), OP.is_le)
+        scan(A("les"), A("ONE"), A("le"), OP.mult, OP.add)
+        cp(A("idx", 0, 2), A("les", 255, 512, 256))
+        ts(A("idx", 2, 4), A("acc", 2, 4), 0.5, OP.mult, 128.0, OP.add)
+        ix = A("idx", 0, 4)
+        lin("v", LA(t, r, 0, 64), IN(A("VL%d" % a), ix), FO * (t < 2))
+        tt(A("Mk"), IN(A("cH"), ix), A("DIAG"), OP.mult)
+        tt(A("K"), IN(A("cH"), ix), A("B4"), OP.subtract)
+        scan(A("Ta"), A("RS", 0, 64), A("Mk"), OP.add, OP.max)
         for s in range(4):
-            act(A("AB", 64 * s, 64 * s + 64), A("K"), AF.Abs, bias=C("Ta", 16 * s + 15), scale=-1.0)
-        ts(A("U", 0, 4), A("Ta", 15, 64, 16), 1.0 / HS, OP.mult)
-        ts(A(la, b0 + 4, b0 + 128, 32), A("idx", 0, 4), 8.0, OP.mult, float(off), OP.add)
-        tt(A("U", 4, 8), A("U", 0, 4), A("TC", 8, 12), OP.add)
-        ts(A(la, b0 + 2, b0 + 128, 32), A("U", 0, 4), 2048.0, OP.min)
+            act(A("AB", 65 * s, 65 * s + 64), A("K"), AF.Abs, bias=C("Ta", 16 * s + 15), scale=-1.0)
+        ts(A("U", 0, 4), A("Ta", 15, 64, 16), 1.0 / HS, OP.mult, C("Pf", 13), OP.add)
+        ts(A("U", 4, 8), ix, 8.0, OP.mult, C("Pf", 14 + a), OP.add)
+        scan(A("nf"), A("RB"), A("AB"), OP.add, OP.min)
         for s in range(4):
-            add("v", lambda e, s=s: e.tensor_reduce(T.nf[:, s:s + 1], T.AB[:, 64 * s:64 * s + 64], AX.X, OP.min, negate=True),
-                [C("nf", s)], [A("AB", 64 * s, 64 * s + 64)])
-        for s in range(4):
-            ts(C(la, b0 + 32 * s), C("nf", s), C("U", 4 + s), OP.add, C("TC", 12 + s), OP.min)
+            ts(LA(t, r, 64 + s, LW, 4), A("U", s, 8, 4), C("nf", 65 * s + 64), OP.subtract, C("TC", 12 + s), OP.min)
         send_lists(t)
+        sent = LA(t, r, 64, LW)
 
-        mm(A("MI", 0, 256), A("ID"), A("XC"), True, False)
-        mm(A("MI", 0, 256), A("ID"), A("XN%d" % a), False, True)
+        lc(A("MI", 0, 256), *([(A("IDB"), A("dead"))] * (t > 0) + [(A("ID"), A("XN%d" % a)), (A("ID"), A("XC"))]))
         act(A("av"), A("MI", 0, 256), bias=1535.75, scale=0.5)
-        act(A("hb"), A("XC"), AF.Relu, bias=1024.0, scale=-1.0)
-        act(A("xh", *z), A("XN%d" % a), bias=1536.0)
-        mm(A("XL", 0, 256), A("IDH"), A("xh", *z), True, False)
-        mm(A("XL", 0, 256), A("ID"), A("hb"), False, True)
-        tt(A("sh", *z), A("av"), A("XL", 0, 256), OP.min)
-        if t < 2:
-            act(own("X%d" % a, a), A("sh", *z), bias=-1536.0)
+        act(A("hb"), A("MI", 0, 256), AF.Relu, bias=1024.0, scale=-1.0)
+        lc(A("XA", 0, 256), (A("ID"), A("XN%d" % a)), (A("ID"), A("C15")), (A("ID"), A("hb")))
+        tt(A("sh", *z), A("av"), A("XA", 0, 256), OP.min)
+        after(sent)
         if t == 0:
+            act(own("X0", 0), A("sh", *z), bias=-1536.0)
+        if t == 1:
+            lc(A("XB", 256, 512), (A("IDB"), A("dead")), (A("IDH"), A("sh", *z)))
+            act(own("X1", 1), A("XB", 256, 512), bias=-1536.0)
+            for n, j in enumerate(j for j in range(N) if j != r):
+                act(A("van", 256 * n, 256 * n + 256), own("PI", 1, j=j), AF.Sign, bias=1.0 - FO)
+                o = A(("KA", "KB")[n % 2], 256, 512)
+                lc(o, (A("IDB"), A("van", 256 * n, 256 * n + 256)), (A("ID"), own("X1", 1, j=j)))
+                act(own("X1", 1, j=j), o)
+        if t == 0:
+            for o, c in ((A("M", 2048, TW), 0), (A("X0", 2048, TW), 0), (A("X1", 2048, TW), 0), (A("VL1", 256, 272), 5000)):
+                const(o, c)
+            iota(A("VL1", 0, 256), [[8, 256]], r + 4)
+            for n in range(256, TW, 256):
+                dma("y", T.PI[:, n:min(n + 256, TW)], T.PI[:, 0:min(256, TW - n)], [A("PI", n, min(n + 256, TW))],
+                    [A("PI", 0, 256), A("cO", 0, 2)], "lp", 2500.0)
+            dma("y", T.F[:, :], T.IO[:, 64:TW + 64], [A("F")], [A("IO")], "lf", 5000.0)
             cp(A("o1"), IN(A("M", 0, 2048), A("L1")))
-            ops[-1][2].extend(A(la, b0, b0 + 16)[1])
+            after(sent)
             for h in range(2):
-                ts(A("VR1", 2048 * h, 2048 * h + 2048), A("VR0", 2048 * h, 2048 * h + 2048), 4.0, OP.add)
-                ops[-1][2].extend(A(la, b0, b0 + 16)[1])
+                ts(A("SK", 1024 * h, 1024 * h + 1024), A("IO", 1024 * h, 1024 * h + 1024), C("Pf", 11), OP.is_equal)
+                after(sent)
             for j in range(4):
-                ms(A("X0", 4 + j, 2048, 8), BIG)
-                ops[-1][2].extend(A(la, b0, b0 + 16)[1])
+                act(A("X0", 4 + j, 2048, 8), A("SEED"), AF.Identity if j else AF.Silu, bias=BIG, scale=0.0, more=0.0 if j else 1300.0)
+                after(sent)
         if t > 0:
             om = A("OM", 256 * a, 256 * a + 256)
-            mm(A("EA", 0, 256), A("NIF"), A("mp", 16, 272), True, False)
-            mm(A("EA", 0, 256), A("IDH"), om, False, True)
-            tt(A("ph"), A("am"), A("EA", 0, 256), OP.mult)
-            mm(A("EA", 256, 512), A("IDH"), om, True, False)
-            mm(A("EA", 256, 512), A("NIH"), A("ph"), False, True)
-            act(A("YM", a, 512, 2), A("EA", 256, 512), bias=2048.0)
+            lc(A("FA", 0, 256), (A("IDF"), mp), (A("NIH"), om))
+            tt(A("ph"), A("dead"), A("FA", 0, 256), OP.mult)
+            after(sent)
+            lc(A("XB", 0, 256), (A("IDF"), mp), (A("NIH"), A("ph")))
+            act(A("YM", a, 512, 2), A("XB", 0, 256))
             marks(t - 1)
         if t == 1:
-            cp(own("M", 1), A("YM", 1, 512, 2))
-            for j in range(N):
-                cp(IN(A("X1"), A("c1", 4 * j, 4 * j + 4)), A("BG"))
+            cp(own("M", 1), mp)
+            after(sent)
         if t == 2:
             dma("y", T.ym[:, :], T.YM[:, :], [], [A("YM")], "sm", 2500.0)
         if t < 2:
-            act(A("XT"), IN(A("XN%d" % (1 - a)), A("PERM")))
-            send_table(t + 1, [A(la)])
+            turn(1 - a)
+            send_table(t + 1, [LA(t, None, 0, LW)])
+        if t == 0:
+            ends("VR1", 1, 0)
 
-        v1, c0 = A("v1", 16 * t, 16 * t + 16), 16 * t
-        cp(v1, A(la, 4, 512, 32))
-        cp(A("c1", c0, c0 + 16), A(la, 0, 512, 32))
-        cp(A("c2"), A(la, 2, 512, 32))
-        act(A("vR"), IN(A("IO"), v1))
-        act(A("cR", *z), IN(A("IO", 0, QW), A("c2")), bias=1.0)
+        c1, v1 = A("c1", 16 * t, 16 * t + 16), A("v1", 16 * t, 16 * t + 16)
+        cp(v1, LA(t, None, 68, 72))
+        ts(c1, LA(t, None, 64, 68), SP - 1.0, OP.min)
         for j in range(N - 1, -1, -1):
-            cp(IN(A("PI"), A("c1", c0 + 4 * j, c0 + 4 * j + 4)), A(la, 128 * j + 1, 128 * j + 128, 2))
-        tt(A("won", *z), IN(A("PI"), A("c2")), A("vR"), OP.is_equal)
+            cp(IN(A("PI"), LA(t, j, 64, 68)), LA(t, j, 0, 64))
+            after(LA(t, None, 64, LW))
+        cp(A("vF"), LA(t, None, 0, 64))
+        tt(A("won", *z), IN(A("PI"), c1), A("vF"), OP.is_equal)
         if t == 2:
-            tt(A("al"), IN(A("PI", 0, QW), A("cO")), A("VL0"), OP.not_equal)
+            tt(A("al"), IN(A("PI", 0, 2048), A("cO")), A("VL0", 0, 256), OP.not_equal)
         if t < 2:
-            lin(sq, A("d2"), IN(A("M", 0, QW), A("c2")))
-            lin(sq, A("d1"), IN(A("M"), v1), FO)
-            ts(A("vF"), A("vR"), FO, OP.add)
-            mm(A("EA", 0, 256), A("NIF"), A("vR"), True, False)
-            mm(A("EA", 0, 256), A("IDH"), A("d2"), False, True)
             for j in range(N - 1, -1, -1):
-                o, i = IN(A("F"), A("c1", c0 + 4 * j, c0 + 4 * j + 4)), A("d1", 64 * j, 64 * j + 64)
+                act(A("d1", 64 * j, 64 * j + 64), IN(A("M"), LA(t, j, 68, 72)), bias=FO)
+                after(LA(t, None, 64, LW))
+            act(A("d2"), IN(A("M"), c1), bias=FO - 1536.0)
+            lc(A("MI", 256, 512), (A("NID"), A("C15")), (A("IDF"), A("vF")), (A("NIH"), A("d2")))
+            for j in range(N - 1, -1, -1):
+                o, i = IN(A("F"), LA(t, j, 64, 68)), A("d1", 64 * j, 64 * j + 64)
                 add("s", lambda e, o=o, i=i: e.activation(o[0], i[0], AF.Silu), [o], [i])
-            tt(A("w"), A("won", *z), A("EA", 0, 256), OP.mult)
-            tt(IN(A("F"), v1), A("vF"), A("w"), OP.add)
-            act(A("junk", 0, 256), A("won", *z), acc=C("CNT", 0))
+            tt(A("w"), A("won", *z), A("MI", 256, 512), OP.mult)
+            tt(IN(A("F"), v1), A("vF"), A("w"), OP.subtract)
+            act(A("wb"), A("won", *z), scale=BIG, acc=C("CNT", 0))
             act(A("XG"), IN(A("X%d" % a), v1))
-            act(A("wb"), A("won", *z), scale=BIG)
             tt(IN(A("X%d" % a), v1), A("XG"), A("wb"), OP.add)
     marks(2)
     dma("s", T.yx[:, :], T.YX[:, :], [], [A("YX")], "sx", 2200.0)
-    if r not in CFG["keep"]:
-        dep, lev = _graph(ops, soft, mid)
-        CFG["keep"][r] = _plan(ops, dep, lev)
-    _emit(g, T, [ops[n] for n in CFG["keep"][r][1]])
+    if not CFG["keep"]:
+        dep, lev = _graph(ops, soft, mid, spare)
+        for c in alts:
+            for n, o in c[0]:
+                ops[n] = o
+        CFG["keep"][0] = _plan(ops, dep, lev, alts)
+    for c, side in zip(alts, CFG["keep"][0][3]):
+        for n, o in c[side]:
+            ops[n] = o
+    _emit(g, T, [ops[n] for n in CFG["keep"][0][1] if ops[n][6] >= 0])

@@ -17,10 +17,14 @@ CFG = {
     "f2": tuple(("vs"[n % 2], 32 * n, 32 * n + 32) for n in range(8)),
     "fg": ((0, 64), (64, 128), (128, 192), (192, 256)),
     "sel": ((0, 128), (128, 192), (192, 256)),
-    "gb": 64, "mk": "vvss",
+    "cnt": 128, "ge": ((0, 64), (64, 128), (128, 192), (192, 256)), "gx": ((0, 64), (64, 128), (128, 192), (192, 224), (224, 256)),
     "abs0": (1, 3, 5, 6), "abs": (1, 2, 3, 4, 5, 6),
     "gam": 1.56, "sig": 3.8, "pe": 0.42, "wake": 90.0, "hop": 3500.0, "look": 600.0, "slack": 60.0, "fac": 1.25, "gfac": 1.05,
-    "keep": {}, "seed": 1, "turns": 10, "jit": 500.0, "moves": 120000, "heat": 200.0, "mean": 0.3,
+    "load": 4000.0, "norm": 1.0, "cases": (
+        {"hop": 2800.0, "load": 3600.0, "fac": 1.25, "gam": 1.56, "sig": 3.8, "wake": 90.0, "norm": 1.0},
+        {"hop": 3300.0, "load": 4000.0, "fac": 1.5, "gam": 1.15, "sig": 2.5, "wake": 130.0, "norm": 1.0},
+        {"hop": 2400.0, "load": 3300.0, "fac": 1.1, "gam": 1.95, "sig": 5.2, "wake": 130.0, "norm": 1.1}),
+    "keep": {}, "seed": 3, "turns": 10, "jit": 500.0, "moves": 700000, "heat": 200.0, "mean": 0.8,
 }
 
 
@@ -30,9 +34,9 @@ def _sb(n, d):
 
 SCRATCH = {
     "M": _sb(TW, I32), "Q0": _sb(2048, I32), "Q1": _sb(2048, I32), "Q2": _sb(2048, I32),
-    "F": _sb(TW, F32), "PI": _sb(TW, F32), "IO": _sb(TW + 64, F32), "X0": _sb(TW, BF), "X1": _sb(TW, BF),
-    "VRH": _sb(2048, F16), "VR0": _sb(4096, F32), "VR1": _sb(4096, F32), "BC": _sb(2048, BF),
-    "E": _sb(4096, BF), "GX": _sb(4096, BF), "MX": _sb(4096, BF), "GF": _sb(4096, F16), "SK": _sb(2048, F16),
+    "F": _sb(TW, F32), "PI": _sb(TW, F32), "IO": _sb(TW, F32), "X0": _sb(TW, BF), "X1": _sb(TW, BF),
+    "VRH": _sb(4096, F16), "VR1": _sb(4096, F32), "BC": _sb(2048, BF),
+    "E": _sb(4096, BF), "GX": _sb(4096, BF), "MX": _sb(4096, BF), "GF": _sb(4096, F16), "SK": _sb(2048, BF),
     "Pi": _sb(8, I32), "Pf": _sb(16, F32), "I16": _sb(64, F32), "G16": _sb(128, F32), "SEED": _sb(256, F32),
     "J": _sb(32, I32), "Jf": _sb(96, F32), "RS": _sb(256, F32), "DIAG": _sb(64, F32), "TB": _sb(128, BF),
     "ONE": _sb(512, BF), "C15": _sb(256, BF),
@@ -47,19 +51,19 @@ SCRATCH = {
     "XN0": _sb(256, BF), "XN1": _sb(256, BF), "XTT": _sb(256, BF), "dead": _sb(256, BF),
     "pm": _sb(256, F32), "df": _sb(256, F32), "dn": _sb(256, F32), "sc": _sb(256, F32),
     "E1": _sb(256, BF), "E2": _sb(256, BF), "XC": _sb(256, BF), "cH": _sb(272, F32),
-    "yy": _sb(256, BF), "cum": _sb(256, BF), "le": _sb(512, F16), "les": _sb(512, F16), "junk": _sb(512, BF), "acc": _sb(8, F32),
+    "yy": _sb(256, BF), "cum": _sb(256, BF), "le": _sb(512, F16), "les": _sb(512, F16), "junk": _sb(1024, BF), "acc": _sb(16, F32), "Kc": _sb(64, F32),
     "K": _sb(64, F32), "Mk": _sb(64, F32), "Ta": _sb(64, F32), "AB": _sb(260, BF), "RB": _sb(260, BF), "U": _sb(8, F32), "nf": _sb(260, F32),
     "LA0": ("sbuf", [128, 4, LW], U16), "LA1": ("sbuf", [128, 4, LW], U16), "LA2": ("sbuf", [128, 4, LW], U16),
     "c1": _sb(48, U16), "v1": _sb(48, U16),
     "vF": _sb(256, F32), "cR": _sb(256, F32), "d1": _sb(256, F32), "d2": _sb(256, F16), "won": _sb(768, F32),
-    "w": _sb(256, F32), "w2": _sb(256, F32), "XG": _sb(256, BF), "wb": _sb(256, BF), "van": _sb(768, BF), "IDH": _sb(128, F16),
+    "w": _sb(256, F32), "w2": _sb(256, F32), "XG": _sb(256, BF), "wb": _sb(256, BF), "van": _sb(768, BF), "IDH": _sb(128, F16), "vR": _sb(256, F32),
     "av": _sb(256, F16), "hb": _sb(256, BF), "sh": _sb(768, F16),
     "al": _sb(256, BF), "pr": _sb(256, BF), "ph": _sb(256, F16), "YM": _sb(512, F32), "YX": _sb(512, BF),
     "KA": ("psum", [128, 512], F32), "KB": ("psum", [128, 512], F32), "XA": ("psum", [128, 512], F32),
     "XB": ("psum", [128, 512], F32), "FA": ("psum", [128, 512], F32), "FB": ("psum", [128, 512], F32),
     "VO": ("psum", [128, 512], F32), "MI": ("psum", [128, 512], F32),
 }
-DMAS = ["lm0", "lm1", "lx1", "lx0", "lth", "lp", "lf", "sp", "sm", "sx"]
+DMAS = ["lm0", "lm1", "lx1", "lx0", "lth", "lp", "lk", "lsM", "lsX0", "lsX1", "sp", "sm", "sx"]
 REMS = ["q0", "q1", "q2", "a0", "a1", "a2", "tq0", "tq1", "tq2", "ta0", "ta1", "ta2"]
 SEMAPHORES = ["sv", "ss", "st", "sg"] + DMAS + REMS
 
@@ -78,6 +82,23 @@ def _masks(topo, src, dsts):
         per = min([len(e) // len(near)] + [len(out[x]) for x in far])
         out[d] = e[n * per:(n + 1) * per]
     return out
+
+
+def _helper(topo, cores, src, dst):
+    if dst in topo.cores_of(src):
+        return None
+    return [c for c in topo.cores_of(src) if c not in cores and topo.die(c) != topo.die(src) and topo.may_write(c, dst)][0]
+
+
+def _hand_on(g, core, T, topo):
+    cores = list(T.cores)
+    for r, src in enumerate(cores):
+        dst = cores[r - 1]
+        if _helper(topo, cores, src, dst) == core:
+            rid, pid = topo.addr(dst, core)
+            g.wait_ge(T.sem["q0"], len([x for x in topo.engines(src, core) if x not in topo.engines(src, dst)]))
+            g.remote_dma(T.Q0[:, 1024:2048], T.Q0[:, 1024:2048], T.sem["q0"], T.sem["tq0"], pid, rid, topo.mask(core, dst))
+            g.wait_ge(T.sem["tq0"], len(topo.engines(core, dst)))
 
 
 def _deps(ops):
@@ -115,7 +136,8 @@ def _graph(ops, soft, mid, spare):
         if o[0] in ("g", "y"):
             if o[0] in last:
                 dep[n].setdefault(last[o[0]], False)
-            last[o[0]] = n
+            if o[0] not in last or ops[last[o[0]]][4] not in REMS:
+                last[o[0]] = n
         if o[0] is None and o[1] is not None:
             dep[n][[m for m in range(n) if ops[m][4] == o[1]][0]] = True
     full = [{m: (ops[m][7] + CFG["wake"] if hard else 0.0) for m, hard in d.items()} for d in dep]
@@ -139,7 +161,8 @@ def _graph(ops, soft, mid, spare):
     return full, lev
 
 
-def _plan(ops, dep, lev, alts):
+def _plan(cases):
+    ops, dep, lev = cases[0][:3]
     back = [{} for _o in ops]
     for n, d in enumerate(dep):
         for m, x in d.items():
@@ -157,60 +180,118 @@ def _plan(ops, dep, lev, alts):
             seed = (seed * 1103515245 + 12345) % 2147483648
             rank.append(x + CFG["jit"] * seed / 2147483648)
         lev = _order(ops, back, rank, [0.0 if back[n] else o[7] for n, o in enumerate(ops)])[1]
-    return _polish(ops, dep, back, best, alts)
+    return _polish(cases, back, best[1])
 
 
-def _times(ops, dep, out, start=0, end=None, why=None):
-    end, why = list(end or [0.0] * len(ops)), list(why or [-1] * len(ops))
-    last = {ops[n][0]: n for n in out[:start]}
-    free = {q: end[n] for q, n in last.items()}
-    for n in out[start:]:
-        q, c = ops[n][0], ops[n][6]
-        t, w = (free.get(q, 0.0), last.get(q, -1)) if q else (0.0, -1)
+def _times(on, cost, dep, out, start, old, stop=1 << 30, loss=0.0):
+    end, free = list(old), {on[n]: old[n] for n in out[max(0, start - 150):start]}
+    for lo in range(start, len(out), 48):
+        part = out[lo:lo + 48]
+        for n in part:
+            q = on[n]
+            t = free.get(q, 0.0)
+            for m, x in dep[n]:
+                x += end[m]
+                if x > t:
+                    t = x
+            end[n] = free[q] = t + cost[n]
+        if lo > stop:
+            lag = [end[n] - old[n] for n in part if on[n] in ("v", "s")]
+            if lag and min(lag) > loss:
+                return None
+            if not any(end[n] != old[n] for n in part):
+                return end
+    return end
+
+
+def _chain(on, cost, dep, out, end, n):
+    before, last, calls, pairs = {}, {}, [], []
+    for k in out:
+        before[k], last[on[k]] = last.get(on[k], -1), k
+    while n >= 0:
+        calls.append(n)
+        t, w = end[n] - cost[n] - 0.01, -1
         for m, x in dep[n]:
             if end[m] + x > t:
-                t, w = end[m] + x, m
-        end[n] = free[q] = t + c if c >= 0 else t - ops[n][7] - CFG["wake"]
-        last[q], why[n] = n, w
-    return end, why
+                w = m
+        if w < 0 <= before[n] and end[before[n]] > t:
+            w = before[n]
+            pairs.append((w, n))
+        n = w
+    return calls, pairs
 
 
-def _polish(ops, dep, back, best, alts):
-    out, side = best[1], [0] * len(alts)
-    pre, seed = [list(d.items()) for d in dep], [CFG["seed"]]
+def _polish(cases, back, out):
+    ops, dep, alts = cases[0][0], cases[0][1], cases[0][3]
+    side, seed = [0] * len(alts), [CFG["seed"]]
+    pre = [[list(d.items()) for d in case[1]] for case in cases]
     tails = [n for n in out if not back[n]]
+    whose = {n: c for c, forms in enumerate(alts) for n, o in forms[0]}
 
     def draw(k):
         seed[0] = (seed[0] * 1103515245 + 12345) % 2147483648
         return (seed[0] >> 8) % k
 
-    def worth(e):
-        return max(e[n] + ops[n][7] for n in tails) + CFG["mean"] * sum(e) / len(e)
+    def span(z, e):
+        return max(e[n] + cases[z][0][n][7] for n in tails)
+
+    def worth(new, i, j, old, each, room):
+        got, val = [], []
+        for z in range(len(cases)):
+            got.append(_times(on, cost[z], pre[z], new, i, old[z], j, room + 20.0))
+            if got[z] is None:
+                return None, None
+            val.append((span(z, got[z]) + CFG["mean"] * sum(got[z]) / len(ops)) / cases[z][5])
+            if val[z] > each[z] + 2.0 * room + 40.0:
+                return None, None
+        return val, got
+
+    def take(n):
+        on[n] = ops[n][0] or n
+        for z, case in enumerate(cases):
+            o = case[0][n]
+            cost[z][n] = o[6] if o[6] >= 0 else -o[7] - case[4]
 
     def flip(c):
         side[c] ^= 1
-        for n, o in alts[c][side[c]]:
-            ops[n] = o
+        for case in cases:
+            for n, o in case[3][c][side[c]]:
+                case[0][n] = o
+        for n, o in alts[c][0]:
+            take(n)
 
-    end, why = _times(ops, pre, out)
-    cur = worth(end)
-    best = (cur, out, end, list(side))
+    on, cost, path = [None] * len(ops), [[0.0] * len(ops) for _c in cases], None
+    for n in out:
+        take(n)
+    cur, now = worth(out, 0, len(out), cost, [1e18] * len(cases), 0.0)
+    best = (sum(cur), out, now, list(side))
     for it in range(CFG["moves"]):
         kind, c = draw(10), -1
-        if kind == 0 and alts:
+        if path is None or it % 64 == 0:
+            z = draw(len(cases))
+            path = _chain(on, cost[z], pre[z], out, now[z], max(tails, key=lambda k: now[z][k] + cases[z][0][k][7]))
+        if it % 256 == 0:
+            key = {}
+            for k, n in enumerate(out):
+                key[n] = (max([now[0][n] - cost[0][n]] + [key[m][0] for m in dep[n]]), k)
+            out = sorted(out, key=key.get)
+            cur, now = worth(out, 0, len(out), cost, [1e18] * len(cases), 0.0)
+            if sum(cur) < best[0]:
+                best = (sum(cur), out, now, list(side))
+            continue
+        if kind < 2:
             c = draw(len(alts))
+            if kind:
+                near = [c] + [whose[n] for n in path[0] if n in whose]
+                c = near[draw(len(near))]
             flip(c)
-            new, i = out, min(out.index(n) for n, o in alts[c][0])
+            new, i, j = out, out.index(alts[c][0][0][0]), out.index(alts[c][0][-1][0])
         else:
-            ahead, far = draw(2), draw(5)
+            ahead, far = draw(2), draw(5 if draw(4) else 30)
             if kind < 6:
-                n, pairs = max(tails, key=lambda z: end[z] + ops[z][7]), []
-                while why[n] >= 0:
-                    if why[n] not in dep[n]:
-                        pairs.append((why[n], n))
-                    n = why[n]
-                y, x = pairs[draw(len(pairs))]
-                i, j = out.index(y), out.index(x)
+                y, x = path[1][draw(len(path[1]))]
+                i, j = sorted((out.index(y), out.index(x)))
+                y, x = out[i], out[j]
             else:
                 i = j = draw(len(out))
                 x = y = out[i]
@@ -232,18 +313,16 @@ def _polish(ops, dep, back, best, alts):
             part = out[i:j + 1]
             a, b = [k for k in part if k in move], [k for k in part if k not in move]
             new = out[:i] + (a + b if ahead else b + a) + out[j + 1:]
-        e2, w2 = _times(ops, pre, new, i, end, why)
-        s2 = worth(e2)
-        if s2 <= cur + CFG["heat"] * (1.0 - it / CFG["moves"]) * draw(64) / 64.0:
-            cur, out, end, why = s2, new, e2, w2
-            if cur < best[0]:
-                best = (cur, out, end, list(side))
+        room = CFG["heat"] * (1.0 - it / CFG["moves"]) * draw(64) / 64.0
+        val, got = worth(new, i, j, now, cur, room)
+        if val and sum(val) <= sum(cur) + room * len(cases):
+            cur, out, now = val, new, got
         elif c >= 0:
             flip(c)
     for c in range(len(alts)):
         if side[c] != best[3][c]:
             flip(c)
-    return (max(best[2][n] + ops[n][7] for n in tails),) + best[1:]
+    return ([span(z, e) for z, e in enumerate(best[2])],) + best[1:]
 
 
 def _order(ops, dep, lev, ready):
@@ -320,11 +399,11 @@ def _emit(g, T, ops):
 def rank_program(g, core, T, topo):
     r = T.rank_of(core)
     if r is None:
-        return
+        return _hand_on(g, core, T, topo)
     cores = list(T.cores)
     N = len(cores)
     ops, soft, tail, mid, grp, alts, spare = [], [], {}, {}, {}, [], set()
-    SEL, FG, GB, fac = CFG["sel"], CFG["fg"], CFG["gb"], CFG["fac"]
+    SEL, FG, fac = CFG["sel"], CFG["fg"], CFG["fac"]
     WM = max(hi - lo for lo, hi in SEL)
 
     def A(name, lo=0, hi=None, st=1, p=None):
@@ -427,13 +506,30 @@ def rank_program(g, core, T, topo):
         else:
             add("s", lambda e: e.activation(o[0], i[0], f, bias=ap(bias), scale=scale, accum_out=acc[0]), [o, acc], [i, bias], more=20.0)
 
-    def lin(q, o, i, bias=0.0):
-        if q == "s":
-            act(o, i, bias=bias)
-        elif bias:
-            ts(o, i, bias, OP.add)
-        else:
-            cp(o, i)
+    def lin(q, o, i, bias=0.0, scale=1.0, wait=()):
+        up = 0.25 if SCRATCH[o[1][0][0]][2] in (U16, I32) else 0.0
+
+        def on_s():
+            act(o, i, bias=bias + up if up else bias, scale=scale)
+            after(*wait)
+
+        def on_v():
+            if scale != 1.0:
+                ts(o, i, scale, OP.mult, bias, OP.add)
+            elif bias:
+                ts(o, i, bias, OP.add)
+            else:
+                cp(o, i)
+            after(*wait)
+
+        either(q == "s", ((on_s, on_v),))
+
+    def flag(q, o, i, c, above):
+        either(q == "s", ((lambda: act(o, i, AF.Sign if above else AF.Relu, bias=-c if above else c + 1.0, scale=1.0 if above else -1.0),
+                           lambda: ts(o, i, c + 0.5, OP.is_gt if above else OP.is_lt)),))
+
+    def fill(q, o, c):
+        either(q == "s", ((lambda: act(o, A("SEED", 0, size(o)), bias=c, scale=0.0), lambda: ms(o, c)),))
 
     def mms(o, terms, a, b):
         c = sum(fac * CFG["pe"] * max(64, size(x)) * (4 if SCRATCH[x[1][0][0]][2] == F32 else 1) for l, x in terms)
@@ -466,17 +562,31 @@ def rank_program(g, core, T, topo):
     def ends(name, a, first):
         for c in range(first, 16 // NS):
             iota(A(name, 256 * NS * c, 256 * NS * (c + 1)), [[8, 16], [128, NS], [0, 16]], 128 * NS * c + 4 * a + r)
+            after(LA(0, r, 64, LW))
 
     def dma(q, o, i, out, ins, sem, lat):
         add(q, lambda e: e.dma_start(o, i), out, ins, sem, 16, cost=60.0, lat=lat)
 
     def send_table(t, wait):
-        d = cores[(r - 1 - t) % N]
+        d, s = cores[(r - 1 - t) % N], cores[(r + 1 + t) % N]
         rid, pid = topo.addr(d, core)
-        src = A("M", 0, 2048)
-        add("g", lambda e: e.remote_dma(T["Q%d" % t][:, :], src[0], T.sem["q%d" % t], T.sem["tq%d" % t], pid, rid, topo.mask(core, d)),
-            [], [src] + wait, "tq%d" % t, len(topo.engines(core, d)), cost=500.0, lat=10000.0)
-        add(None, "tq%d" % t, [A("Q%d" % t)], [], "q%d" % t, len(topo.engines(cores[(r + 1 + t) % N], core)), cost=0.0)
+        src, q, h = A("M", 0, 2048), T["Q%d" % t], _helper(topo, cores, core, d) if t == 0 else None
+        n = len(topo.engines(core, d))
+        if h is None:
+            def call(e):
+                e.remote_dma(q[:, :], src[0], T.sem["q%d" % t], T.sem["tq%d" % t], pid, rid, topo.mask(core, d))
+        else:
+            rest = [x for x in topo.engines(core, h) if x not in topo.engines(core, d)]
+            n += len(rest)
+            trs = [RemoteDMATransfer(dst_ids=[DstId(rid=a, pnc=b)], dma_engine_mask=mask, remote_sem=T.sem["q0"],
+                                     src=T.M[:, lo:lo + 1024], dst=q[:, lo:lo + 1024])
+                   for (a, b), mask, lo in (((rid, pid), topo.mask(core, d), 0), (topo.addr(h, core), sum(1 << x for x in rest), 1024))]
+
+            def call(e):
+                e.remote_dma_fused(trs, local_sem=T.sem["tq0"])
+        add("g", call, [], [src] + wait, "tq%d" % t, n, cost=500.0, lat=10000.0)
+        h = _helper(topo, cores, s, core) if t == 0 else None
+        add(None, "tq%d" % t, [A("Q%d" % t)], [], "q%d" % t, len(topo.engines(s, core)) + (len(topo.engines(h, core)) if h else 0), cost=0.0)
 
     def send_lists(t):
         peers = [c for c in cores if c != core]
@@ -487,7 +597,7 @@ def rank_program(g, core, T, topo):
             rid, pid = topo.addr(d, core)
             trs.append(RemoteDMATransfer(dst_ids=[DstId(rid=rid, pnc=pid)], dma_engine_mask=sum(1 << x for x in mk[d]),
                                          remote_sem=T.sem["a%d" % t], src=src[0], dst=src[0]))
-        add("g", lambda e: e.remote_dma_fused(trs, local_sem=T.sem["ta%d" % t]), [], [src], "ta%d" % t,
+        add("g", lambda e: e.remote_dma_fused(trs, local_sem=T.sem["ta%d" % t]), [], [src, A("SK")] + [A("F", 0, 928)] * (t == 0), "ta%d" % t,
             sum(len(mk[d]) for d in peers), cost=500.0, lat=CFG["hop"] - 500.0)
         n = sum(len(_masks(topo, s, [c for c in cores if c != s])[core]) for s in peers)
         add(None, "ta%d" % t, [LA(t, j, 0, LW) for j in range(N) if j != r], [], "a%d" % t, n, cost=0.0)
@@ -501,14 +611,14 @@ def rank_program(g, core, T, topo):
         return A(("KA", "KB")[n % 2], lo % 256, (hi - 1) % 256 + 1)
 
     ms(A("thi"), 0)
-    dma("y", T.M[:, 0:1024], T.mt[:, 0:1024], [A("M", 0, 1024)], [], "lm0", 4000.0)
-    dma("s", T.M[:, 1024:2048], T.mt[:, 1024:2048], [A("M", 1024, 2048)], [], "lm1", 4000.0)
-    dma("y", T.X1[:, 0:2048], T.xv[:, :], [A("X1", 0, 2048), C("Ai", 7)], [], "lx1", 4500.0)
+    dma("y", T.M[:, 0:1024], T.mt[:, 0:1024], [A("M", 0, 1024)], [], "lm0", CFG["load"])
+    dma("s", T.M[:, 1024:2048], T.mt[:, 1024:2048], [A("M", 1024, 2048)], [], "lm1", CFG["load"])
+    dma("y", T.X1[:, 0:2048], T.xv[:, :], [A("X1", 0, 2048), C("Ai", 7)], [], "lx1", CFG["load"] + 700.0)
     dma("y", T.thi[0:128:16, 0:1], T.th[:], [A("thi")], [], "lth", 2500.0)
     dma("y", T.X0[:, 0:2048], T.xv[:, :], [A("X0", 0, 2048)], [C("Ai", 7)], "lx0", 3500.0)
 
-    iota(A("SEED"), [[8, 16 // NS], [128, NS], [0, 16]], r)
     iota(C("Pi", 0), [[0, 1]], 0, 1)
+    iota(A("SEED"), [[8, 16 // NS], [128, NS], [0, 16]], r)
     iota(A("Jf", 0, 16), [[128 * NS, 16 // NS], [128 // NS, NS]], r)
     iota(A("IO", 0, 256), [[1, 256]], 1)
     iota(A("G16"), [[1, 8], [0, 16]], 0)
@@ -519,34 +629,45 @@ def rank_program(g, core, T, topo):
     const(A("mp", 0, 16), 0)
     const(A("mp", 272, 288), 0)
     send_table(0, [])
-    ends("VR0", 0, 8 // NS)
     iota(A("VL0", 0, 256), [[8, 256]], r)
     iota(A("IO", 256, 2048), [[1, 1792]], 257)
     iota(A("B4"), [[int(KU), 64]], 0)
     const(A("VL0", 256, 272), 5000)
-    iota(A("IO", 2048, TW + 64), [[1, TW - 1984]], 2049)
-    const(A("PI", 0, 256), FO - 1)
-    const(A("RB"), 0)
-    const(A("C15"), 1536)
-    cp(A("VRH", 0, 256), A("SEED"))
+    iota(A("IO", 2048, TW), [[1, TW - 2048]], 2049)
+    const(A("PI", 0, 256), -1)
+    ms(A("ONE"), 1.0)
+    for n in range(0, 2048, 256):
+        dma("y", T.SK[:, n:n + 256], T.ONE[:, 0:256], [A("SK", n, n + 256)], [A("ONE", 0, 256), C("Ai", 7)], "lk", 4000.0)
+    for n in range(256, TW, 256):
+        dma("y", T.PI[:, n:min(n + 256, TW)], T.PI[:, 0:min(256, TW - n)], [A("PI", n, min(n + 256, TW))],
+            [A("PI", 0, 256), A("X0", 0, 16)], "lp", 5000.0)
+    for n in range(0, 2048, 1024):
+        o = A("SK", n, n + 1024)
+        add("g", lambda e, o=o, n=n: e.affine_select(o[0], o[0], [[-1, 8], [512, 8], [33, 16]], OP.is_equal, 0.0, -n // 128, -32),
+            [A("SK")], [A("SK")], cost=fac * (170 + 1.66 * 1024))
+    ms(A("RB", 0, 130), 0.0)
+    ms(A("RB", 130, 260), -KU)
+    for nm, src in (("M", T.mt), ("X0", T.xv), ("X1", T.xv)):
+        dma("y", T[nm][:, 2048:TW], src[:, 0:TW - 2048], [A(nm, 2048, TW)], [C("Ai", 7)], "ls" + nm, 3500.0)
+    iota(A("F", 0, 928), [[1, 928]], int(FO))
+    for n in range(928, TW, 464):
+        lin("s", A("F", n, n + 464), A("IO", n, n + 464), FO - 1.0)
+    lin("s", A("VRH", 0, 256), A("SEED"))
     for n in (256, 512, 1024):
-        ts(A("VRH", n, 2 * n), A("VRH", 0, n), n / 2.0 / (NS if n < 256 * NS else 1), OP.add)
+        lin("v", A("VRH", n, 2 * n), A("VRH", 0, n), n / 2.0 / (NS if n < 256 * NS else 1))
+    for n in (2048, 3072):
+        lin("v", A("VRH", n, n + 1024), A("VRH", 0, 1024), n / 2.0)
     ts(C("Pi", 1), C("Pi", 0), 15, OP.bitwise_and)
     ts(C("Pi", 2), C("Pi", 0), 4, OP.logical_shift_right)
     ts(C("Pi", 3), C("Pi", 0), NS - 1, OP.bitwise_and)
     ts(C("Pi", 4), C("Pi", 0), 15, OP.bitwise_and, NS.bit_length() - 1, OP.logical_shift_right)
     cp(A("Pf", 0, 5), A("Pi", 0, 5))
-    ms(A("ONE"), 1.0)
-    ms(C("ONE", 256), 0.0)
-    act(A("AB", 64, 260, 65), A("IO", 0, 4), bias=1e29, scale=0.0)
-    act(C("Pf", 5), C("Pf", 0), bias=1.0)
-    act(C("Pf", 6), C("Pf", 2), bias=16.0, scale=16.0)
-    act(C("Pf", 8), C("Pf", 4), scale=8.0)
-    act(C("Pf", 7), C("Pf", 3), bias=C("Pf", 8), scale=128.0)
-    act(C("Pf", 9), C("Pf", 1), scale=float(NS))
-    act(C("Pf", 10), C("Pf", 0), bias=float(r), scale=8.0)
-    act(C("Pf", 11), C("Pf", 1), bias=C("Pf", 5), scale=128.0)
-    act(C("Pf", 12), C("Pf", 2), scale=-16.0)
+    fill("v", C("ONE", 256), 0.0)
+    fill("s", A("AB", 64, 260, 65), 1e29)
+    for n, m, bias, scale in ((5, 0, 1.0, 1.0), (6, 2, 16.0, 16.0), (8, 4, 0.0, 8.0), (7, 3, C("Pf", 8), 128.0), (9, 1, 0.0, float(NS)),
+                              (10, 0, float(r), 8.0), (12, 2, 0.0, -16.0),
+                              (13, 1, 0.0, KU), (14, 1, float(r), KU), (15, 1, r + 4.0, KU)):
+        lin("s", C("Pf", n), C("Pf", m), bias, scale)
     ts(A("L0"), A("Jf", 0, 16), C("Pf", 7), OP.add)
     ts(A("L1"), A("Jf", 0, 16), C("Pf", 7), OP.add, 4.0, OP.add)
     ts(A("PERM"), A("Jf", 16, 32), C("Pf", 9), OP.add)
@@ -556,41 +677,40 @@ def rank_program(g, core, T, topo):
     for n in range(0, 2048, 1024):
         ts(A("BC", n, n + 1024), A("VRH", n, n + 1024), C("Pf", 10), OP.is_equal)
     for nm, wt in (("WG", 16.0), ("WM", -32.0), ("WA", -16.0)):
-        act(A(nm), A("WE"), scale=wt / 65536.0)
-    act(A("BON"), A("BO"), scale=-1.0 / 8192)
+        lin("s", A(nm), A("WE"), 0.0, wt / 65536.0)
+    lin("s", A("BON"), A("BO"), 0.0, -1.0 / 8192)
     for nm, wt in (("NID", -1.0), ("IDF", 1.0), ("NIH", -1.0), ("IDH", 1.0), ("IDB", BIG), ("IDN", -64.0)):
-        act(A(nm), A("ID"), scale=wt)
-    ms(A("RS", 0, WM), 0.0)
-    ms(A("RS", 0, WM, 16), -1e29)
+        lin("s", A(nm), A("ID"), 0.0, wt)
+    fill("s", A("RS", 0, WM), 0.0)
+    fill("s", A("RS", 0, WM, 16), -1e29)
     ts(A("DIAG"), A("I16"), C("Pf", 1), OP.is_equal)
     ts(A("J", 16, 32), A("J", 0, 16), 4, OP.logical_shift_right, 1, OP.bitwise_and)
-    ts(A("Jf", 32, 48), A("J", 0, 16), C("Pf", 12), OP.add)
-    ts(A("Jf", 48, 64), A("J", 16, 32), 272.0, OP.mult)
+    lin("s", A("Jf", 32, 48), A("J", 0, 16), C("Pf", 12))
+    lin("s", A("Jf", 48, 64), A("J", 16, 32), 0.0, 272.0)
     tt(A("Jf", 64, 80), A("Jf", 32, 48), A("Jf", 48, 64), OP.add)
-    cp(A("OW"), A("Jf", 64, 80))
-    act(A("TC", 0, 4), A("IO", 0, 4), bias=C("Pf", 1), scale=16.0)
-    act(A("TC", 4, 8), A("TC", 0, 4), bias=-32.0, scale=2.0)
-    act(A("TC", 8, 12), A("TC", 0, 4), bias=-31.0, scale=2.0)
-    act(A("TC", 12, 16), A("TC", 0, 4), bias=float(SP + 64 * r - 16))
-    for n, c in ((13, 0), (14, r), (15, r + 4)):
-        act(C("Pf", n), C("Pf", 1), bias=float(c), scale=KU)
-    act(A("RB", 64, 260, 65), A("IO", 0, 4), bias=16.0 * KU, scale=-16.0 * KU)
-    act(A("RB", 0, 260, 65), A("IO", 0, 4), bias=1e29, scale=0.0)
-    act(C("CNT", 1), C("ONE", 0), scale=-1.5 * BIG / 8)
-    act(A("O16"), A("G16"), bias=0.0625 / BIG, scale=0.0)
-    act(A("cH", 256, 272), A("G16", 0, 16), bias=4000.0 * HS, scale=0.0)
-    cp(C("thb", 0), C("thi", 0))
+    lin("s", A("OW"), A("Jf", 64, 80))
+    lin("s", A("TC", 0, 4), A("IO", 0, 4), C("Pf", 1), 16.0)
+    lin("s", A("TC", 4, 8), A("TC", 0, 4), -32.0, 2.0)
+    lin("s", A("TC", 8, 12), A("TC", 0, 4), -31.0, 2.0)
+    lin("s", A("TC", 12, 16), A("TC", 0, 4), float(SP + 64 * r - 16))
+    lin("s", A("RB", 64, 130, 65), A("IO", 0, 2), 16.0 * KU, -16.0 * KU)
+    lin("s", A("RB", 194, 260, 65), A("IO", 2, 4), 272.0 * KU, -16.0 * KU)
+    for o, c in ((A("RB", 0, 260, 65), 1e29), (C("CNT", 1), -1.5 * BIG / 8), (A("O16"), 0.0625 / BIG), (A("cH", 256, 272), 4000.0 * HS)):
+        fill("s", o, c)
+    lin("s", C("thb", 0), C("thi", 0))
 
     def choose(t, blocks, oc):
         a = t % 2
         for n in range(8):
             lo, hi = 512 * n, 512 * n + 512
-            if 32 * n % GB == 0:
-                o = A(oc, 32 * n, 32 * n + GB)
-                tt(A("E", lo, lo + 16 * GB), IN(A("M", 0, 2048), o), A("VR%d" % a if a or lo >= 2048 else "VRH", lo, lo + 16 * GB), OP.is_equal)
-                chain("v")
-                act(A("GX", lo, lo + 16 * GB), IN(A("X%d" % (1 - a), 0, 2048), o))
-                chain("s")
+            for x, y in CFG["ge"]:
+                if x == 32 * n:
+                    tt(A("E", lo, 16 * y), IN(A("M", 0, 2048), A(oc, x, y)), A("VR1" if a else "VRH", lo, 16 * y), OP.is_equal)
+                    chain("v")
+            for x, y in CFG["gx"]:
+                if x == 32 * n:
+                    lin("s", A("GX", lo, 16 * y), IN(A("X%d" % (1 - a), 0, 2048), A(oc, x, y)))
+                    chain("s")
             c0 = 32 * n // (16 * NS) * 16 * NS
             sel = [i for i, (x, y) in enumerate(SEL) if x <= c0 < y][0]
             kb = key(sel, c0, c0 + 16 * NS)
@@ -617,7 +737,7 @@ def rank_program(g, core, T, topo):
     def turn(a):
         for h in range(2):
             mm(A("XB", 128 * h, 128 * h + 128), A("XN%d" % a, 128 * h, 128 * h + 128), A("ID"), True, True)
-        act(A("XTT"), A("XB", 0, 256))
+        lin("s", A("XTT"), A("XB", 0, 256))
 
     def vote(t, n):
         a, (lo, hi) = t % 2, SEL[n]
@@ -630,11 +750,11 @@ def rank_program(g, core, T, topo):
         tt(A("dn", lo, hi), IN(A("mW"), A("OW", lo // 16, hi // 16)), A("df", lo, hi), OP.subtract)
         scan(A("sc", lo, hi), A("df", lo, hi), A("dn", lo, hi), OP.min, OP.max)
         c = A("cO", lo // 16, hi // 16)
-        cp(c, A("sc", lo + 15, hi, 16))
-        act(A("XC", lo, hi), IN(A("X%d" % (1 - a), 0, 2048), c))
+        lin("v", c, A("sc", lo + 15, hi, 16))
+        lin("s", A("XC", lo, hi), IN(A("X%d" % (1 - a), 0, 2048), c))
         tt(A("E2", lo, hi), IN(A("Q%d" % t), c), A("VL%d" % a, lo, hi), OP.is_equal)
         tt(A("E1", lo, hi), IN(A("M", 0, 2048), c), A("VL%d" % a, lo, hi), OP.is_equal)
-        act(A("cH", lo, hi), IN(A("IO", 0, 2048), c), scale=HS, bias=-HS)
+        lin("s", A("cH", lo, hi), IN(A("IO", 0, 2048), c), -HS, HS)
         vo = A("VO", lo, hi)
         lc(vo, *([(A("IDN"), A("dead", lo, hi))] * (t > 0) +
                  [(A("BON"), A("XC", lo, hi)), (A("BO"), A("E2", lo, hi)), (A("BO"), A("E1", lo, hi))]))
@@ -643,35 +763,34 @@ def rank_program(g, core, T, topo):
 
     def follow(units, src, dst, col):
         for q, lo, hi in units:
-            o, i = A("GF", 16 * lo, 16 * hi), IN(A("F", 0, 2048), A(src, lo, hi))
-            either(q == "s", ((lambda: lin("s", o, i, -FO), lambda: lin("v", o, i, -FO)),))
+            lin(q, A("GF", 16 * lo, 16 * hi), IN(A("F", 0, 2048), A(src, lo, hi)), -FO)
             chain(q + dst)
         for n, (lo, hi) in enumerate(FG):
             o = A("FB" if col else "FA", lo, hi)
             mms(o, [(A("SK", 128 * k, 128 * k + 128), A("GF", 16 * lo + k, 16 * hi, 16)) for k in range(16)], True, True)
-            cp(A(dst, lo, hi), o)
-            if col:
-                act(A("m2", lo, hi), o, bias=RND)
+            lin("v", A(dst, lo, hi), o)
+        if col:
+            lin("s", A("m2"), A("FB", 0, 256), RND)
 
     def marks(t):
         a, z = t % 2, (256 * t, 256 * t + 256)
         cw = IN(A("IO", 0, TW), A("c1", 16 * t, 16 * t + 16))
         if t == 2:
-            act(A("cR"), cw)
+            lin("s", A("cR"), cw)
             mm(A("FB", 0, 256), A("IDF"), A("cR"), True, True)
             tt(A("w2"), A("won", *z), A("FB", 0, 256), OP.mult)
         else:
             tt(A("w2"), cw, A("won", *z), OP.mult)
-            after(LA(t + 1, r, 64, LW))
-        ts(IN(A("PI"), A("v1", 16 * t, 16 * t + 16)), A("w2"), 1.0, OP.mult, FO * (t == 0) - 1.0, OP.add)
+            after(A("AB"))
+        ts(IN(A("PI"), A("v1", 16 * t, 16 * t + 16)), A("w2"), 1.0, OP.mult, -1.0, OP.add)
         if t == 2:
             dma("y", T.yp[:, :], T.PI[0:128:16, 0:2048], [], [A("PI")], "sp", 2200.0)
         else:
-            act(A("al"), own("PI", a), AF.Relu, scale=-1.0, bias=FO * (t == 0))
+            flag("s", A("al"), own("PI", a), -1.0, False)
         lc(A("KA", 0, 256), (A("ID"), A("XN%d" % a)), (A("ID"), A("C15")), (A("NIH"), A("sh", *z)))
         tt(A("pr"), A("al"), A("KA", 0, 256), OP.mult)
         lc(A("KB", 0, 256), (A("ID"), A("XN%d" % a)), (A("NID"), A("pr")))
-        act(A("XN0") if t == 0 else A("YX", a, 512, 2), A("KB", 0, 256))
+        lin("s", A("XN0") if t == 0 else A("YX", a, 512, 2), A("KB", 0, 256))
 
     for t in range(3):
         a = t % 2
@@ -679,102 +798,102 @@ def rank_program(g, core, T, topo):
         z = (256 * t, 256 * t + 256)
         if t == 0:
             for lo, hi in ((0, 64), (64, 256)):
-                cp(A("o0", lo, hi), IN(A("M", 0, 2048), A("L0", lo // 16, hi // 16)))
-            act(A("XN0"), own("X1", 0))
-            for j in range(4):
-                if CFG["mk"][j] == "v":
-                    ms(A("X1", j, 2048, 8), BIG)
-                else:
-                    act(A("X1", j, 2048, 8), A("SEED"), bias=BIG, scale=0.0)
-            act(A("XN1"), own("X1", 1))
-            act(mp, own("M", 0))
+                lin("s" if lo else "v", A("o0", lo, hi), IN(A("M", 0, 2048), A("L0", lo // 16, hi // 16)))
+            lin("s", A("XN0"), own("X1", 0))
+            const(A("X1", 0, 2048, 8), BIG)
+            for j in range(1, 4):
+                fill("vs"[j % 2], A("X1", j, 2048, 8), BIG)
+            lin("s", A("XN1"), own("X1", 1))
+            lin("s", mp, own("M", 0))
             for b in range(2):
-                act(A("OM", 256 * b, 256 * b + 256), own("M", b))
+                lin("s", A("OM", 256 * b, 256 * b + 256), own("M", b))
             mm(A("VO", 256, 257), A("BO"), C("thb", 0), True, True)
-            act(C("THR", 0), A("VO", 256, 257), bias=0.5, scale=-1.0)
-            act(C("THR", 6), C("THR", 0), bias=-1.5)
+            lin("s", C("THR", 0), A("VO", 256, 257), 0.5, -1.0)
+            lin("s", C("THR", 6), C("THR", 0), -1.5)
             turn(0)
             choose(0, CFG["abs0"], "o0")
         else:
-            act(A("dead"), own("PI", a), AF.Sign, bias=1.0 - FO)
-            if t == 2:
-                for n in range(0, TW, 580):
-                    act(A("PI", n, n + 580), A("PI", n, n + 580), bias=-FO)
+            flag("s", A("dead"), own("PI", a), -1.0, True)
             lc(A("VO", 256, 257), (A("O16"), C("CNT", 1)), (A("O16"), C("CNT", 0)))
-            act(C("THR", 3), A("VO", 256, 257), bias=C("THR", 6), scale=-1.0)
-            act(C("THR", 4), A("VO", 256, 257), bias=RND, scale=0.25)
-            act(C("THR", 5), C("THR", 4), bias=-RND)
-            act(C("THR", t), C("THR", 5), bias=C("THR", 3), scale=4.0)
+            lin("s", C("THR", 3), A("VO", 256, 257), C("THR", 6), -1.0)
+            lin("s", C("THR", 4), A("VO", 256, 257), RND, 0.25)
+            lin("s", C("THR", 5), C("THR", 4), -RND)
+            lin("s", C("THR", t), C("THR", 5), C("THR", 3), 4.0)
             follow(CFG["f1"], "o%d" % a, "o2", 0)
             follow(CFG["f2"], "o2", "oc", 256)
-            act(mp, IN(A("m2"), A("PERM")), bias=-RND)
+            lin("s", mp, IN(A("m2"), A("PERM")), -RND)
             choose(t, CFG["abs"], "oc")
 
+        lo = CFG["cnt"]
+        w = 256 - lo
+        if lo:
+            for s in range(4):
+                act(A("junk", 256 * s, 256 * s + lo), A("cum", 0, lo), AF.Sign, bias=C("TC", 8 + s), scale=-1.0, acc=C("acc", s))
+            lin("s", A("acc", 4, 6), A("acc", 0, 2), lo / 2.0 + 0.25, 0.5)
+            lin("s", A("acc", 6, 8), A("acc", 2, 4), 128.25, 0.5)
         for s in (2, 3):
-            act(A("junk", 256 * s - 512, 256 * s - 256), A("cum"), AF.Sign, bias=C("TC", 8 + s), scale=-1.0, acc=C("acc", s))
+            act(A("junk", 256 * s + lo, 256 * s + 256), A("cum", lo, 256), AF.Sign, bias=C("TC", 8 + s), scale=-1.0, acc=C("acc", 8 + s))
+            if lo:
+                act(C("idx", s), C("acc", 8 + s), bias=C("acc", 4 + s), scale=0.5)
         for s in (0, 1):
-            ts(A("le", 256 * s, 256 * s + 256), A("cum"), C("TC", 4 + s), OP.is_le)
-        scan(A("les"), A("ONE"), A("le"), OP.mult, OP.add)
-        cp(A("idx", 0, 2), A("les", 255, 512, 256))
-        ts(A("idx", 2, 4), A("acc", 2, 4), 0.5, OP.mult, 128.0, OP.add)
+            ts(A("le", w * s, w * s + w), A("cum", lo, 256), C("TC", 4 + s), OP.is_le)
+        scan(A("les", 0, 2 * w), A("ONE", 256 - w, 256 + w), A("le", 0, 2 * w), OP.mult, OP.add)
+        if lo:
+            for s in (0, 1):
+                ts(C("idx", s), C("les", w * s + w - 1), C("acc", 4 + s), OP.add)
+        else:
+            lin("v", A("idx", 0, 2), A("les", 255, 512, 256))
+            lin("s", A("idx", 2, 4), A("acc", 10, 12), 128.0, 0.5)
         ix = A("idx", 0, 4)
-        lin("v", LA(t, r, 0, 64), IN(A("VL%d" % a), ix), FO * (t < 2))
+        lin("s", LA(t, r, 0, 64), IN(A("VL%d" % a), ix))
         tt(A("Mk"), IN(A("cH"), ix), A("DIAG"), OP.mult)
         tt(A("K"), IN(A("cH"), ix), A("B4"), OP.subtract)
+        lin("s", A("Kc"), IN(A("cH"), ix))
         scan(A("Ta"), A("RS", 0, 64), A("Mk"), OP.add, OP.max)
-        for s in range(4):
+        for s in (0, 1):
             act(A("AB", 65 * s, 65 * s + 64), A("K"), AF.Abs, bias=C("Ta", 16 * s + 15), scale=-1.0)
-        ts(A("U", 0, 4), A("Ta", 15, 64, 16), 1.0 / HS, OP.mult, C("Pf", 13), OP.add)
-        ts(A("U", 4, 8), ix, 8.0, OP.mult, C("Pf", 14 + a), OP.add)
+        for s in (2, 3):
+            ts(A("AB", 65 * s, 65 * s + 64), A("Kc"), C("Ta", 16 * s + 15), OP.is_equal, -193.0 * KU, OP.mult)
+        lin("v", A("U", 0, 4), A("Ta", 15, 64, 16), C("Pf", 13), 1.0 / HS)
+        lin("s", A("U", 4, 8), ix, C("Pf", 14 + a), 8.0)
         scan(A("nf"), A("RB"), A("AB"), OP.add, OP.min)
         for s in range(4):
             ts(LA(t, r, 64 + s, LW, 4), A("U", s, 8, 4), C("nf", 65 * s + 64), OP.subtract, C("TC", 12 + s), OP.min)
         send_lists(t)
         sent = LA(t, r, 64, LW)
+        if t == 0:
+            act(A("C15"), A("ONE", 0, 256), AF.Silu, scale=1536.0, more=1300.0)
+            after(A("AB"))
 
         lc(A("MI", 0, 256), *([(A("IDB"), A("dead"))] * (t > 0) + [(A("ID"), A("XN%d" % a)), (A("ID"), A("XC"))]))
-        act(A("av"), A("MI", 0, 256), bias=1535.75, scale=0.5)
+        lin("s", A("av"), A("MI", 0, 256), 1535.75, 0.5)
         act(A("hb"), A("MI", 0, 256), AF.Relu, bias=1024.0, scale=-1.0)
         lc(A("XA", 0, 256), (A("ID"), A("XN%d" % a)), (A("ID"), A("C15")), (A("ID"), A("hb")))
         tt(A("sh", *z), A("av"), A("XA", 0, 256), OP.min)
-        after(sent)
         if t == 0:
-            act(own("X0", 0), A("sh", *z), bias=-1536.0)
+            lin("s", own("X0", 0), A("sh", *z), -1536.0)
         if t == 1:
-            lc(A("XB", 256, 512), (A("IDB"), A("dead")), (A("IDH"), A("sh", *z)))
-            act(own("X1", 1), A("XB", 256, 512), bias=-1536.0)
             for n, j in enumerate(j for j in range(N) if j != r):
-                act(A("van", 256 * n, 256 * n + 256), own("PI", 1, j=j), AF.Sign, bias=1.0 - FO)
-                o = A(("KA", "KB")[n % 2], 256, 512)
+                act(A("van", 256 * n, 256 * n + 256), own("PI", 1, j=j), AF.Sign, bias=1.0)
+                after(A("MX"))
+                o = A(("FA", "FB")[n % 2], 256, 512)
                 lc(o, (A("IDB"), A("van", 256 * n, 256 * n + 256)), (A("ID"), own("X1", 1, j=j)))
-                act(own("X1", 1, j=j), o)
+                lin("s", own("X1", 1, j=j), o)
+            lc(A("XB", 256, 512), (A("IDB"), A("dead")), (A("IDH"), A("sh", *z)))
+            lin("s", own("X1", 1), A("XB", 256, 512), -1536.0)
         if t == 0:
-            for o, c in ((A("M", 2048, TW), 0), (A("X0", 2048, TW), 0), (A("X1", 2048, TW), 0), (A("VL1", 256, 272), 5000)):
-                const(o, c)
-            iota(A("VL1", 0, 256), [[8, 256]], r + 4)
-            for n in range(256, TW, 256):
-                dma("y", T.PI[:, n:min(n + 256, TW)], T.PI[:, 0:min(256, TW - n)], [A("PI", n, min(n + 256, TW))],
-                    [A("PI", 0, 256), A("cO", 0, 2)], "lp", 2500.0)
-            dma("y", T.F[:, :], T.IO[:, 64:TW + 64], [A("F")], [A("IO")], "lf", 5000.0)
-            cp(A("o1"), IN(A("M", 0, 2048), A("L1")))
-            after(sent)
-            for h in range(2):
-                ts(A("SK", 1024 * h, 1024 * h + 1024), A("IO", 1024 * h, 1024 * h + 1024), C("Pf", 11), OP.is_equal)
-                after(sent)
+            lin("v", A("o1"), IN(A("M", 0, 2048), A("L1")))
             for j in range(4):
-                act(A("X0", 4 + j, 2048, 8), A("SEED"), AF.Identity if j else AF.Silu, bias=BIG, scale=0.0, more=0.0 if j else 1300.0)
-                after(sent)
+                fill("v", A("X0", 4 + j, 2048, 8), BIG)
         if t > 0:
             om = A("OM", 256 * a, 256 * a + 256)
             lc(A("FA", 0, 256), (A("IDF"), mp), (A("NIH"), om))
             tt(A("ph"), A("dead"), A("FA", 0, 256), OP.mult)
-            after(sent)
             lc(A("XB", 0, 256), (A("IDF"), mp), (A("NIH"), A("ph")))
-            act(A("YM", a, 512, 2), A("XB", 0, 256))
+            lin("s", A("YM", a, 512, 2), A("XB", 0, 256))
             marks(t - 1)
         if t == 1:
-            cp(own("M", 1), mp)
-            after(sent)
+            lin("s", own("M", 1), mp)
         if t == 2:
             dma("y", T.ym[:, :], T.YM[:, :], [], [A("YM")], "sm", 2500.0)
         if t < 2:
@@ -782,39 +901,49 @@ def rank_program(g, core, T, topo):
             send_table(t + 1, [LA(t, None, 0, LW)])
         if t == 0:
             ends("VR1", 1, 0)
+            iota(A("VL1", 0, 256), [[8, 256]], r + 4)
+            after(sent)
+            const(A("VL1", 256, 272), 5000)
+            after(sent)
 
         c1, v1 = A("c1", 16 * t, 16 * t + 16), A("v1", 16 * t, 16 * t + 16)
-        cp(v1, LA(t, None, 68, 72))
+        lin("v", v1, LA(t, None, 68, 72))
         ts(c1, LA(t, None, 64, 68), SP - 1.0, OP.min)
         for j in range(N - 1, -1, -1):
             cp(IN(A("PI"), LA(t, j, 64, 68)), LA(t, j, 0, 64))
             after(LA(t, None, 64, LW))
-        cp(A("vF"), LA(t, None, 0, 64))
-        tt(A("won", *z), IN(A("PI"), c1), A("vF"), OP.is_equal)
+        lin("s", A("vR"), LA(t, None, 0, 64))
+        tt(A("won", *z), IN(A("PI"), c1), A("vR"), OP.is_equal)
         if t == 2:
             tt(A("al"), IN(A("PI", 0, 2048), A("cO")), A("VL0", 0, 256), OP.not_equal)
         if t < 2:
-            for j in range(N - 1, -1, -1):
-                act(A("d1", 64 * j, 64 * j + 64), IN(A("M"), LA(t, j, 68, 72)), bias=FO)
-                after(LA(t, None, 64, LW))
-            act(A("d2"), IN(A("M"), c1), bias=FO - 1536.0)
-            lc(A("MI", 256, 512), (A("NID"), A("C15")), (A("IDF"), A("vF")), (A("NIH"), A("d2")))
+            lin("s", A("d1", 192, 256), IN(A("M"), LA(t, N - 1, 68, 72)), FO, wait=[LA(t, None, 64, LW)])
+            lin("s", A("d1", 0, 192), IN(A("M"), A("v1", 16 * t, 16 * t + 12)), FO)
+            lin("s", A("d2"), IN(A("M"), c1))
+            lin("v", A("vF"), LA(t, None, 0, 64), FO)
+            lc(A("MI", 256, 512), (A("IDF"), A("vR")), (A("NIH"), A("d2")))
             for j in range(N - 1, -1, -1):
                 o, i = IN(A("F"), LA(t, j, 64, 68)), A("d1", 64 * j, 64 * j + 64)
-                add("s", lambda e, o=o, i=i: e.activation(o[0], i[0], AF.Silu), [o], [i])
+                add("s", lambda e, o=o, i=i: e.activation(o[0], i[0], AF.Silu), [o], [i, A("C15")])
             tt(A("w"), A("won", *z), A("MI", 256, 512), OP.mult)
             tt(IN(A("F"), v1), A("vF"), A("w"), OP.subtract)
             act(A("wb"), A("won", *z), scale=BIG, acc=C("CNT", 0))
-            act(A("XG"), IN(A("X%d" % a), v1))
+            lin("s", A("XG"), IN(A("X%d" % a), v1))
             tt(IN(A("X%d" % a), v1), A("XG"), A("wb"), OP.add)
     marks(2)
     dma("s", T.yx[:, :], T.YX[:, :], [], [A("YX")], "sx", 2200.0)
-    if not CFG["keep"]:
+    if g is None:
         dep, lev = _graph(ops, soft, mid, spare)
         for c in alts:
             for n, o in c[0]:
                 ops[n] = o
-        CFG["keep"][0] = _plan(ops, dep, lev, alts)
+        return ops, dep, lev, alts, CFG["wake"], CFG["norm"]
+    if not CFG["keep"]:
+        cases = []
+        for case in CFG["cases"]:
+            CFG.update(case)
+            cases.append(rank_program(None, core, T, topo))
+        CFG["keep"][0] = _plan(cases)
     for c, side in zip(alts, CFG["keep"][0][3]):
         for n, o in c[side]:
             ops[n] = o

import math
from concourse.bass import DstId, RemoteDMATransfer
from concourse.mybir import AluOpType as OP, AxisListType as AX, ActivationFunctionType as AF

F32, BF, F16, I32, U16 = "float32", "bfloat16", "float16", "int32", "uint16"
TW = 2320
SP = 2064
LW = 72
NS = 4
BIG = 32768.0
KU = 4096.0
HS = 524288.0
FO = 65.0
RND = 12582912.0
CFG = {
    "f1": tuple(("vs"[n % 2], 32 * n, 32 * n + 32) for n in range(8)),
    "f2": tuple(("vs"[n % 2], 32 * n, 32 * n + 32) for n in range(8)),
    "fg": ((0, 64), (64, 128), (128, 192), (192, 256)),
    "sel": ((0, 128), (128, 192), (192, 256)),
    "cnt": 128, "ge": ((0, 64), (64, 128), (128, 192), (192, 256)), "gx": ((0, 64), (64, 128), (128, 192), (192, 224), (224, 256)),
    "abs0": (1, 3, 5, 6), "abs": (1, 2, 3, 4, 5, 6),
    "gam": 1.56, "sig": 3.8, "pe": 0.42, "wake": 90.0, "hop": 3500.0, "look": 600.0, "slack": 60.0, "fac": 1.25, "gfac": 1.05,
    "load": 4000.0, "norm": 1.0, "cases": (
        {"hop": 2800.0, "load": 3600.0, "fac": 1.25, "gam": 1.56, "sig": 3.8, "wake": 90.0, "norm": 1.0},
        {"hop": 3300.0, "load": 4000.0, "fac": 1.5, "gam": 1.15, "sig": 2.5, "wake": 130.0, "norm": 1.0},
        {"hop": 2400.0, "load": 3300.0, "fac": 1.1, "gam": 1.95, "sig": 5.2, "wake": 130.0, "norm": 1.1}),
    "keep": {}, "seed": 3, "turns": 10, "jit": 500.0, "moves": 700000, "heat": 200.0, "mean": 0.8,
}


def _sb(n, d):
    return ("sbuf", [128, n], d)


SCRATCH = {
    "M": _sb(TW, I32), "Q0": _sb(2048, I32), "Q1": _sb(2048, I32), "Q2": _sb(2048, I32),
    "F": _sb(TW, F32), "PI": _sb(TW, F32), "IO": _sb(TW, F32), "X0": _sb(TW, BF), "X1": _sb(TW, BF),
    "VRH": _sb(4096, F16), "VR1": _sb(4096, F32), "BC": _sb(2048, BF),
    "E": _sb(4096, BF), "GX": _sb(4096, BF), "MX": _sb(4096, BF), "GF": _sb(4096, F16), "SK": _sb(2048, BF),
    "Pi": _sb(8, I32), "Pf": _sb(16, F32), "I16": _sb(64, F32), "G16": _sb(128, F32), "SEED": _sb(256, F32),
    "J": _sb(32, I32), "Jf": _sb(96, F32), "RS": _sb(256, F32), "DIAG": _sb(64, F32), "TB": _sb(128, BF),
    "ONE": _sb(512, BF), "C15": _sb(256, BF),
    "WE": _sb(144, BF), "WM": _sb(144, BF), "WG": _sb(144, BF), "WA": _sb(144, BF),
    "ID": _sb(128, BF), "NID": _sb(128, BF), "NIH": _sb(128, F16), "IDF": _sb(128, F32), "IDB": _sb(128, BF), "IDN": _sb(128, BF),
    "BO": _sb(128, BF), "BON": _sb(128, BF), "O16": _sb(128, F32),
    "VL0": _sb(272, F32), "VL1": _sb(272, F32), "TC": _sb(24, F32), "B4": _sb(64, F32),
    "L0": _sb(16, U16), "L1": _sb(16, U16), "PERM": _sb(16, U16), "OW": _sb(16, U16),
    "thi": _sb(8, I32), "thb": _sb(8, BF), "THR": _sb(8, F32), "Ai": _sb(8, I32), "CNT": _sb(8, F32),
    "o0": _sb(256, U16), "o1": _sb(256, U16), "o2": _sb(256, U16), "oc": _sb(256, U16), "cO": _sb(16, U16), "idx": _sb(8, U16),
    "m2": _sb(256, F32), "mp": _sb(288, F32), "mW": _sb(544, F32), "OM": _sb(512, F16),
    "XN0": _sb(256, BF), "XN1": _sb(256, BF), "XTT": _sb(256, BF), "dead": _sb(256, BF),
    "pm": _sb(256, F32), "df": _sb(256, F32), "dn": _sb(256, F32), "sc": _sb(256, F32),
    "E1": _sb(256, BF), "E2": _sb(256, BF), "XC": _sb(256, BF), "cH": _sb(272, F32),
    "yy": _sb(256, BF), "cum": _sb(256, BF), "le": _sb(512, F16), "les": _sb(512, F16), "junk": _sb(1024, BF), "acc": _sb(16, F32), "Kc": _sb(64, F32),
    "K": _sb(64, F32), "Mk": _sb(64, F32), "Ta": _sb(64, F32), "AB": _sb(260, BF), "RB": _sb(260, BF), "U": _sb(8, F32), "nf": _sb(260, F32),
    "LA0": ("sbuf", [128, 4, LW], U16), "LA1": ("sbuf", [128, 4, LW], U16), "LA2": ("sbuf", [128, 4, LW], U16),
    "c1": _sb(48, U16), "v1": _sb(48, U16),
    "vF": _sb(256, F32), "cR": _sb(256, F32), "d1": _sb(256, F32), "d2": _sb(256, F16), "won": _sb(768, F32),
    "w": _sb(256, F32), "w2": _sb(256, F32), "XG": _sb(256, BF), "wb": _sb(256, BF), "van": _sb(768, BF), "IDH": _sb(128, F16), "vR": _sb(256, F32),
    "av": _sb(256, F16), "hb": _sb(256, BF), "sh": _sb(768, F16),
    "al": _sb(256, BF), "pr": _sb(256, BF), "ph": _sb(256, F16), "YM": _sb(512, F32), "YX": _sb(512, BF),
    "KA": ("psum", [128, 512], F32), "KB": ("psum", [128, 512], F32), "XA": ("psum", [128, 512], F32),
    "XB": ("psum", [128, 512], F32), "FA": ("psum", [128, 512], F32), "FB": ("psum", [128, 512], F32),
    "VO": ("psum", [128, 512], F32), "MI": ("psum", [128, 512], F32),
}
DMAS = ["lm0", "lm1", "lx1", "lx0", "lth", "lp", "lk", "lsM", "lsX0", "lsX1", "sp", "sm", "sx"]
REMS = ["q0", "q1", "q2", "a0", "a1", "a2", "tq0", "tq1", "tq2", "ta0", "ta1", "ta2"]
SEMAPHORES = ["sv", "ss", "st", "sg"] + DMAS + REMS


def _masks(topo, src, dsts):
    far = [d for d in dsts if d not in topo.cores_of(src)]
    near = [d for d in dsts if d in topo.cores_of(src)]
    out, used = {}, []
    for n, d in enumerate(far):
        e = topo.engines(src, d)
        per = len(e) // len(far)
        out[d] = e[n * per:(n + 1) * per]
        used += e
    for n, d in enumerate(near):
        e = [x for x in topo.engines(src, d) if x not in used]
        per = min([len(e) // len(near)] + [len(out[x]) for x in far])
        out[d] = e[n * per:(n + 1) * per]
    return out


def _helper(topo, cores, src, dst):
    if dst in topo.cores_of(src):
        return None
    return [c for c in topo.cores_of(src) if c not in cores and topo.die(c) != topo.die(src) and topo.may_write(c, dst)][0]


def _hand_on(g, core, T, topo):
    cores = list(T.cores)
    for r, src in enumerate(cores):
        dst = cores[r - 1]
        if _helper(topo, cores, src, dst) == core:
            rid, pid = topo.addr(dst, core)
            g.wait_ge(T.sem["q0"], len([x for x in topo.engines(src, core) if x not in topo.engines(src, dst)]))
            g.remote_dma(T.Q0[:, 1024:2048], T.Q0[:, 1024:2048], T.sem["q0"], T.sem["tq0"], pid, rid, topo.mask(core, dst))
            g.wait_ge(T.sem["tq0"], len(topo.engines(core, dst)))


def _deps(ops):
    hist, out = {}, []
    for n, (q, fn, rd, wr, sem, inc, cost, lat) in enumerate(ops):
        dep = {}
        for mode, regs in (("r", rd), ("w", wr)):
            for (name, lo, hi, st) in regs:
                bank = SCRATCH[name][0] == "psum"
                for (m, mo, l2, h2, st2) in hist.get(name, []):
                    plain = ops[m][4] is None and sem is None
                    same = ops[m][0] == q and plain
                    if bank and (not same or q == "t"):
                        hard = not same
                    elif l2 >= hi or lo >= h2 or (mode == "r" and mo == "r") or (
                            plain and (lo - l2) % (math.gcd(st * (hi - lo > 1), st2 * (h2 - l2 > 1)) or 1)):
                        continue
                    else:
                        hard = True
                    dep[m] = dep.get(m, False) or hard
        out.append(dep)
        for mode, regs in (("r", rd), ("w", wr)):
            for (name, lo, hi, st) in regs:
                hist.setdefault(name, []).append((n, mode, lo, hi, st))
    return out


def _graph(ops, soft, mid, spare):
    dep = _deps(ops)
    for n in mid:
        for m in [m for m in dep[n] if mid.get(m) == mid[n]]:
            del dep[n][m]
    last = {}
    for n, o in enumerate(ops):
        if o[0] in ("g", "y"):
            if o[0] in last:
                dep[n].setdefault(last[o[0]], False)
            if o[0] not in last or ops[last[o[0]]][4] not in REMS:
                last[o[0]] = n
        if o[0] is None and o[1] is not None:
            dep[n][[m for m in range(n) if ops[m][4] == o[1]][0]] = True
    full = [{m: (ops[m][7] + CFG["wake"] if hard else 0.0) for m, hard in d.items()} for d in dep]
    anc = []
    for n, d in enumerate(full):
        keep, mask = {}, 0
        for m in sorted(d, reverse=True):
            if not any(anc[k] >> m & 1 and k not in spare and ops[k][6] + d[k] >= d[m] for k in keep):
                keep[m] = d[m]
            mask |= anc[m] | 1 << m
        full[n] = keep
        anc.append(mask)
    lev = [0.0] * len(ops)
    hint = dict(soft)
    for n in range(len(ops) - 1, -1, -1):
        lev[n] += ops[n][6] + ops[n][7] + 1.0
        for m, x in full[n].items():
            lev[m] = max(lev[m], lev[n] + x - ops[m][7])
        if n in hint:
            lev[hint[n]] = max(lev[hint[n]], lev[n])
    return full, lev


def _plan(cases):
    ops, dep, lev = cases[0][:3]
    back = [{} for _o in ops]
    for n, d in enumerate(dep):
        for m, x in d.items():
            back[m][n] = x
    best, seed = None, CFG["seed"]
    for it in range(CFG["turns"]):
        out, end = _order(ops, dep, lev, [0.0] * len(ops))
        span = max(end[n] + ops[n][7] for n in out)
        if best is None or span < best[0]:
            best = (span, out, end)
        if it % 3 == 2:
            end = best[2]
        rank = []
        for x in end:
            seed = (seed * 1103515245 + 12345) % 2147483648
            rank.append(x + CFG["jit"] * seed / 2147483648)
        lev = _order(ops, back, rank, [0.0 if back[n] else o[7] for n, o in enumerate(ops)])[1]
    return _polish(cases, back, best[1])


def _times(on, cost, dep, out, start, old, stop=1 << 30, loss=0.0):
    end, free = list(old), {on[n]: old[n] for n in out[max(0, start - 150):start]}
    for lo in range(start, len(out), 48):
        part = out[lo:lo + 48]
        for n in part:
            q = on[n]
            t = free.get(q, 0.0)
            for m, x in dep[n]:
                x += end[m]
                if x > t:
                    t = x
            end[n] = free[q] = t + cost[n]
        if lo > stop:
            lag = [end[n] - old[n] for n in part if on[n] in ("v", "s")]
            if lag and min(lag) > loss:
                return None
            if not any(end[n] != old[n] for n in part):
                return end
    return end


def _chain(on, cost, dep, out, end, n):
    before, last, calls, pairs = {}, {}, [], []
    for k in out:
        before[k], last[on[k]] = last.get(on[k], -1), k
    while n >= 0:
        calls.append(n)
        t, w = end[n] - cost[n] - 0.01, -1
        for m, x in dep[n]:
            if end[m] + x > t:
                w = m
        if w < 0 <= before[n] and end[before[n]] > t:
            w = before[n]
            pairs.append((w, n))
        n = w
    return calls, pairs


def _polish(cases, back, out):
    ops, dep, alts = cases[0][0], cases[0][1], cases[0][3]
    side, seed = [0] * len(alts), [CFG["seed"]]
    pre = [[list(d.items()) for d in case[1]] for case in cases]
    tails = [n for n in out if not back[n]]
    whose = {n: c for c, forms in enumerate(alts) for n, o in forms[0]}

    def draw(k):
        seed[0] = (seed[0] * 1103515245 + 12345) % 2147483648
        return (seed[0] >> 8) % k

    def span(z, e):
        return max(e[n] + cases[z][0][n][7] for n in tails)

    def worth(new, i, j, old, each, room):
        got, val = [], []
        for z in range(len(cases)):
            got.append(_times(on, cost[z], pre[z], new, i, old[z], j, room + 20.0))
            if got[z] is None:
                return None, None
            val.append((span(z, got[z]) + CFG["mean"] * sum(got[z]) / len(ops)) / cases[z][5])
            if val[z] > each[z] + 2.0 * room + 40.0:
                return None, None
        return val, got

    def take(n):
        on[n] = ops[n][0] or n
        for z, case in enumerate(cases):
            o = case[0][n]
            cost[z][n] = o[6] if o[6] >= 0 else -o[7] - case[4]

    def flip(c):
        side[c] ^= 1
        for case in cases:
            for n, o in case[3][c][side[c]]:
                case[0][n] = o
        for n, o in alts[c][0]:
            take(n)

    on, cost, path = [None] * len(ops), [[0.0] * len(ops) for _c in cases], None
    for n in out:
        take(n)
    cur, now = worth(out, 0, len(out), cost, [1e18] * len(cases), 0.0)
    best = (sum(cur), out, now, list(side))
    for it in range(CFG["moves"]):
        kind, c = draw(10), -1
        if path is None or it % 64 == 0:
            z = draw(len(cases))
            path = _chain(on, cost[z], pre[z], out, now[z], max(tails, key=lambda k: now[z][k] + cases[z][0][k][7]))
        if it % 256 == 0:
            key = {}
            for k, n in enumerate(out):
                key[n] = (max([now[0][n] - cost[0][n]] + [key[m][0] for m in dep[n]]), k)
            out = sorted(out, key=key.get)
            cur, now = worth(out, 0, len(out), cost, [1e18] * len(cases), 0.0)
            if sum(cur) < best[0]:
                best = (sum(cur), out, now, list(side))
            continue
        if kind < 2:
            c = draw(len(alts))
            if kind:
                near = [c] + [whose[n] for n in path[0] if n in whose]
                c = near[draw(len(near))]
            flip(c)
            new, i, j = out, out.index(alts[c][0][0][0]), out.index(alts[c][0][-1][0])
        else:
            ahead, far = draw(2), draw(5 if draw(4) else 30)
            if kind < 6:
                y, x = path[1][draw(len(path[1]))]
                i, j = sorted((out.index(y), out.index(x)))
                y, x = out[i], out[j]
            else:
                i = j = draw(len(out))
                x = y = out[i]
                far += 1
            q, k, step = ops[x][0], (i if ahead else j), (-1 if ahead else 1)
            while far and 0 <= k + step < len(out):
                k += step
                if ops[out[k]][0] == q:
                    far -= 1
                    i, j = (k, j) if ahead else (i, k)
            if i == j or q is None:
                continue
            rel = dep if ahead else back
            move, need = {x if ahead else y}, set(rel[x if ahead else y])
            for k in (range(j - 1, i - 1, -1) if ahead else range(i + 1, j + 1)):
                if out[k] in need:
                    move.add(out[k])
                    need.update(rel[out[k]])
            part = out[i:j + 1]
            a, b = [k for k in part if k in move], [k for k in part if k not in move]
            new = out[:i] + (a + b if ahead else b + a) + out[j + 1:]
        room = CFG["heat"] * (1.0 - it / CFG["moves"]) * draw(64) / 64.0
        val, got = worth(new, i, j, now, cur, room)
        if val and sum(val) <= sum(cur) + room * len(cases):
            cur, out, now = val, new, got
        elif c >= 0:
            flip(c)
    for c in range(len(alts)):
        if side[c] != best[3][c]:
            flip(c)
    return ([span(z, e) for z, e in enumerate(best[2])],) + best[1:]


def _order(ops, dep, lev, ready):
    succ = [[] for _o in ops]
    left = [len(d) for d in dep]
    for n, d in enumerate(dep):
        for m in d:
            succ[m].append(n)
    ends, free, pool, out = [0.0] * len(ops), {}, {}, []
    for n in range(len(ops)):
        if not left[n]:
            pool.setdefault(ops[n][0], []).append(n)
    while len(out) < len(ops):
        best = None
        for q, p in pool.items():
            if p:
                t0 = max(free.get(q, 0.0) if q else 0.0, min(ready[n] for n in p))
                if best is None or t0 < best[0]:
                    best = (t0, q)
        t0, q = best
        top = max((n for n in pool[q] if ready[n] <= t0 + CFG["look"]), key=lambda z: (lev[z], -z))
        fit = [n for n in pool[q] if max(ready[n], t0) + ops[n][6] <= ready[top] + CFG["slack"]]
        n = max(fit, key=lambda z: (lev[z], -z)) if fit and ready[top] > t0 else top
        pool[q].remove(n)
        end = max(ready[n], t0 if q else 0.0) + ops[n][6]
        free[q] = ends[n] = end
        out.append(n)
        for k in succ[n]:
            ready[k] = max(ready[k], end + dep[k][n])
            left[k] -= 1
            if not left[k]:
                pool.setdefault(ops[k][0], []).append(k)
    return out, ends


def _emit(g, T, ops):
    Q = {"v": g.vector, "s": g.scalar, "t": g.tensor, "g": g, "y": g.sync}
    own = {"v": "sv", "s": "ss", "t": "st", "g": "sg"}
    count = {k: 0 for k in SEMAPHORES}
    known = {k: {} for k in Q}
    done, dep = [], _deps(ops)
    for n, (q, fn, rd, wr, sem, inc, cost, lat) in enumerate(ops):
        if q is None:
            count[sem] += inc
            done.append((sem, count[sem], {}))
            continue
        need = {}
        for m, hard in dep[n].items():
            s, c, _k = done[m]
            if hard and c > need.get(s, (0, 0))[0]:
                need[s] = (c, m)
        for s in sorted(need, key=lambda z: -need[z][1]):
            c, m = need[s]
            if known[q].get(s, 0) < c:
                Q[q].wait_ge(T.sem[s], c)
                known[q][s] = c
                for s3, c3 in done[m][2].items():
                    known[q][s3] = max(known[q].get(s3, 0), c3)
        s = sem or own[q]
        if s in REMS:
            fn(Q[q])
        elif q == "t":
            for i in fn(Q[q]):
                i.then_inc(T.sem[s], 1)
        else:
            fn(Q[q]).then_inc(T.sem[s], inc)
        count[s] += inc
        done.append((s, count[s], dict(known[q])))
    for s in SEMAPHORES:
        if count[s] and max(known[q].get(s, 0) for q in Q) < count[s]:
            g.wait_ge(T.sem[s], count[s])


def rank_program(g, core, T, topo):
    r = T.rank_of(core)
    if r is None:
        return _hand_on(g, core, T, topo)
    cores = list(T.cores)
    N = len(cores)
    ops, soft, tail, mid, grp, alts, spare = [], [], {}, {}, {}, [], set()
    SEL, FG, fac = CFG["sel"], CFG["fg"], CFG["fac"]
    WM = max(hi - lo for lo, hi in SEL)

    def A(name, lo=0, hi=None, st=1, p=None):
        hi = SCRATCH[name][1][1] if hi is None else hi
        ps = slice(0, 128) if p is None else slice(*p)
        return (T[name][ps, lo:hi:st] if st > 1 else T[name][ps, lo:hi], [(name, lo, hi, st)])

    def C(name, c):
        return A(name, c, c + 1)

    def LA(t, j, lo, hi, st=1):
        name = "LA%d" % t
        if j is None:
            return (T[name][:, :, lo:hi], [(name, LW * i + lo, LW * i + hi, 1) for i in range(N)])
        return (T[name][:, j, lo:hi:st] if st > 1 else T[name][:, j, lo:hi], [(name, LW * j + lo, LW * j + hi, st)])

    def IN(win, off):
        return (win[0].indirect(off[0]), win[1] + off[1], win[1], off[1])

    def ap(x):
        return x[0] if isinstance(x, tuple) else x

    def size(x):
        name, lo, hi, st = x[1][-1]
        return (hi - lo + st - 1) // st * (16 if len(x) == 4 else 1)

    def add(q, fn, out, ins, sem=None, inc=1, cost=None, lat=0.0, two=False, more=0.0):
        rd, wr = [], []
        full = [x for x in ins if isinstance(x, tuple)]
        for x in full:
            rd += x[1]
        for x in out:
            wr += x[2] if len(x) == 4 else x[1]
            rd += x[3] if len(x) == 4 else []
        if cost is None:
            n = max(size(x) for x in full + out)
            c0 = 50 if q == "v" else 65
            if len(out[0]) == 4:
                cost = (c0 + CFG["sig"] * 0.83 * size(out[0])) * CFG["gfac"] / fac
            elif full and len(full[0]) == 4:
                cost = (c0 + CFG["gam"] * 0.83 * size(full[0])) * CFG["gfac"] / fac
            else:
                kinds = [SCRATCH[x[1][0][0]] for x in full + out if size(x) == n]
                k = 0.5 if q == "v" and all(z[2] in (BF, F16, U16) for z in kinds) else 1.0
                if two:
                    k = 1.0 if any(z[0] == "psum" for z in kinds) else 2.0
                cost = 30 + 0.83 * max(64, k * n)
            cost = (cost + more) * fac
        ops.append((q, fn, rd, wr, sem, inc, cost, lat))

    def after(*regs):
        for x in regs:
            ops[-1][2].extend(x[1])

    def either(first, steps):
        forms = ([], [])
        for step in steps:
            n, made = len(ops), []
            for f in step:
                if f:
                    f()
                made.append(ops.pop() if f else None)
            whole = [o for o in made if o]
            ops.append(whole[0][:2] + (sum((o[2] for o in whole), []),) + whole[0][3:])
            for side in (0, 1):
                forms[side].append((n, made[side] or (None, None, [], [], None, 0, -1.0, whole[0][7])))
            if len(whole) < 2:
                spare.add(n)
        alts.append(forms if first else forms[::-1])

    def chain(key):
        if key in tail:
            soft.append((len(ops) - 1, tail[key]))
        tail[key] = len(ops) - 1

    def cp(o, i):
        add("v", lambda e: e.tensor_copy(o[0], i[0]), [o], [i])

    def tt(o, a, b, op):
        add("v", lambda e: e.tensor_tensor(o[0], a[0], b[0], op), [o], [a, b], two=True)

    def ts(o, a, s1, op0, s2=None, op1=None):
        if op1 is None:
            add("v", lambda e: e.tensor_scalar(o[0], a[0], ap(s1), None, op0), [o], [a, s1])
        else:
            add("v", lambda e: e.tensor_scalar(o[0], a[0], ap(s1), ap(s2), op0, op1), [o], [a, s1, s2])

    def scan(o, a, b, op0, op1, init=0.0):
        add("v", lambda e: e.tensor_tensor_scan(o[0], a[0], b[0], ap(init), op0, op1), [o], [a, b, init])

    def tr(o, i):
        add("v", lambda e: e.transpose(o[0], i[0]), [o], [i])

    def ms(o, c):
        add("v", lambda e: e.memset(o[0], c), [o], [])

    def act(o, i, f=AF.Identity, bias=0.0, scale=1.0, acc=None, more=0.0):
        if acc is None:
            add("s", lambda e: e.activation(o[0], i[0], f, bias=ap(bias), scale=ap(scale)), [o], [i, bias, scale], more=more)
        else:
            add("s", lambda e: e.activation(o[0], i[0], f, bias=ap(bias), scale=scale, accum_out=acc[0]), [o, acc], [i, bias], more=20.0)

    def lin(q, o, i, bias=0.0, scale=1.0, wait=()):
        up = 0.25 if SCRATCH[o[1][0][0]][2] in (U16, I32) else 0.0

        def on_s():
            act(o, i, bias=bias + up if up else bias, scale=scale)
            after(*wait)

        def on_v():
            if scale != 1.0:
                ts(o, i, scale, OP.mult, bias, OP.add)
            elif bias:
                ts(o, i, bias, OP.add)
            else:
                cp(o, i)
            after(*wait)

        either(q == "s", ((on_s, on_v),))

    def flag(q, o, i, c, above):
        either(q == "s", ((lambda: act(o, i, AF.Sign if above else AF.Relu, bias=-c if above else c + 1.0, scale=1.0 if above else -1.0),
                           lambda: ts(o, i, c + 0.5, OP.is_gt if above else OP.is_lt)),))

    def fill(q, o, c):
        either(q == "s", ((lambda: act(o, A("SEED", 0, size(o)), bias=c, scale=0.0), lambda: ms(o, c)),))

    def mms(o, terms, a, b):
        c = sum(fac * CFG["pe"] * max(64, size(x)) * (4 if SCRATCH[x[1][0][0]][2] == F32 else 1) for l, x in terms)
        z = len(terms) - 1
        add("t", lambda e: [e.matmul(o[0], l[0], x[0], a and n == 0, b and n == z) for n, (l, x) in enumerate(terms)],
            [o], [y for lx in terms for y in lx], inc=z + 1, cost=c, lat=100.0)
        bank = o[1][0][0]
        if a:
            grp[bank] = len(ops)
        if not a and not b:
            mid[len(ops) - 1] = grp[bank]

    def mm(o, l, x, a, b):
        mms(o, [(l, x)], a, b)

    def lc(o, *terms):
        for n, (l, x) in enumerate(terms):
            mm(o, l, x, n == 0, n == len(terms) - 1)

    def iota(o, pat, base, ch=0):
        c = fac * (130 + 1.66 * size(o))
        if SCRATCH[o[1][0][0]][2] != I32:
            add("g", lambda e: e.iota(o[0], pat, base, ch, allow_small_or_imprecise_dtypes=True), [o], [], cost=c)
        else:
            add("g", lambda e: e.iota(o[0], pat, base, ch), [o], [], cost=c)

    def const(o, c):
        iota(o, [[0, size(o)]], int(c))

    def ends(name, a, first):
        for c in range(first, 16 // NS):
            iota(A(name, 256 * NS * c, 256 * NS * (c + 1)), [[8, 16], [128, NS], [0, 16]], 128 * NS * c + 4 * a + r)
            after(LA(0, r, 64, LW))

    def dma(q, o, i, out, ins, sem, lat):
        add(q, lambda e: e.dma_start(o, i), out, ins, sem, 16, cost=60.0, lat=lat)

    def send_table(t, wait):
        d, s = cores[(r - 1 - t) % N], cores[(r + 1 + t) % N]
        rid, pid = topo.addr(d, core)
        src, q, h = A("M", 0, 2048), T["Q%d" % t], _helper(topo, cores, core, d) if t == 0 else None
        n = len(topo.engines(core, d))
        if h is None:
            def call(e):
                e.remote_dma(q[:, :], src[0], T.sem["q%d" % t], T.sem["tq%d" % t], pid, rid, topo.mask(core, d))
        else:
            rest = [x for x in topo.engines(core, h) if x not in topo.engines(core, d)]
            n += len(rest)
            trs = [RemoteDMATransfer(dst_ids=[DstId(rid=a, pnc=b)], dma_engine_mask=mask, remote_sem=T.sem["q0"],
                                     src=T.M[:, lo:lo + 1024], dst=q[:, lo:lo + 1024])
                   for (a, b), mask, lo in (((rid, pid), topo.mask(core, d), 0), (topo.addr(h, core), sum(1 << x for x in rest), 1024))]

            def call(e):
                e.remote_dma_fused(trs, local_sem=T.sem["tq0"])
        add("g", call, [], [src] + wait, "tq%d" % t, n, cost=500.0, lat=10000.0)
        h = _helper(topo, cores, s, core) if t == 0 else None
        add(None, "tq%d" % t, [A("Q%d" % t)], [], "q%d" % t, len(topo.engines(s, core)) + (len(topo.engines(h, core)) if h else 0), cost=0.0)

    def send_lists(t):
        peers = [c for c in cores if c != core]
        mk = _masks(topo, core, peers)
        src = LA(t, r, 0, LW)
        trs = []
        for d in peers:
            rid, pid = topo.addr(d, core)
            trs.append(RemoteDMATransfer(dst_ids=[DstId(rid=rid, pnc=pid)], dma_engine_mask=sum(1 << x for x in mk[d]),
                                         remote_sem=T.sem["a%d" % t], src=src[0], dst=src[0]))
        add("g", lambda e: e.remote_dma_fused(trs, local_sem=T.sem["ta%d" % t]), [], [src, A("SK")] + [A("F", 0, 928)] * (t == 0), "ta%d" % t,
            sum(len(mk[d]) for d in peers), cost=500.0, lat=CFG["hop"] - 500.0)
        n = sum(len(_masks(topo, s, [c for c in cores if c != s])[core]) for s in peers)
        add(None, "ta%d" % t, [LA(t, j, 0, LW) for j in range(N) if j != r], [], "a%d" % t, n, cost=0.0)

    def own(name, a, lo=0, hi=256, j=r):
        return (A(name, 4 * a + j + 8 * lo, 8 * hi, 8)[0], [(name, 4 * a + i + 8 * lo, 8 * hi, 8) for i in range(N)])

    mp = A("mp", 16, 272)

    def key(n, lo, hi):
        return A(("KA", "KB")[n % 2], lo % 256, (hi - 1) % 256 + 1)

    ms(A("thi"), 0)
    dma("y", T.M[:, 0:1024], T.mt[:, 0:1024], [A("M", 0, 1024)], [], "lm0", CFG["load"])
    dma("s", T.M[:, 1024:2048], T.mt[:, 1024:2048], [A("M", 1024, 2048)], [], "lm1", CFG["load"])
    dma("y", T.X1[:, 0:2048], T.xv[:, :], [A("X1", 0, 2048), C("Ai", 7)], [], "lx1", CFG["load"] + 700.0)
    dma("y", T.thi[0:128:16, 0:1], T.th[:], [A("thi")], [], "lth", 2500.0)
    dma("y", T.X0[:, 0:2048], T.xv[:, :], [A("X0", 0, 2048)], [C("Ai", 7)], "lx0", 3500.0)

    iota(C("Pi", 0), [[0, 1]], 0, 1)
    iota(A("SEED"), [[8, 16 // NS], [128, NS], [0, 16]], r)
    iota(A("Jf", 0, 16), [[128 * NS, 16 // NS], [128 // NS, NS]], r)
    iota(A("IO", 0, 256), [[1, 256]], 1)
    iota(A("G16"), [[1, 8], [0, 16]], 0)
    iota(A("TB", 0, 16 * NS), [[0, NS], [-int(KU), 16]], int(16 * KU))
    iota(A("J", 0, 16), [[16, 16]], 0, 1)
    iota(A("I16"), [[0, 4], [1, 16]], 0)
    iota(A("Jf", 16, 32), [[16 * NS, 16 // NS], [1, NS]], 0)
    const(A("mp", 0, 16), 0)
    const(A("mp", 272, 288), 0)
    send_table(0, [])
    iota(A("VL0", 0, 256), [[8, 256]], r)
    iota(A("IO", 256, 2048), [[1, 1792]], 257)
    iota(A("B4"), [[int(KU), 64]], 0)
    const(A("VL0", 256, 272), 5000)
    iota(A("IO", 2048, TW), [[1, TW - 2048]], 2049)
    const(A("PI", 0, 256), -1)
    ms(A("ONE"), 1.0)
    for n in range(0, 2048, 256):
        dma("y", T.SK[:, n:n + 256], T.ONE[:, 0:256], [A("SK", n, n + 256)], [A("ONE", 0, 256), C("Ai", 7)], "lk", 4000.0)
    for n in range(256, TW, 256):
        dma("y", T.PI[:, n:min(n + 256, TW)], T.PI[:, 0:min(256, TW - n)], [A("PI", n, min(n + 256, TW))],
            [A("PI", 0, 256), A("X0", 0, 16)], "lp", 5000.0)
    for n in range(0, 2048, 1024):
        o = A("SK", n, n + 1024)
        add("g", lambda e, o=o, n=n: e.affine_select(o[0], o[0], [[-1, 8], [512, 8], [33, 16]], OP.is_equal, 0.0, -n // 128, -32),
            [A("SK")], [A("SK")], cost=fac * (170 + 1.66 * 1024))
    ms(A("RB", 0, 130), 0.0)
    ms(A("RB", 130, 260), -KU)
    for nm, src in (("M", T.mt), ("X0", T.xv), ("X1", T.xv)):
        dma("y", T[nm][:, 2048:TW], src[:, 0:TW - 2048], [A(nm, 2048, TW)], [C("Ai", 7)], "ls" + nm, 3500.0)
    iota(A("F", 0, 928), [[1, 928]], int(FO))
    for n in range(928, TW, 464):
        lin("s", A("F", n, n + 464), A("IO", n, n + 464), FO - 1.0)
    lin("s", A("VRH", 0, 256), A("SEED"))
    for n in (256, 512, 1024):
        lin("v", A("VRH", n, 2 * n), A("VRH", 0, n), n / 2.0 / (NS if n < 256 * NS else 1))
    for n in (2048, 3072):
        lin("v", A("VRH", n, n + 1024), A("VRH", 0, 1024), n / 2.0)
    ts(C("Pi", 1), C("Pi", 0), 15, OP.bitwise_and)
    ts(C("Pi", 2), C("Pi", 0), 4, OP.logical_shift_right)
    ts(C("Pi", 3), C("Pi", 0), NS - 1, OP.bitwise_and)
    ts(C("Pi", 4), C("Pi", 0), 15, OP.bitwise_and, NS.bit_length() - 1, OP.logical_shift_right)
    cp(A("Pf", 0, 5), A("Pi", 0, 5))
    fill("v", C("ONE", 256), 0.0)
    fill("s", A("AB", 64, 260, 65), 1e29)
    for n, m, bias, scale in ((5, 0, 1.0, 1.0), (6, 2, 16.0, 16.0), (8, 4, 0.0, 8.0), (7, 3, C("Pf", 8), 128.0), (9, 1, 0.0, float(NS)),
                              (10, 0, float(r), 8.0), (12, 2, 0.0, -16.0),
                              (13, 1, 0.0, KU), (14, 1, float(r), KU), (15, 1, r + 4.0, KU)):
        lin("s", C("Pf", n), C("Pf", m), bias, scale)
    ts(A("L0"), A("Jf", 0, 16), C("Pf", 7), OP.add)
    ts(A("L1"), A("Jf", 0, 16), C("Pf", 7), OP.add, 4.0, OP.add)
    ts(A("PERM"), A("Jf", 16, 32), C("Pf", 9), OP.add)
    ts(A("ID"), A("IO", 0, 128), C("Pf", 5), OP.is_equal)
    ts(A("WE"), A("IO", 0, 144), C("Pf", 6), OP.is_equal, 65536.0 * KU, OP.mult)
    ts(A("BO"), A("G16"), C("Pf", 2), OP.is_equal)
    for n in range(0, 2048, 1024):
        ts(A("BC", n, n + 1024), A("VRH", n, n + 1024), C("Pf", 10), OP.is_equal)
    for nm, wt in (("WG", 16.0), ("WM", -32.0), ("WA", -16.0)):
        lin("s", A(nm), A("WE"), 0.0, wt / 65536.0)
    lin("s", A("BON"), A("BO"), 0.0, -1.0 / 8192)
    for nm, wt in (("NID", -1.0), ("IDF", 1.0), ("NIH", -1.0), ("IDH", 1.0), ("IDB", BIG), ("IDN", -64.0)):
        lin("s", A(nm), A("ID"), 0.0, wt)
    fill("s", A("RS", 0, WM), 0.0)
    fill("s", A("RS", 0, WM, 16), -1e29)
    ts(A("DIAG"), A("I16"), C("Pf", 1), OP.is_equal)
    ts(A("J", 16, 32), A("J", 0, 16), 4, OP.logical_shift_right, 1, OP.bitwise_and)
    lin("s", A("Jf", 32, 48), A("J", 0, 16), C("Pf", 12))
    lin("s", A("Jf", 48, 64), A("J", 16, 32), 0.0, 272.0)
    tt(A("Jf", 64, 80), A("Jf", 32, 48), A("Jf", 48, 64), OP.add)
    lin("s", A("OW"), A("Jf", 64, 80))
    lin("s", A("TC", 0, 4), A("IO", 0, 4), C("Pf", 1), 16.0)
    lin("s", A("TC", 4, 8), A("TC", 0, 4), -32.0, 2.0)
    lin("s", A("TC", 8, 12), A("TC", 0, 4), -31.0, 2.0)
    lin("s", A("TC", 12, 16), A("TC", 0, 4), float(SP + 64 * r - 16))
    lin("s", A("RB", 64, 130, 65), A("IO", 0, 2), 16.0 * KU, -16.0 * KU)
    lin("s", A("RB", 194, 260, 65), A("IO", 2, 4), 272.0 * KU, -16.0 * KU)
    for o, c in ((A("RB", 0, 260, 65), 1e29), (C("CNT", 1), -1.5 * BIG / 8), (A("O16"), 0.0625 / BIG), (A("cH", 256, 272), 4000.0 * HS)):
        fill("s", o, c)
    lin("s", C("thb", 0), C("thi", 0))

    def choose(t, blocks, oc):
        a = t % 2
        for n in range(8):
            lo, hi = 512 * n, 512 * n + 512
            for x, y in CFG["ge"]:
                if x == 32 * n:
                    tt(A("E", lo, 16 * y), IN(A("M", 0, 2048), A(oc, x, y)), A("VR1" if a else "VRH", lo, 16 * y), OP.is_equal)
                    chain("v")
            for x, y in CFG["gx"]:
                if x == 32 * n:
                    lin("s", A("GX", lo, 16 * y), IN(A("X%d" % (1 - a), 0, 2048), A(oc, x, y)))
                    chain("s")
            c0 = 32 * n // (16 * NS) * 16 * NS
            sel = [i for i, (x, y) in enumerate(SEL) if x <= c0 < y][0]
            kb = key(sel, c0, c0 + 16 * NS)
            if 32 * n == c0:
                mm(kb, A("ID"), A("TB", 0, 16 * NS), True, False)
            bank = A(("XA", "XB")[n % 2])
            def keys(src, wn):
                mms(kb, [(A(wn, 15 - (x - c0) // NS, 143 - (x - c0) // NS), A(src, 16 * x, 16 * x + 16 * NS))
                         for x in range(32 * n, 32 * n + 32, NS)], False, src == "MX" and 32 * n + 32 == c0 + 16 * NS)

            def spread(stop):
                mm(bank, A("XTT", 128 * (n // 4), 128 * (n // 4) + 128), A("BC", lo % 2048, lo % 2048 + 512), True, stop)

            keys("E", "WE")
            either(n in blocks, (
                (lambda: spread(False), lambda: spread(True)),
                (lambda: mm(bank, A("NID"), A("GX", lo, hi), False, True), None),
                (lambda: act(A("MX", lo, hi), bank, AF.Abs), lambda: tt(A("MX", lo, hi), A("GX", lo, hi), bank, OP.max)),
                (None, lambda: keys("GX", "WG")),
                (lambda: keys("MX", "WA"), lambda: keys("MX", "WM"))))
            if 32 * n + 32 == SEL[sel][1]:
                vote(t, sel)

    def turn(a):
        for h in range(2):
            mm(A("XB", 128 * h, 128 * h + 128), A("XN%d" % a, 128 * h, 128 * h + 128), A("ID"), True, True)
        lin("s", A("XTT"), A("XB", 0, 256))

    def vote(t, n):
        a, (lo, hi) = t % 2, SEL[n]
        w, kb = hi - lo, key(n, lo, hi)
        if n == 0:
            tr(A("mW", 0, 256), A("mp", 16, 272))
            tr(A("mW", 256, 544), A("mp"))
        scan(A("pm", lo, hi), A("RS", 0, w), kb, OP.add, OP.max)
        tt(A("df", lo, hi), A("pm", lo, hi), kb, OP.subtract)
        tt(A("dn", lo, hi), IN(A("mW"), A("OW", lo // 16, hi // 16)), A("df", lo, hi), OP.subtract)
        scan(A("sc", lo, hi), A("df", lo, hi), A("dn", lo, hi), OP.min, OP.max)
        c = A("cO", lo // 16, hi // 16)
        lin("v", c, A("sc", lo + 15, hi, 16))
        lin("s", A("XC", lo, hi), IN(A("X%d" % (1 - a), 0, 2048), c))
        tt(A("E2", lo, hi), IN(A("Q%d" % t), c), A("VL%d" % a, lo, hi), OP.is_equal)
        tt(A("E1", lo, hi), IN(A("M", 0, 2048), c), A("VL%d" % a, lo, hi), OP.is_equal)
        lin("s", A("cH", lo, hi), IN(A("IO", 0, 2048), c), -HS, HS)
        vo = A("VO", lo, hi)
        lc(vo, *([(A("IDN"), A("dead", lo, hi))] * (t > 0) +
                 [(A("BON"), A("XC", lo, hi)), (A("BO"), A("E2", lo, hi)), (A("BO"), A("E1", lo, hi))]))
        act(A("yy", lo, hi), vo, AF.Sign, bias=C("THR", t))
        scan(A("cum", lo, hi), A("yy", lo, hi), A("ONE", 0, w), OP.add, OP.add, C("cum", lo - 1) if lo else 0.0)

    def follow(units, src, dst, col):
        for q, lo, hi in units:
            lin(q, A("GF", 16 * lo, 16 * hi), IN(A("F", 0, 2048), A(src, lo, hi)), -FO)
            chain(q + dst)
        for n, (lo, hi) in enumerate(FG):
            o = A("FB" if col else "FA", lo, hi)
            mms(o, [(A("SK", 128 * k, 128 * k + 128), A("GF", 16 * lo + k, 16 * hi, 16)) for k in range(16)], True, True)
            lin("v", A(dst, lo, hi), o)
        if col:
            lin("s", A("m2"), A("FB", 0, 256), RND)

    def marks(t):
        a, z = t % 2, (256 * t, 256 * t + 256)
        cw = IN(A("IO", 0, TW), A("c1", 16 * t, 16 * t + 16))
        if t == 2:
            lin("s", A("cR"), cw)
            mm(A("FB", 0, 256), A("IDF"), A("cR"), True, True)
            tt(A("w2"), A("won", *z), A("FB", 0, 256), OP.mult)
        else:
            tt(A("w2"), cw, A("won", *z), OP.mult)
            after(A("AB"))
        ts(IN(A("PI"), A("v1", 16 * t, 16 * t + 16)), A("w2"), 1.0, OP.mult, -1.0, OP.add)
        if t == 2:
            dma("y", T.yp[:, :], T.PI[0:128:16, 0:2048], [], [A("PI")], "sp", 2200.0)
        else:
            flag("s", A("al"), own("PI", a), -1.0, False)
        lc(A("KA", 0, 256), (A("ID"), A("XN%d" % a)), (A("ID"), A("C15")), (A("NIH"), A("sh", *z)))
        tt(A("pr"), A("al"), A("KA", 0, 256), OP.mult)
        lc(A("KB", 0, 256), (A("ID"), A("XN%d" % a)), (A("NID"), A("pr")))
        lin("s", A("XN0") if t == 0 else A("YX", a, 512, 2), A("KB", 0, 256))

    for t in range(3):
        a = t % 2
        off = 4 * a + r
        z = (256 * t, 256 * t + 256)
        if t == 0:
            for lo, hi in ((0, 64), (64, 256)):
                lin("s" if lo else "v", A("o0", lo, hi), IN(A("M", 0, 2048), A("L0", lo // 16, hi // 16)))
            lin("s", A("XN0"), own("X1", 0))
            const(A("X1", 0, 2048, 8), BIG)
            for j in range(1, 4):
                fill("vs"[j % 2], A("X1", j, 2048, 8), BIG)
            lin("s", A("XN1"), own("X1", 1))
            lin("s", mp, own("M", 0))
            for b in range(2):
                lin("s", A("OM", 256 * b, 256 * b + 256), own("M", b))
            mm(A("VO", 256, 257), A("BO"), C("thb", 0), True, True)
            lin("s", C("THR", 0), A("VO", 256, 257), 0.5, -1.0)
            lin("s", C("THR", 6), C("THR", 0), -1.5)
            turn(0)
            choose(0, CFG["abs0"], "o0")
        else:
            flag("s", A("dead"), own("PI", a), -1.0, True)
            lc(A("VO", 256, 257), (A("O16"), C("CNT", 1)), (A("O16"), C("CNT", 0)))
            lin("s", C("THR", 3), A("VO", 256, 257), C("THR", 6), -1.0)
            lin("s", C("THR", 4), A("VO", 256, 257), RND, 0.25)
            lin("s", C("THR", 5), C("THR", 4), -RND)
            lin("s", C("THR", t), C("THR", 5), C("THR", 3), 4.0)
            follow(CFG["f1"], "o%d" % a, "o2", 0)
            follow(CFG["f2"], "o2", "oc", 256)
            lin("s", mp, IN(A("m2"), A("PERM")), -RND)
            choose(t, CFG["abs"], "oc")

        lo = CFG["cnt"]
        w = 256 - lo
        if lo:
            for s in range(4):
                act(A("junk", 256 * s, 256 * s + lo), A("cum", 0, lo), AF.Sign, bias=C("TC", 8 + s), scale=-1.0, acc=C("acc", s))
            lin("s", A("acc", 4, 6), A("acc", 0, 2), lo / 2.0 + 0.25, 0.5)
            lin("s", A("acc", 6, 8), A("acc", 2, 4), 128.25, 0.5)
        for s in (2, 3):
            act(A("junk", 256 * s + lo, 256 * s + 256), A("cum", lo, 256), AF.Sign, bias=C("TC", 8 + s), scale=-1.0, acc=C("acc", 8 + s))
            if lo:
                act(C("idx", s), C("acc", 8 + s), bias=C("acc", 4 + s), scale=0.5)
        for s in (0, 1):
            ts(A("le", w * s, w * s + w), A("cum", lo, 256), C("TC", 4 + s), OP.is_le)
        scan(A("les", 0, 2 * w), A("ONE", 256 - w, 256 + w), A("le", 0, 2 * w), OP.mult, OP.add)
        if lo:
            for s in (0, 1):
                ts(C("idx", s), C("les", w * s + w - 1), C("acc", 4 + s), OP.add)
        else:
            lin("v", A("idx", 0, 2), A("les", 255, 512, 256))
            lin("s", A("idx", 2, 4), A("acc", 10, 12), 128.0, 0.5)
        ix = A("idx", 0, 4)
        lin("s", LA(t, r, 0, 64), IN(A("VL%d" % a), ix))
        tt(A("Mk"), IN(A("cH"), ix), A("DIAG"), OP.mult)
        tt(A("K"), IN(A("cH"), ix), A("B4"), OP.subtract)
        lin("s", A("Kc"), IN(A("cH"), ix))
        scan(A("Ta"), A("RS", 0, 64), A("Mk"), OP.add, OP.max)
        for s in (0, 1):
            act(A("AB", 65 * s, 65 * s + 64), A("K"), AF.Abs, bias=C("Ta", 16 * s + 15), scale=-1.0)
        for s in (2, 3):
            ts(A("AB", 65 * s, 65 * s + 64), A("Kc"), C("Ta", 16 * s + 15), OP.is_equal, -193.0 * KU, OP.mult)
        lin("v", A("U", 0, 4), A("Ta", 15, 64, 16), C("Pf", 13), 1.0 / HS)
        lin("s", A("U", 4, 8), ix, C("Pf", 14 + a), 8.0)
        scan(A("nf"), A("RB"), A("AB"), OP.add, OP.min)
        for s in range(4):
            ts(LA(t, r, 64 + s, LW, 4), A("U", s, 8, 4), C("nf", 65 * s + 64), OP.subtract, C("TC", 12 + s), OP.min)
        send_lists(t)
        sent = LA(t, r, 64, LW)
        if t == 0:
            act(A("C15"), A("ONE", 0, 256), AF.Silu, scale=1536.0, more=1300.0)
            after(A("AB"))

        lc(A("MI", 0, 256), *([(A("IDB"), A("dead"))] * (t > 0) + [(A("ID"), A("XN%d" % a)), (A("ID"), A("XC"))]))
        lin("s", A("av"), A("MI", 0, 256), 1535.75, 0.5)
        act(A("hb"), A("MI", 0, 256), AF.Relu, bias=1024.0, scale=-1.0)
        lc(A("XA", 0, 256), (A("ID"), A("XN%d" % a)), (A("ID"), A("C15")), (A("ID"), A("hb")))
        tt(A("sh", *z), A("av"), A("XA", 0, 256), OP.min)
        if t == 0:
            lin("s", own("X0", 0), A("sh", *z), -1536.0)
        if t == 1:
            for n, j in enumerate(j for j in range(N) if j != r):
                act(A("van", 256 * n, 256 * n + 256), own("PI", 1, j=j), AF.Sign, bias=1.0)
                after(A("MX"))
                o = A(("FA", "FB")[n % 2], 256, 512)
                lc(o, (A("IDB"), A("van", 256 * n, 256 * n + 256)), (A("ID"), own("X1", 1, j=j)))
                lin("s", own("X1", 1, j=j), o)
            lc(A("XB", 256, 512), (A("IDB"), A("dead")), (A("IDH"), A("sh", *z)))
            lin("s", own("X1", 1), A("XB", 256, 512), -1536.0)
        if t == 0:
            lin("v", A("o1"), IN(A("M", 0, 2048), A("L1")))
            for j in range(4):
                fill("v", A("X0", 4 + j, 2048, 8), BIG)
        if t > 0:
            om = A("OM", 256 * a, 256 * a + 256)
            lc(A("FA", 0, 256), (A("IDF"), mp), (A("NIH"), om))
            tt(A("ph"), A("dead"), A("FA", 0, 256), OP.mult)
            lc(A("XB", 0, 256), (A("IDF"), mp), (A("NIH"), A("ph")))
            lin("s", A("YM", a, 512, 2), A("XB", 0, 256))
            marks(t - 1)
        if t == 1:
            lin("s", own("M", 1), mp)
        if t == 2:
            dma("y", T.ym[:, :], T.YM[:, :], [], [A("YM")], "sm", 2500.0)
        if t < 2:
            turn(1 - a)
            send_table(t + 1, [LA(t, None, 0, LW)])
        if t == 0:
            ends("VR1", 1, 0)
            iota(A("VL1", 0, 256), [[8, 256]], r + 4)
            after(sent)
            const(A("VL1", 256, 272), 5000)
            after(sent)

        c1, v1 = A("c1", 16 * t, 16 * t + 16), A("v1", 16 * t, 16 * t + 16)
        lin("v", v1, LA(t, None, 68, 72))
        ts(c1, LA(t, None, 64, 68), SP - 1.0, OP.min)
        for j in range(N - 1, -1, -1):
            cp(IN(A("PI"), LA(t, j, 64, 68)), LA(t, j, 0, 64))
            after(LA(t, None, 64, LW))
        lin("s", A("vR"), LA(t, None, 0, 64))
        tt(A("won", *z), IN(A("PI"), c1), A("vR"), OP.is_equal)
        if t == 2:
            tt(A("al"), IN(A("PI", 0, 2048), A("cO")), A("VL0", 0, 256), OP.not_equal)
        if t < 2:
            lin("s", A("d1", 192, 256), IN(A("M"), LA(t, N - 1, 68, 72)), FO, wait=[LA(t, None, 64, LW)])
            lin("s", A("d1", 0, 192), IN(A("M"), A("v1", 16 * t, 16 * t + 12)), FO)
            lin("s", A("d2"), IN(A("M"), c1))
            lin("v", A("vF"), LA(t, None, 0, 64), FO)
            lc(A("MI", 256, 512), (A("IDF"), A("vR")), (A("NIH"), A("d2")))
            for j in range(N - 1, -1, -1):
                o, i = IN(A("F"), LA(t, j, 64, 68)), A("d1", 64 * j, 64 * j + 64)
                add("s", lambda e, o=o, i=i: e.activation(o[0], i[0], AF.Silu), [o], [i, A("C15")])
            tt(A("w"), A("won", *z), A("MI", 256, 512), OP.mult)
            tt(IN(A("F"), v1), A("vF"), A("w"), OP.subtract)
            act(A("wb"), A("won", *z), scale=BIG, acc=C("CNT", 0))
            lin("s", A("XG"), IN(A("X%d" % a), v1))
            tt(IN(A("X%d" % a), v1), A("XG"), A("wb"), OP.add)
    marks(2)
    dma("s", T.yx[:, :], T.YX[:, :], [], [A("YX")], "sx", 2200.0)
    if g is None:
        dep, lev = _graph(ops, soft, mid, spare)
        for c in alts:
            for n, o in c[0]:
                ops[n] = o
        return ops, dep, lev, alts, CFG["wake"], CFG["norm"]
    if not CFG["keep"]:
        cases = []
        for case in CFG["cases"]:
            CFG.update(case)
            cases.append(rank_program(None, core, T, topo))
        CFG["keep"][0] = _plan(cases)
    for c, side in zip(alts, CFG["keep"][0][3]):
        for n, o in c[side]:
            ops[n] = o
    _emit(g, T, [ops[n] for n in CFG["keep"][0][1] if ops[n][6] >= 0])
